import numpy as np
import ml_dtypes


def mxq(x, axis, fmt="e4m3"):
    dtype, down = {"e4m3": (ml_dtypes.float8_e4m3fn, 7), "e5m2": (ml_dtypes.float8_e5m2, 14)}[fmt]
    v = np.moveaxis(np.asarray(x, np.float32).astype(ml_dtypes.bfloat16).astype(np.float64), axis, -1)
    blocks = v.reshape(v.shape[:-1] + (-1, 32))
    amax = np.abs(blocks).max(-1, keepdims=True)
    byte = np.maximum(np.where(amax > 0, np.frexp(amax)[1] - 1 + 127, 0) - down, 1)
    scale = np.exp2(byte - 127.0)
    codes = (blocks / scale).astype(np.float32).astype(dtype).astype(np.float64)
    return np.moveaxis((codes * scale).reshape(v.shape), -1, axis)


WIDE = False


def mx_kscale(k):
    if not WIDE:
        return np.ones(k)
    levels = np.array([18, -18])
    if k % 512:
        return np.exp2(np.random.permutation(np.resize(levels, k // 32))).repeat(32)
    a = np.empty((k // 512, 16))
    for p in range(k // 512):
        a[p, :8] = np.random.permutation(np.resize(levels, 8))
        for g in range(8):
            far = levels[np.abs(levels - a[p, g]) >= 10]
            a[p, g + 8] = far[np.random.randint(len(far))]
    return np.exp2(a.ravel()).repeat(32)


def f64(x):
    return np.asarray(x).astype(np.float64)


def striped(idx):
    return np.tile(np.asarray(idx).reshape(-1, 16).T, (8, 1)).astype(np.uint16)


def unstriped(offs):
    return offs[:16].T.reshape(-1).astype(np.int64)


def setup_inputs():
    n = np.random.standard_normal
    uni = np.random.uniform
    idx = np.random.permutation(2048)[:512]
    jdx = np.random.permutation(2048)[:512]
    soft_y = np.exp(0.4 * n((512, 512)))
    f_d = mx_kscale(512)
    f_i = np.ones(2048)
    f_i[idx] = mx_kscale(512)
    return {
        "uT": (0.35 * n((512, 2048)) / np.sqrt(512) * f_d[:, None] * f_i[None, :]).astype(np.float32),
        "vT": (n((512, 2048)) / f_d[:, None]).astype(np.float32),
        "su": np.tile(uni(0.75, 1.3, 2048) / f_i, (128, 1)).astype(np.float32),
        "sv": np.tile(uni(0.75, 1.3, 2048), (128, 1)).astype(np.float32),
        "y": (soft_y / soft_y.sum(-1, keepdims=True)).astype(np.float32),
        "offs": striped(idx),
        "qoffs": striped(jdx),
    }


def reference(uT, vT, su, sv, y, offs, qoffs):
    idx = unstriped(offs)
    jdx = unstriped(qoffs)
    uT_i = f64(uT)[:, idx]
    vT_j = f64(vT)[:, jdx]
    su_i = f64(su)[:1][:, idx]
    sv_j = f64(sv)[:1][:, jdx]
    suc = su_i.T
    a = mxq(uT_i, 0, "e4m3").T @ mxq(vT_j, 0, "e4m3")
    e = np.exp(suc * sv_j * a)
    r1 = (e).sum(-1, keepdims=True)
    f = e / r1
    ft = f.T
    c1 = (ft).sum(-1, keepdims=True)
    cr = c1.T
    g = suc * sv_j * (f / cr - f64(y))
    dv = mxq(uT_i, 1, "e4m3") @ mxq(g, 0, "e5m2")
    out = np.zeros((512, 2048))
    out[:, jdx] = dv
    return out

@@ -1,0 +1,285 @@
+from contextlib import ExitStack
+
+import concourse.mybir as mybir
+from concourse.masks import make_identity
+
+F32 = mybir.dt.float32
+BF16 = mybir.dt.bfloat16
+U32 = mybir.dt.uint32
+U16 = mybir.dt.uint16
+U8 = mybir.dt.uint8
+E4M3 = mybir.dt.float8_e4m3fn_x4
+E5M2 = mybir.dt.float8_e5m2_x4
+ALU = mybir.AluOpType
+ACT = mybir.ActivationFunctionType
+AXIS = mybir.AxisListType
+
+P = 128
+PACK = 4
+SLOTS = 512
+POOL = 2048
+FEATURES = 512
+
+FLOPS = 2 * 2 * SLOTS * SLOTS * FEATURES
+BYTES = 4 * (3 * FEATURES * POOL + SLOTS * SLOTS + 2 * POOL) + 2 * 2 * P * (SLOTS // 16)
+
+
+def tile_attend_gsink_v_kernel(tc, uT, vT, su, sv, y, offs, qoffs, out):
+    nc = tc.nc
+    four = range(PACK)
+
+    def block(n):
+        return slice(n * P, (n + 1) * P)
+
+    with ExitStack() as ctx:
+        sb = ctx.enter_context(tc.tile_pool(name="sb", bufs=1))
+        ps = ctx.enter_context(tc.psum_pool(name="ps", bufs=1))
+
+        def sbuf(name, shape, dtype, over=None):
+            return sb.tile(shape, dtype, name=name, tag=over or name, align_bytes=64)
+
+        def bank(n, name, dtype=F32):
+            return ps.tile([P, PACK, P], dtype, name=name, tag="bank%d" % n)
+
+        i_list = sb.tile([P, SLOTS // 16], U16, name="i_list")
+        j_list = sb.tile([P, SLOTS // 16], U16, name="j_list")
+        nc.sync.dma_start(i_list[:], offs)
+        nc.sync.dma_start(j_list[:], qoffs)
+
+        su_pool = sbuf("su_pool", [P, POOL], F32)
+        sv_pool = sbuf("sv_pool", [P, POOL], F32)
+        nc.vector.memset(su_pool[0 : P - 1, :], 0.0)
+        nc.vector.memset(sv_pool[0 : P - 1, :], 0.0)
+        u_rows = uT.rearrange("(p t) c -> p t c", t=PACK)
+        v_rows = vT.rearrange("(p t) c -> p t c", t=PACK)
+        out_rows = out.rearrange("(p t) c -> p t c", t=PACK)
+        u_pool = [sbuf("u_pool%d" % t, [P, POOL], F32) for t in four]
+        v_pool = [sbuf("v_pool%d" % t, [P, POOL], F32) for t in four]
+        nc.sync.dma_start(u_pool[0][:], u_rows[:, 0, :])
+        nc.sync.dma_start(su_pool[P - 1 : P, :], su[0:1, :])
+        nc.sync.dma_start(sv_pool[P - 1 : P, :], sv[0:1, :])
+        for t in range(1, PACK):
+            nc.sync.dma_start(u_pool[t][:], u_rows[:, t, :])
+        for t in four:
+            nc.sync.dma_start(v_pool[t][:], v_rows[:, t, :])
+        y_sb = sbuf("y_sb", [P, PACK, SLOTS], F32)
+        nc.sync.dma_start(y_sb[:], y.rearrange("(p r) j -> p r j", r=PACK))
+
+        ident = sbuf("ident", [P, P], F32)
+        ident_bf = sbuf("ident_bf", [P, P], BF16)
+        make_identity(nc, ident[:])
+        make_identity(nc, ident_bf[:])
+        warm = sbuf("warm", [P, 1], F32)
+        nc.scalar.activation(warm[:], ident[:, 0:1], ACT.Exp)
+
+        window = [sbuf("window%d" % t, [P, POOL], F32) for t in four]
+        for t in four:
+            nc.gpsimd.memset(window[t][:], 0.0)
+
+        u_planes = sbuf("u_planes", [P, PACK, SLOTS], BF16)
+
+        def gather_u(t):
+            nc.vector.tensor_copy(u_planes[:, t, :], u_pool[t][:].indirect(i_list[:]))
+
+        gather_u(0)
+        su_row = sbuf("su_row", [P, SLOTS], F32)
+        sv_row = sbuf("sv_row", [P, SLOTS], F32)
+        nc.vector.tensor_copy(su_row[:], su_pool[:].indirect(i_list[:]))
+        nc.vector.tensor_copy(sv_row[:], sv_pool[:].indirect(j_list[:]))
+        su_turned = bank(4, "su_turned")
+        sv_turned = bank(5, "sv_turned")
+        for n in four:
+            nc.tensor.transpose(su_turned[:, n, :], su_row[:, n::PACK], ident[:])
+        for n in four:
+            nc.tensor.transpose(sv_turned[:, n, :], sv_row[:, block(n)], ident[:])
+        su_col = sbuf("su_col", [P, PACK], F32)
+        sv_col = sbuf("sv_col", [P, PACK], F32)
+        nc.scalar.copy(su_col[:], su_turned[:, :, P - 1])
+        nc.scalar.copy(sv_col[:], sv_turned[:, :, P - 1])
+        sv_spread = bank(6, "sv_spread")
+        for n in four:
+            nc.tensor.transpose(sv_spread[:, n, :], sv_col[:, n : n + 1].to_broadcast([P, P]), ident[:])
+        sv_all = sbuf("sv_all", [P, SLOTS], F32)
+        nc.scalar.copy(sv_all[:], sv_spread[:].rearrange("p n j -> p (n j)"))
+
+        for t in range(1, PACK):
+            gather_u(t)
+
+        u_along_d = sbuf("u_along_d", [P, SLOTS, PACK], BF16)
+        nc.scalar.copy(
+            u_along_d[:].rearrange("p (r s) t -> p s t r", r=PACK),
+            u_planes[:].rearrange("p t (s r) -> p s t r", r=PACK),
+        )
+
+        u_along_i = sbuf("u_along_i", [P, PACK, P, PACK], BF16)
+        for t in four:
+            turned = bank(t, "u_turned%d" % t, BF16)
+            for r in four:
+                nc.tensor.transpose(turned[:, r, :], u_planes[:, t, r::PACK], ident_bf[:])
+            nc.scalar.copy(u_along_i[:, t], turned[:].rearrange("s r p -> s p r"))
+
+        factor_planes = sbuf("factor_planes", [P, PACK, SLOTS], F32, over="u_planes")
+        for r in four:
+            nc.scalar.activation(factor_planes[:, r, :], sv_all[:], ACT.Copy, scale=su_col[:, r : r + 1])
+        factor = sbuf("factor", [P, SLOTS, PACK], F32)
+        nc.scalar.copy(factor[:], factor_planes[:].rearrange("s r j -> s j r"))
+
+        v_along_d = sbuf("v_along_d", [P, SLOTS, PACK], BF16)
+
+        def gather_v(t, first=0, last=SLOTS):
+            nc.vector.tensor_copy(
+                v_along_d[:, first:last, t], v_pool[t][:].indirect(j_list[:, first // 16 : last // 16])
+            )
+
+        def operand(name, over=None):
+            return sbuf(name + "_codes", [P, SLOTS], U32, over), sbuf(name + "_scales", [P, SLOTS], U8)
+
+        v_codes, v_scales = operand("v")
+        g_codes, g_scales = operand("g")
+
+        gather_v(0)
+        gather_v(1)
+        ud_codes, ud_scales = operand("ud", over="v_pool1")
+        nc.vector.quantize_mx(ud_codes[:].bitcast(E4M3), ud_scales[:], u_along_d[:].rearrange("p n t -> p (n t)"))
+        gather_v(2)
+        halves = (slice(0, SLOTS // 2), slice(SLOTS // 2, SLOTS))
+        for half in halves:
+            gather_v(3, half.start, half.stop)
+        for half in halves:
+            nc.vector.quantize_mx(
+                v_codes[:, half].bitcast(E4M3), v_scales[:, half], v_along_d[:, half, :].rearrange("p n t -> p (n t)")
+            )
+        ui_codes, ui_scales = operand("ui", over="v_along_d")
+        nc.vector.quantize_mx(ui_codes[:].bitcast(E4M3), ui_scales[:], u_along_i[:].rearrange("s t p r -> s (t p r)"))
+
+        scores = []
+        for r in four:
+            a = bank(r, "scores%d" % r)
+            for half in halves:
+                nc.tensor.matmul_mx(
+                    a[:].rearrange("p n j -> p (n j)")[:, half],
+                    lhsT=ud_codes[:, block(r)].bitcast(E4M3), lhsT_scale=ud_scales[:, block(r)],
+                    rhs=v_codes[:, half].bitcast(E4M3), rhs_scale=v_scales[:, half], start=True, stop=True,
+                )
+            scores.append(a)
+
+        y_turned = []
+        for n in four:
+            turned = bank(4 + n, "y_turned%d" % n)
+            for r in four:
+                nc.tensor.transpose(turned[:, r, :], y_sb[:, r, block(n)], ident[:])
+            y_turned.append(turned)
+
+        z = [sbuf("z%d" % r, [P, SLOTS], F32) for r in four]
+        e = [sbuf("e%d" % r, [P, SLOTS], F32) for r in four]
+        f = [sbuf("f%d" % r, [P, SLOTS], F32) for r in four]
+        neg_max = [sbuf("neg_max%d" % r, [P, 1], F32) for r in four]
+        row_sum = [sbuf("row_sum%d" % r, [P, 1], F32) for r in four]
+        row_inv = [sbuf("row_inv%d" % r, [P, 1], F32) for r in four]
+
+        def logits(r):
+            nc.vector.scalar_tensor_tensor(
+                z[r][:], scores[r][:].rearrange("p n j -> p (n j)"), su_col[:, r : r + 1], sv_all[:], ALU.mult, ALU.mult
+            )
+
+        def exponent(r):
+            nc.vector.tensor_reduce(neg_max[r][:], z[r][:], AXIS.X, ALU.max, negate=True)
+            nc.scalar.activation(e[r][:], z[r][:], ACT.Exp, bias=neg_max[r][:], accum_out=row_sum[r][:])
+
+        def invert(r):
+            nc.vector.reciprocal(row_inv[r][:], row_sum[r][:])
+
+        def normalise(r):
+            nc.vector.tensor_scalar(f[r][:], e[r][:], row_inv[r][:], None, ALU.mult)
+
+        logits(0)
+        logits(1)
+        exponent(0)
+        logits(2)
+        exponent(1)
+        invert(0)
+        nc.scalar.activation(f[0][:], e[0][:], ACT.Copy, scale=row_inv[0][:])
+        logits(3)
+        exponent(2)
+        invert(1)
+        exponent(3)
+        normalise(1)
+        invert(2)
+        normalise(2)
+        invert(3)
+        normalise(3)
+
+        f_turned = [bank(n, "f_turned%d" % n) for n in four]
+
+        def turn(n, r):
+            nc.tensor.transpose(f_turned[n][:, r, :], f[r][:, block(n)], ident[:])
+
+        for r in (0, 1):
+            for n in four:
+                turn(n, r)
+        for n in four:
+            for r in (2, 3):
+                turn(n, r)
+
+        col_sum = [sbuf("col_sum%d" % n, [P, 1], F32) for n in four]
+        col_inv = [sbuf("col_inv%d" % n, [P, 1], F32) for n in four]
+        f_cols = [sbuf("f_cols%d" % n, [P, SLOTS], F32) for n in four]
+        gap = [sbuf("gap%d" % n, [P, SLOTS], F32) for n in four]
+        g_along_i = sbuf("g_along_i", [P, SLOTS, PACK], BF16)
+        back = []
+
+        def column_sum(n):
+            nc.scalar.activation(
+                f_cols[n][:], f_turned[n][:].rearrange("j r s -> j (r s)"), ACT.Copy, accum_out=col_sum[n][:]
+            )
+            nc.vector.reciprocal(col_inv[n][:], col_sum[n][:])
+
+        def difference(n):
+            nc.vector.scalar_tensor_tensor(
+                gap[n][:], f_cols[n][:], col_inv[n][:], y_turned[n][:].rearrange("j r s -> j (r s)"),
+                ALU.mult, ALU.subtract,
+            )
+            h = bank(n, "back%d" % n)
+            for r in four:
+                nc.tensor.transpose(h[:, r, :], gap[n][:, block(r)], ident[:])
+            back.append(h)
+
+        def gradient(n):
+            nc.vector.tensor_tensor(
+                g_along_i[:, block(n), :], back[n][:].rearrange("s r j -> s j r"), factor[:, block(n), :], ALU.mult
+            )
+
+        def quantise_gradient(n):
+            nc.vector.quantize_mx(
+                g_codes[:, block(n)].bitcast(E5M2), g_scales[:, block(n)],
+                g_along_i[:, block(n), :].rearrange("s j r -> s (j r)"),
+            )
+
+        column_sum(0)
+        difference(0)
+        column_sum(1)
+        difference(1)
+        column_sum(2)
+        gradient(0)
+        difference(2)
+        column_sum(3)
+        gradient(1)
+        difference(3)
+        quantise_gradient(0)
+        gradient(2)
+        quantise_gradient(1)
+        gradient(3)
+        quantise_gradient(2)
+        quantise_gradient(3)
+
+        for t in four:
+            acc = bank(4 + t, "dv%d" % t)
+            nc.tensor.matmul_mx(
+                acc[:].rearrange("p n j -> p (n j)"),
+                lhsT=ui_codes[:, block(t)].bitcast(E4M3), lhsT_scale=ui_scales[:, block(t)],
+                rhs=g_codes[:].bitcast(E5M2), rhs_scale=g_scales[:], start=True, stop=True,
+            )
+            dv = sbuf("dv_sb%d" % t, [P, SLOTS], F32)
+            nc.scalar.copy(dv[:], acc[:].rearrange("p n j -> p (n j)"))
+            nc.vector.tensor_copy(window[t][:].indirect(j_list[:]), dv[:])
+            nc.sync.dma_start(out_rows[:, t, :], window[t][:])

@@ -43,8 +43,6 @@ def tile_attend_gsink_v_kernel(tc, uT, vT, su, sv, y, offs, qoffs, out):
 
         i_list = sb.tile([P, SLOTS // 16], U16, name="i_list")
         j_list = sb.tile([P, SLOTS // 16], U16, name="j_list")
-        nc.sync.dma_start(i_list[:], offs)
-        nc.sync.dma_start(j_list[:], qoffs)
 
         su_pool = sbuf("su_pool", [P, POOL], F32)
         sv_pool = sbuf("sv_pool", [P, POOL], F32)
@@ -56,6 +54,8 @@ def tile_attend_gsink_v_kernel(tc, uT, vT, su, sv, y, offs, qoffs, out):
         u_pool = [sbuf("u_pool%d" % t, [P, POOL], F32) for t in four]
         v_pool = [sbuf("v_pool%d" % t, [P, POOL], F32) for t in four]
         nc.sync.dma_start(u_pool[0][:], u_rows[:, 0, :])
+        nc.sync.dma_start(i_list[:], offs)
+        nc.sync.dma_start(j_list[:], qoffs)
         nc.sync.dma_start(su_pool[P - 1 : P, :], su[0:1, :])
         nc.sync.dma_start(sv_pool[P - 1 : P, :], sv[0:1, :])
         for t in range(1, PACK):
@@ -72,9 +72,14 @@ def tile_attend_gsink_v_kernel(tc, uT, vT, su, sv, y, offs, qoffs, out):
         warm = sbuf("warm", [P, 1], F32)
         nc.scalar.activation(warm[:], ident[:, 0:1], ACT.Exp)
 
-        window = [sbuf("window%d" % t, [P, POOL], F32) for t in four]
-        for t in four:
-            nc.gpsimd.memset(window[t][:], 0.0)
+        window = []
+
+        def clear_window(engine, over):
+            cleared = sbuf("window%d" % len(window), [P, POOL], F32, over)
+            engine.memset(cleared[:], 0.0)
+            window.append(cleared)
+
+        clear_window(nc.vector, None)
 
         u_planes = sbuf("u_planes", [P, PACK, SLOTS], BF16)
 
@@ -104,6 +109,7 @@ def tile_attend_gsink_v_kernel(tc, uT, vT, su, sv, y, offs, qoffs, out):
 
         for t in range(1, PACK):
             gather_u(t)
+        clear_window(nc.vector, "u_pool3")
 
         u_along_d = sbuf("u_along_d", [P, SLOTS, PACK], BF16)
         nc.scalar.copy(
@@ -162,6 +168,9 @@ def tile_attend_gsink_v_kernel(tc, uT, vT, su, sv, y, offs, qoffs, out):
                     rhs=v_codes[:, half].bitcast(E4M3), rhs_scale=v_scales[:, half], start=True, stop=True,
                 )
             scores.append(a)
+
+        clear_window(nc.gpsimd, "u_along_i")
+        clear_window(nc.gpsimd, "v_pool1")
 
         y_turned = []
         for n in four:
@@ -280,6 +289,8 @@ def tile_attend_gsink_v_kernel(tc, uT, vT, su, sv, y, offs, qoffs, out):
                 rhs=g_codes[:].bitcast(E5M2), rhs_scale=g_scales[:], start=True, stop=True,
             )
             dv = sbuf("dv_sb%d" % t, [P, SLOTS], F32)
-            nc.scalar.copy(dv[:], acc[:].rearrange("p n j -> p (n j)"))
-            nc.vector.tensor_copy(window[t][:].indirect(j_list[:]), dv[:])
+            for part in halves if t == 0 else (slice(0, SLOTS),):
+                nc.scalar.copy(dv[:, part], acc[:].rearrange("p n j -> p (n j)")[:, part])
+                places = j_list[:, part.start // 16 : part.stop // 16]
+                nc.vector.tensor_copy(window[t][:].indirect(places), dv[:, part])
             nc.sync.dma_start(out_rows[:, t, :], window[t][:])

@@ -6,6 +6,7 @@ from concourse.masks import make_identity
 F32 = mybir.dt.float32
 BF16 = mybir.dt.bfloat16
 U32 = mybir.dt.uint32
+I32 = mybir.dt.int32
 U16 = mybir.dt.uint16
 U8 = mybir.dt.uint8
 E4M3 = mybir.dt.float8_e4m3fn_x4
@@ -46,8 +47,8 @@ def tile_attend_gsink_v_kernel(tc, uT, vT, su, sv, y, offs, qoffs, out):
 
         su_pool = sbuf("su_pool", [P, POOL], F32)
         sv_pool = sbuf("sv_pool", [P, POOL], F32)
-        nc.vector.memset(su_pool[0 : P - 1, :], 0.0)
-        nc.vector.memset(sv_pool[0 : P - 1, :], 0.0)
+        nc.vector.memset(su_pool[0 : P - 1, :].bitcast(I32), 0)
+        nc.vector.memset(sv_pool[0 : P - 1, :].bitcast(I32), 0)
         u_rows = uT.rearrange("(p t) c -> p t c", t=PACK)
         v_rows = vT.rearrange("(p t) c -> p t c", t=PACK)
         out_rows = out.rearrange("(p t) c -> p t c", t=PACK)
@@ -76,7 +77,7 @@ def tile_attend_gsink_v_kernel(tc, uT, vT, su, sv, y, offs, qoffs, out):
 
         def clear_window(engine, over):
             cleared = sbuf("window%d" % len(window), [P, POOL], F32, over)
-            engine.memset(cleared[:], 0.0)
+            engine.memset(cleared[:].bitcast(I32), 0)
             window.append(cleared)
 
         clear_window(nc.vector, None)
@@ -170,7 +171,6 @@ def tile_attend_gsink_v_kernel(tc, uT, vT, su, sv, y, offs, qoffs, out):
             scores.append(a)
 
         clear_window(nc.gpsimd, "u_along_i")
-        clear_window(nc.gpsimd, "v_pool1")
 
         y_turned = []
         for n in four:
@@ -212,8 +212,8 @@ def tile_attend_gsink_v_kernel(tc, uT, vT, su, sv, y, offs, qoffs, out):
         exponent(2)
         invert(1)
         exponent(3)
-        normalise(1)
         invert(2)
+        normalise(1)
         normalise(2)
         invert(3)
         normalise(3)
@@ -223,11 +223,8 @@ def tile_attend_gsink_v_kernel(tc, uT, vT, su, sv, y, offs, qoffs, out):
         def turn(n, r):
             nc.tensor.transpose(f_turned[n][:, r, :], f[r][:, block(n)], ident[:])
 
-        for r in (0, 1):
+        for r in four:
             for n in four:
-                turn(n, r)
-        for n in four:
-            for r in (2, 3):
                 turn(n, r)
 
         col_sum = [sbuf("col_sum%d" % n, [P, 1], F32) for n in four]
@@ -264,6 +261,24 @@ def tile_attend_gsink_v_kernel(tc, uT, vT, su, sv, y, offs, qoffs, out):
                 g_along_i[:, block(n), :].rearrange("s j r -> s (j r)"),
             )
 
+        early_planes = PACK - 1
+
+        def early_product():
+            acc = bank(4, "early")
+            nc.tensor.matmul_mx(
+                acc[:].rearrange("j t p -> j (t p)"),
+                lhsT=g_codes[:, block(0)].bitcast(E5M2), lhsT_scale=g_scales[:, block(0)],
+                rhs=ui_codes[:].bitcast(E4M3), rhs_scale=ui_scales[:], start=True, stop=True,
+            )
+            rows = sbuf("early_rows", [P, early_planes, P], F32)
+            nc.scalar.copy(rows[:], acc[:, 0:early_planes, :])
+            turned = bank(5, "early_turned")
+            for t in range(early_planes):
+                nc.tensor.transpose(turned[:, t, :], rows[:, t, :], ident[:])
+            cols = sbuf("early_cols", [P, early_planes, P], F32)
+            nc.scalar.copy(cols[:], turned[:, 0:early_planes, :])
+            return cols
+
         column_sum(0)
         difference(0)
         column_sum(1)
@@ -271,26 +286,31 @@ def tile_attend_gsink_v_kernel(tc, uT, vT, su, sv, y, offs, qoffs, out):
         column_sum(2)
         gradient(0)
         difference(2)
+        quantise_gradient(0)
+        early_cols = early_product()
         column_sum(3)
         gradient(1)
         difference(3)
-        quantise_gradient(0)
         gradient(2)
         quantise_gradient(1)
         gradient(3)
         quantise_gradient(2)
         quantise_gradient(3)
+        zeros = sbuf("zeros", [P, P], F32, over="factor")
+        nc.gpsimd.memset(zeros[:], 0.0)
 
+        for t in range(early_planes):
+            nc.vector.tensor_tensor(window[t][:].indirect(j_list[:, 0 : P // 16]), early_cols[:, t, :], zeros[:], ALU.add)
         for t in four:
-            acc = bank(4 + t, "dv%d" % t)
+            acc = bank(4 + (t + 2) % PACK, "dv%d" % t)
             nc.tensor.matmul_mx(
                 acc[:].rearrange("p n j -> p (n j)"),
                 lhsT=ui_codes[:, block(t)].bitcast(E4M3), lhsT_scale=ui_scales[:, block(t)],
                 rhs=g_codes[:].bitcast(E5M2), rhs_scale=g_scales[:], start=True, stop=True,
             )
-            dv = sbuf("dv_sb%d" % t, [P, SLOTS], F32)
-            for part in halves if t == 0 else (slice(0, SLOTS),):
-                nc.scalar.copy(dv[:, part], acc[:].rearrange("p n j -> p (n j)")[:, part])
-                places = j_list[:, part.start // 16 : part.stop // 16]
-                nc.vector.tensor_copy(window[t][:].indirect(places), dv[:, part])
-            nc.sync.dma_start(out_rows[:, t, :], window[t][:])
+            first = P if t < early_planes else 0
+            dv = sbuf("dv_sb%d" % t, [P, SLOTS - first], F32)
+            nc.scalar.copy(dv[:], acc[:].rearrange("p n j -> p (n j)")[:, first:])
+            target = window[t % len(window)]
+            nc.vector.tensor_copy(target[:].indirect(j_list[:, first // 16 :]), dv[:])
+            nc.sync.dma_start(out_rows[:, t, :], target[:])

@@ -70,8 +70,6 @@ def tile_attend_gsink_v_kernel(tc, uT, vT, su, sv, y, offs, qoffs, out):
         ident_bf = sbuf("ident_bf", [P, P], BF16)
         make_identity(nc, ident[:])
         make_identity(nc, ident_bf[:])
-        warm = sbuf("warm", [P, 1], F32)
-        nc.scalar.activation(warm[:], ident[:, 0:1], ACT.Exp)
 
         window = []
 
@@ -80,7 +78,6 @@ def tile_attend_gsink_v_kernel(tc, uT, vT, su, sv, y, offs, qoffs, out):
             engine.memset(cleared[:].bitcast(I32), 0)
             window.append(cleared)
 
-        clear_window(nc.vector, None)
 
         u_planes = sbuf("u_planes", [P, PACK, SLOTS], BF16)
 
@@ -110,7 +107,7 @@ def tile_attend_gsink_v_kernel(tc, uT, vT, su, sv, y, offs, qoffs, out):
 
         for t in range(1, PACK):
             gather_u(t)
-        clear_window(nc.vector, "u_pool3")
+        clear_window(nc.gpsimd, "u_pool3")
 
         u_along_d = sbuf("u_along_d", [P, SLOTS, PACK], BF16)
         nc.scalar.copy(
@@ -156,8 +153,6 @@ def tile_attend_gsink_v_kernel(tc, uT, vT, su, sv, y, offs, qoffs, out):
             nc.vector.quantize_mx(
                 v_codes[:, half].bitcast(E4M3), v_scales[:, half], v_along_d[:, half, :].rearrange("p n t -> p (n t)")
             )
-        ui_codes, ui_scales = operand("ui", over="v_along_d")
-        nc.vector.quantize_mx(ui_codes[:].bitcast(E4M3), ui_scales[:], u_along_i[:].rearrange("s t p r -> s (t p r)"))
 
         scores = []
         for r in four:
@@ -170,7 +165,8 @@ def tile_attend_gsink_v_kernel(tc, uT, vT, su, sv, y, offs, qoffs, out):
                 )
             scores.append(a)
 
-        clear_window(nc.gpsimd, "u_along_i")
+        clear_window(nc.gpsimd, "v_along_d")
+        clear_window(nc.gpsimd, "v_pool1")
 
         y_turned = []
         for n in four:
@@ -217,6 +213,8 @@ def tile_attend_gsink_v_kernel(tc, uT, vT, su, sv, y, offs, qoffs, out):
         normalise(2)
         invert(3)
         normalise(3)
+        ui_codes, ui_scales = operand("ui", over="e3")
+        nc.vector.quantize_mx(ui_codes[:].bitcast(E4M3), ui_scales[:], u_along_i[:].rearrange("s t p r -> s (t p r)"))
 
         f_turned = [bank(n, "f_turned%d" % n) for n in four]
 
@@ -261,7 +259,7 @@ def tile_attend_gsink_v_kernel(tc, uT, vT, su, sv, y, offs, qoffs, out):
                 g_along_i[:, block(n), :].rearrange("s j r -> s (j r)"),
             )
 
-        early_planes = PACK - 1
+        early_planes = 2
 
         def early_product():
             acc = bank(4, "early")

@@ -1,3 +1,4 @@
+import math
 from contextlib import ExitStack
 
 import concourse.mybir as mybir
@@ -18,8 +19,10 @@ AXIS = mybir.AxisListType
 P = 128
 PACK = 4
 SLOTS = 512
+HALF = SLOTS // 2
 POOL = 2048
 FEATURES = 512
+SOFTEN = 8.0
 
 FLOPS = 2 * 2 * SLOTS * SLOTS * FEATURES
 BYTES = 4 * (3 * FEATURES * POOL + SLOTS * SLOTS + 2 * POOL) + 2 * 2 * P * (SLOTS // 16)
@@ -28,9 +31,13 @@ BYTES = 4 * (3 * FEATURES * POOL + SLOTS * SLOTS + 2 * POOL) + 2 * 2 * P * (SLOT
 def tile_attend_gsink_v_kernel(tc, uT, vT, su, sv, y, offs, qoffs, out):
     nc = tc.nc
     four = range(PACK)
+    halves = (slice(0, HALF), slice(HALF, SLOTS))
 
     def block(n):
         return slice(n * P, (n + 1) * P)
+
+    def flat(t):
+        return t[:].rearrange("p a b -> p (a b)")
 
     with ExitStack() as ctx:
         sb = ctx.enter_context(tc.tile_pool(name="sb", bufs=1))
@@ -54,15 +61,14 @@ def tile_attend_gsink_v_kernel(tc, uT, vT, su, sv, y, offs, qoffs, out):
         out_rows = out.rearrange("(p t) c -> p t c", t=PACK)
         u_pool = [sbuf("u_pool%d" % t, [P, POOL], F32) for t in four]
         v_pool = [sbuf("v_pool%d" % t, [P, POOL], F32) for t in four]
-        nc.sync.dma_start(u_pool[0][:], u_rows[:, 0, :])
         nc.sync.dma_start(i_list[:], offs)
-        nc.sync.dma_start(j_list[:], qoffs)
         nc.sync.dma_start(su_pool[P - 1 : P, :], su[0:1, :])
+        nc.sync.dma_start(j_list[:], qoffs)
         nc.sync.dma_start(sv_pool[P - 1 : P, :], sv[0:1, :])
-        for t in range(1, PACK):
-            nc.sync.dma_start(u_pool[t][:], u_rows[:, t, :])
         for t in four:
             nc.sync.dma_start(v_pool[t][:], v_rows[:, t, :])
+        for t in four:
+            nc.sync.dma_start(u_pool[t][:], u_rows[:, t, :])
         y_sb = sbuf("y_sb", [P, PACK, SLOTS], F32)
         nc.sync.dma_start(y_sb[:], y.rearrange("(p r) j -> p r j", r=PACK))
 
@@ -71,181 +77,251 @@ def tile_attend_gsink_v_kernel(tc, uT, vT, su, sv, y, offs, qoffs, out):
         make_identity(nc, ident[:])
         make_identity(nc, ident_bf[:])
 
-        window = []
+        def operand(name, width=SLOTS, over=None):
+            return sbuf(name + "_codes", [P, width], U32, over), sbuf(name + "_scales", [P, width], U8)
 
-        def clear_window(engine, over):
-            cleared = sbuf("window%d" % len(window), [P, POOL], F32, over)
-            engine.memset(cleared[:].bitcast(I32), 0)
-            window.append(cleared)
+        g_codes, g_scales = operand("g", HALF + SLOTS)
+        nc.gpsimd.memset(g_codes[:, 0:HALF], 0)
+        nc.gpsimd.memset(g_scales[:, 0:HALF], 0)
 
+        v_along_d = sbuf("v_along_d", [P, SLOTS, PACK], BF16)
 
-        u_planes = sbuf("u_planes", [P, PACK, SLOTS], BF16)
+        def gather_v(t):
+            nc.vector.tensor_copy(v_along_d[:, :, t], v_pool[t][:].indirect(j_list[:]))
 
-        def gather_u(t):
-            nc.vector.tensor_copy(u_planes[:, t, :], u_pool[t][:].indirect(i_list[:]))
-
-        gather_u(0)
         su_row = sbuf("su_row", [P, SLOTS], F32)
         sv_row = sbuf("sv_row", [P, SLOTS], F32)
         nc.vector.tensor_copy(su_row[:], su_pool[:].indirect(i_list[:]))
         nc.vector.tensor_copy(sv_row[:], sv_pool[:].indirect(j_list[:]))
         su_turned = bank(4, "su_turned")
-        sv_turned = bank(5, "sv_turned")
+        su_dealt_turned = bank(5, "su_dealt_turned")
+        sv_turned = bank(6, "sv_turned")
         for n in four:
-            nc.tensor.transpose(su_turned[:, n, :], su_row[:, n::PACK], ident[:])
+            nc.tensor.transpose(su_turned[:, n, :], su_row[:, block(n)], ident[:])
+        for n in four:
+            nc.tensor.transpose(su_dealt_turned[:, n, :], su_row[:, n::PACK], ident[:])
         for n in four:
             nc.tensor.transpose(sv_turned[:, n, :], sv_row[:, block(n)], ident[:])
         su_col = sbuf("su_col", [P, PACK], F32)
+        su_dealt = sbuf("su_dealt", [P, PACK], F32)
         sv_col = sbuf("sv_col", [P, PACK], F32)
         nc.scalar.copy(su_col[:], su_turned[:, :, P - 1])
+        nc.scalar.copy(su_dealt[:], su_dealt_turned[:, :, P - 1])
         nc.scalar.copy(sv_col[:], sv_turned[:, :, P - 1])
-        sv_spread = bank(6, "sv_spread")
+        sv_spread = bank(7, "sv_spread")
         for n in four:
             nc.tensor.transpose(sv_spread[:, n, :], sv_col[:, n : n + 1].to_broadcast([P, P]), ident[:])
         sv_all = sbuf("sv_all", [P, SLOTS], F32)
-        nc.scalar.copy(sv_all[:], sv_spread[:].rearrange("p n j -> p (n j)"))
-
-        for t in range(1, PACK):
-            gather_u(t)
-        clear_window(nc.gpsimd, "u_pool3")
-
-        u_along_d = sbuf("u_along_d", [P, SLOTS, PACK], BF16)
-        nc.scalar.copy(
-            u_along_d[:].rearrange("p (r s) t -> p s t r", r=PACK),
-            u_planes[:].rearrange("p t (s r) -> p s t r", r=PACK),
-        )
-
-        u_along_i = sbuf("u_along_i", [P, PACK, P, PACK], BF16)
-        for t in four:
-            turned = bank(t, "u_turned%d" % t, BF16)
-            for r in four:
-                nc.tensor.transpose(turned[:, r, :], u_planes[:, t, r::PACK], ident_bf[:])
-            nc.scalar.copy(u_along_i[:, t], turned[:].rearrange("s r p -> s p r"))
-
-        factor_planes = sbuf("factor_planes", [P, PACK, SLOTS], F32, over="u_planes")
+        nc.scalar.copy(sv_all[:], flat(sv_spread))
+        factor_planes = sbuf("factor_planes", [P, PACK, SLOTS], F32)
         for r in four:
-            nc.scalar.activation(factor_planes[:, r, :], sv_all[:], ACT.Copy, scale=su_col[:, r : r + 1])
+            nc.scalar.activation(factor_planes[:, r, :], sv_all[:], ACT.Copy, scale=su_dealt[:, r : r + 1])
         factor = sbuf("factor", [P, SLOTS, PACK], F32)
         nc.scalar.copy(factor[:], factor_planes[:].rearrange("s r j -> s j r"))
 
-        v_along_d = sbuf("v_along_d", [P, SLOTS, PACK], BF16)
-
-        def gather_v(t, first=0, last=SLOTS):
-            nc.vector.tensor_copy(
-                v_along_d[:, first:last, t], v_pool[t][:].indirect(j_list[:, first // 16 : last // 16])
-            )
-
-        def operand(name, over=None):
-            return sbuf(name + "_codes", [P, SLOTS], U32, over), sbuf(name + "_scales", [P, SLOTS], U8)
+        for t in four:
+            gather_v(t)
+        window = [sbuf("window%d" % t, [P, POOL], F32, over="v_pool%d" % t) for t in range(PACK - 1)]
+        for cleared in window:
+            nc.gpsimd.memset(cleared[:].bitcast(I32), 0)
 
         v_codes, v_scales = operand("v")
-        g_codes, g_scales = operand("g")
+        nc.vector.quantize_mx(v_codes[:].bitcast(E4M3), v_scales[:], flat(v_along_d))
 
-        gather_v(0)
-        gather_v(1)
-        ud_codes, ud_scales = operand("ud", over="v_pool1")
-        nc.vector.quantize_mx(ud_codes[:].bitcast(E4M3), ud_scales[:], u_along_d[:].rearrange("p n t -> p (n t)"))
-        gather_v(2)
-        halves = (slice(0, SLOTS // 2), slice(SLOTS // 2, SLOTS))
-        for half in halves:
-            gather_v(3, half.start, half.stop)
-        for half in halves:
-            nc.vector.quantize_mx(
-                v_codes[:, half].bitcast(E4M3), v_scales[:, half], v_along_d[:, half, :].rearrange("p n t -> p (n t)")
+        u_along_d = sbuf("u_along_d", [P, SLOTS, PACK], BF16)
+        u_along_i = sbuf("u_along_i", [P, PACK, P, PACK], BF16, over="factor_planes")
+        ud_codes, ud_scales = operand("ud")
+
+        def gather_u(t, part=slice(0, SLOTS)):
+            nc.vector.tensor_copy(
+                u_along_d[:, part, t], u_pool[t][:].indirect(i_list[:, part.start // 16 : part.stop // 16])
             )
+
+        u_pair = sbuf("u_pair", [P, 2, SLOTS], BF16)
+        u_plane = [u_pair[:, 0, :], u_pair[:, 1, :]]
+        u_plane += [sbuf("u_plane2", [P, SLOTS], BF16)[:], u_along_d[:, :, 3]]
+
+        def gather_plane(t):
+            nc.vector.tensor_copy(u_plane[t], u_pool[t][:].indirect(i_list[:]))
+
+        u_turned = {}
+
+        def turn_u(t, n):
+            u_turned[t] = bank(n, "u_turned%d" % t, BF16)
+            for r in four:
+                nc.tensor.transpose(u_turned[t][:, r, :], u_plane[t][:, r::PACK], ident_bf[:])
+
+        def lay_u(t):
+            nc.scalar.copy(u_along_i[:, t], u_turned[t][:].rearrange("s r p -> s p r"))
+
+        def quantise_ud(half):
+            nc.vector.quantize_mx(
+                ud_codes[:, half].bitcast(E4M3), ud_scales[:, half], u_along_d[:, half, :].rearrange("p n t -> p (n t)")
+            )
+
+        gather_plane(0)
+        turn_u(0, 0)
+        lay_u(0)
+        gather_plane(1)
+        turn_u(1, 1)
+        lay_u(1)
+        nc.vector.tensor_copy(u_along_d[:, :, 0:2], u_pair[:].rearrange("p t i -> p i t"))
+        gather_plane(2)
+        nc.vector.tensor_copy(u_along_d[:, :, 2], u_plane[2])
+        turn_u(2, 2)
+        lay_u(2)
 
         scores = []
-        for r in four:
-            a = bank(r, "scores%d" % r)
-            for half in halves:
-                nc.tensor.matmul_mx(
-                    a[:].rearrange("p n j -> p (n j)")[:, half],
-                    lhsT=ud_codes[:, block(r)].bitcast(E4M3), lhsT_scale=ud_scales[:, block(r)],
-                    rhs=v_codes[:, half].bitcast(E4M3), rhs_scale=v_scales[:, half], start=True, stop=True,
-                )
+
+        def score(q):
+            a = bank(q, "scores%d" % q)
+            nc.tensor.matmul_mx(
+                flat(a), lhsT=ud_codes[:, block(q)].bitcast(E4M3), lhsT_scale=ud_scales[:, block(q)],
+                rhs=v_codes[:].bitcast(E4M3), rhs_scale=v_scales[:], start=True, stop=True,
+            )
             scores.append(a)
 
-        clear_window(nc.gpsimd, "v_along_d")
-        clear_window(nc.gpsimd, "v_pool1")
+        z = [sbuf("z%d" % q, [P, SLOTS], F32) for q in four]
+        e = [sbuf("e%d" % q, [P, SLOTS], F32) for q in four]
+        f = [sbuf("f%d" % q, [P, SLOTS], F32) for q in four]
+        soft_sum = [sbuf("soft_sum%d" % q, [P, 1], F32) for q in range(2)]
+        neg_shift = [sbuf("neg_shift%d" % q, [P, 1], F32) for q in four]
+        row_sum = [sbuf("row_sum%d" % q, [P, 1], F32) for q in four]
+        row_inv = [sbuf("row_inv%d" % q, [P, 1], F32) for q in four]
 
-        y_turned = []
-        for n in four:
-            turned = bank(4 + n, "y_turned%d" % n)
-            for r in four:
-                nc.tensor.transpose(turned[:, r, :], y_sb[:, r, block(n)], ident[:])
-            y_turned.append(turned)
+        def logits(q):
+            nc.vector.scalar_tensor_tensor(z[q][:], flat(scores[q]), su_col[:, q : q + 1], sv_all[:], ALU.mult, ALU.mult)
 
-        z = [sbuf("z%d" % r, [P, SLOTS], F32) for r in four]
-        e = [sbuf("e%d" % r, [P, SLOTS], F32) for r in four]
-        f = [sbuf("f%d" % r, [P, SLOTS], F32) for r in four]
-        neg_max = [sbuf("neg_max%d" % r, [P, 1], F32) for r in four]
-        row_sum = [sbuf("row_sum%d" % r, [P, 1], F32) for r in four]
-        row_inv = [sbuf("row_inv%d" % r, [P, 1], F32) for r in four]
+        def soft_bound(q):
+            nc.scalar.activation(e[q][:], z[q][:], ACT.Exp, scale=1.0 / SOFTEN, accum_out=soft_sum[q][:])
 
-        def logits(r):
-            nc.vector.scalar_tensor_tensor(
-                z[r][:], scores[r][:].rearrange("p n j -> p (n j)"), su_col[:, r : r + 1], sv_all[:], ALU.mult, ALU.mult
+        def soft_shift(q):
+            per_bit = SOFTEN * math.log(2.0)
+            nc.vector.tensor_scalar(
+                neg_shift[q][:], soft_sum[q][:].bitcast(I32), -per_bit / 2.0**23, per_bit * (127 + 9), ALU.mult, ALU.add
             )
 
-        def exponent(r):
-            nc.vector.tensor_reduce(neg_max[r][:], z[r][:], AXIS.X, ALU.max, negate=True)
-            nc.scalar.activation(e[r][:], z[r][:], ACT.Exp, bias=neg_max[r][:], accum_out=row_sum[r][:])
+        def row_max(q):
+            nc.vector.tensor_reduce(neg_shift[q][:], z[q][:], AXIS.X, ALU.max, negate=True)
 
-        def invert(r):
-            nc.vector.reciprocal(row_inv[r][:], row_sum[r][:])
+        def exponent(q):
+            nc.scalar.activation(e[q][:], z[q][:], ACT.Exp, bias=neg_shift[q][:], accum_out=row_sum[q][:])
 
-        def normalise(r):
-            nc.vector.tensor_scalar(f[r][:], e[r][:], row_inv[r][:], None, ALU.mult)
+        def invert(q):
+            nc.vector.reciprocal(row_inv[q][:], row_sum[q][:])
 
+        def normalise(q, cols=slice(0, SLOTS)):
+            nc.vector.tensor_scalar(f[q][:, cols], e[q][:, cols], row_inv[q][:], None, ALU.mult)
+
+        y_turned = {}
+
+        def turn_y(n):
+            y_turned[n] = bank(4 + n, "y_turned%d" % n)
+            for r in four:
+                nc.tensor.transpose(y_turned[n][:, r, :], y_sb[:, r, block(n)], ident[:])
+
+        gather_u(3, halves[0])
+        quantise_ud(halves[0])
+        score(0)
+        score(1)
+        gather_u(3, halves[1])
         logits(0)
+        soft_bound(0)
+        quantise_ud(halves[1])
+        score(2)
+        score(3)
         logits(1)
+        soft_bound(1)
+        soft_shift(0)
         exponent(0)
         logits(2)
+        soft_shift(1)
         exponent(1)
-        invert(0)
-        nc.scalar.activation(f[0][:], e[0][:], ACT.Copy, scale=row_inv[0][:])
         logits(3)
+        row_max(2)
         exponent(2)
-        invert(1)
+        invert(0)
+        row_max(3)
         exponent(3)
+        invert(1)
+        turn_y(0)
+        turn_y(1)
+        nc.gpsimd.tensor_scalar(f[0][:], e[0][:], row_inv[0][:], 0.0, ALU.mult, ALU.add)
         invert(2)
         normalise(1)
         normalise(2)
         invert(3)
-        normalise(3)
-        ui_codes, ui_scales = operand("ui", over="e3")
-        nc.vector.quantize_mx(ui_codes[:].bitcast(E4M3), ui_scales[:], u_along_i[:].rearrange("s t p r -> s (t p r)"))
+        normalise(3, block(0))
+        normalise(3, slice(P, SLOTS))
+        ui = {}
+
+        def quantise_ui(first, over):
+            codes, scales = operand("ui%d" % first, 2 * P, over)
+            nc.vector.quantize_mx(
+                codes[:].bitcast(E4M3), scales[:], u_along_i[:, first : first + 2].rearrange("s t p r -> s (t p r)")
+            )
+            for t in range(2):
+                ui[first + t] = (codes[:, block(t)], scales[:, block(t)])
+
+        quantise_ui(0, "e3")
 
         f_turned = [bank(n, "f_turned%d" % n) for n in four]
 
-        def turn(n, r):
-            nc.tensor.transpose(f_turned[n][:, r, :], f[r][:, block(n)], ident[:])
-
-        for r in four:
-            for n in four:
-                turn(n, r)
+        def turn_f(n, q):
+            nc.tensor.transpose(f_turned[n][:, q, :], f[q][:, block(n)], ident[:])
 
         col_sum = [sbuf("col_sum%d" % n, [P, 1], F32) for n in four]
         col_inv = [sbuf("col_inv%d" % n, [P, 1], F32) for n in four]
-        f_cols = [sbuf("f_cols%d" % n, [P, SLOTS], F32) for n in four]
+        f_cols = [sbuf("f_cols%d" % n, [P, PACK, P], F32) for n in four]
         gap = [sbuf("gap%d" % n, [P, SLOTS], F32) for n in four]
         g_along_i = sbuf("g_along_i", [P, SLOTS, PACK], BF16)
         back = []
 
         def column_sum(n):
             nc.scalar.activation(
-                f_cols[n][:], f_turned[n][:].rearrange("j r s -> j (r s)"), ACT.Copy, accum_out=col_sum[n][:]
+                f_cols[n][:], flat(f_turned[n]).rearrange("j (s r) -> j r s", r=PACK), ACT.Copy, accum_out=col_sum[n][:]
             )
             nc.vector.reciprocal(col_inv[n][:], col_sum[n][:])
 
+        def dealt(n):
+            return flat(f_turned[n]).rearrange("j (s r) -> j r s", r=PACK)
+
+        last_rows = P // 2
+        part_sum = sbuf("part_sum", [P, 1], F32)
+        for q in range(2):
+            for n in four:
+                turn_f(n, q)
+        nc.scalar.activation(f_cols[0][:, :, 0:last_rows], dealt(0)[:, :, 0:last_rows], ACT.Copy, accum_out=part_sum[:])
+        for q in range(2, PACK):
+            for n in four:
+                turn_f(n, q)
+        turn_y(2)
+        turn_y(3)
+        neg_y = sbuf("neg_y", [P, SLOTS], F32, over="z3")
+        nc.scalar.activation(neg_y[:], flat(y_turned[3]), ACT.Copy, scale=-1.0)
+        turn_u(3, 7)
+        nc.vector.tensor_scalar(
+            f_cols[0][:, :, last_rows:], dealt(0)[:, :, last_rows:], 1.0, part_sum[:], ALU.mult, ALU.add,
+            accum_out=col_sum[0][:],
+        )
+        nc.vector.reciprocal(col_inv[0][:], col_sum[0][:])
+
         def difference(n):
             nc.vector.scalar_tensor_tensor(
-                gap[n][:], f_cols[n][:], col_inv[n][:], y_turned[n][:].rearrange("j r s -> j (r s)"),
-                ALU.mult, ALU.subtract,
+                gap[n][:], flat(f_cols[n]), col_inv[n][:], flat(y_turned[n]), ALU.mult, ALU.subtract
             )
             h = bank(n, "back%d" % n)
             for r in four:
                 nc.tensor.transpose(h[:, r, :], gap[n][:, block(r)], ident[:])
+            back.append(h)
+
+        def difference_in_psum(n):
+            scaled = sbuf("scaled%d" % n, [P, SLOTS], F32)
+            nc.scalar.activation(scaled[:], flat(f_cols[n]), ACT.Copy, scale=col_inv[n][:])
+            h = bank(4 + n, "back%d" % n)
+            for r in four:
+                nc.tensor.matmul(h[:, r, :], neg_y[:, block(r)], ident[:], start=True, stop=False, is_transpose=True)
+                nc.tensor.matmul(h[:, r, :], scaled[:, block(r)], ident[:], start=False, stop=True, is_transpose=True)
             back.append(h)
 
         def gradient(n):
@@ -253,62 +329,46 @@ def tile_attend_gsink_v_kernel(tc, uT, vT, su, sv, y, offs, qoffs, out):
                 g_along_i[:, block(n), :], back[n][:].rearrange("s r j -> s j r"), factor[:, block(n), :], ALU.mult
             )
 
-        def quantise_gradient(n):
+        def quantise_gradient(half):
+            cols = slice(HALF + half.start, HALF + half.stop)
             nc.vector.quantize_mx(
-                g_codes[:, block(n)].bitcast(E5M2), g_scales[:, block(n)],
-                g_along_i[:, block(n), :].rearrange("s j r -> s (j r)"),
+                g_codes[:, cols].bitcast(E5M2), g_scales[:, cols], g_along_i[:, half, :].rearrange("s j r -> s (j r)")
             )
 
-        early_planes = 2
-
-        def early_product():
-            acc = bank(4, "early")
+        def product(t, n, cols):
+            acc = bank(n, "dv%d_%d" % (t, cols.start))
             nc.tensor.matmul_mx(
-                acc[:].rearrange("j t p -> j (t p)"),
-                lhsT=g_codes[:, block(0)].bitcast(E5M2), lhsT_scale=g_scales[:, block(0)],
-                rhs=ui_codes[:].bitcast(E4M3), rhs_scale=ui_scales[:], start=True, stop=True,
+                flat(acc), lhsT=ui[t][0].bitcast(E4M3), lhsT_scale=ui[t][1],
+                rhs=g_codes[:, cols].bitcast(E5M2), rhs_scale=g_scales[:, cols], start=True, stop=True,
             )
-            rows = sbuf("early_rows", [P, early_planes, P], F32)
-            nc.scalar.copy(rows[:], acc[:, 0:early_planes, :])
-            turned = bank(5, "early_turned")
-            for t in range(early_planes):
-                nc.tensor.transpose(turned[:, t, :], rows[:, t, :], ident[:])
-            cols = sbuf("early_cols", [P, early_planes, P], F32)
-            nc.scalar.copy(cols[:], turned[:, 0:early_planes, :])
-            return cols
+            return flat(acc)
 
-        column_sum(0)
+        def place(t, part, sums):
+            dv = sbuf("dv_sb%d_%d" % (t, part.start), [P, part.stop - part.start], F32)
+            nc.scalar.copy(dv[:], sums)
+            target = window[t % len(window)]
+            nc.vector.tensor_copy(target[:].indirect(j_list[:, part.start // 16 : part.stop // 16]), dv[:])
+
         difference(0)
         column_sum(1)
         difference(1)
         column_sum(2)
-        gradient(0)
         difference(2)
-        quantise_gradient(0)
-        early_cols = early_product()
         column_sum(3)
+        lay_u(3)
+        difference_in_psum(3)
+        gradient(0)
         gradient(1)
-        difference(3)
+        quantise_gradient(halves[0])
+        early = product(0, 4, slice(0, SLOTS))
         gradient(2)
-        quantise_gradient(1)
         gradient(3)
-        quantise_gradient(2)
-        quantise_gradient(3)
-        zeros = sbuf("zeros", [P, P], F32, over="factor")
-        nc.gpsimd.memset(zeros[:], 0.0)
+        quantise_gradient(halves[1])
+        quantise_ui(2, "g_along_i")
 
-        for t in range(early_planes):
-            nc.vector.tensor_tensor(window[t][:].indirect(j_list[:, 0 : P // 16]), early_cols[:, t, :], zeros[:], ALU.add)
+        place(0, halves[0], early[:, halves[1]])
         for t in four:
-            acc = bank(4 + (t + 2) % PACK, "dv%d" % t)
-            nc.tensor.matmul_mx(
-                acc[:].rearrange("p n j -> p (n j)"),
-                lhsT=ui_codes[:, block(t)].bitcast(E4M3), lhsT_scale=ui_scales[:, block(t)],
-                rhs=g_codes[:].bitcast(E5M2), rhs_scale=g_scales[:], start=True, stop=True,
-            )
-            first = P if t < early_planes else 0
-            dv = sbuf("dv_sb%d" % t, [P, SLOTS - first], F32)
-            nc.scalar.copy(dv[:], acc[:].rearrange("p n j -> p (n j)")[:, first:])
-            target = window[t % len(window)]
-            nc.vector.tensor_copy(target[:].indirect(j_list[:, first // 16 :]), dv[:])
-            nc.sync.dma_start(out_rows[:, t, :], target[:])
+            sums = product(t, 4 + (t + 1) % PACK, slice(HALF, HALF + SLOTS))
+            part = halves[1] if t == 0 else slice(0, SLOTS)
+            place(t, part, sums[:, part])
+            nc.sync.dma_start(out_rows[:, t, :], window[t % len(window)][:])

@@ -129,7 +129,7 @@ def tile_attend_gsink_v_kernel(tc, uT, vT, su, sv, y, offs, qoffs, out):
         nc.vector.quantize_mx(v_codes[:].bitcast(E4M3), v_scales[:], flat(v_along_d))
 
         u_along_d = sbuf("u_along_d", [P, SLOTS, PACK], BF16)
-        u_along_i = sbuf("u_along_i", [P, PACK, P, PACK], BF16, over="factor_planes")
+        u_along_i = sbuf("u_along_i", [P, PACK - 1, P, PACK], BF16, over="factor_planes")
         ud_codes, ud_scales = operand("ud")
 
         def gather_u(t, part=slice(0, SLOTS)):
@@ -139,7 +139,7 @@ def tile_attend_gsink_v_kernel(tc, uT, vT, su, sv, y, offs, qoffs, out):
 
         u_pair = sbuf("u_pair", [P, 2, SLOTS], BF16)
         u_plane = [u_pair[:, 0, :], u_pair[:, 1, :]]
-        u_plane += [sbuf("u_plane2", [P, SLOTS], BF16)[:], u_along_d[:, :, 3]]
+        u_plane += [sbuf("u_plane%d" % t, [P, SLOTS], BF16)[:] for t in range(2, PACK)]
 
         def gather_plane(t):
             nc.vector.tensor_copy(u_plane[t], u_pool[t][:].indirect(i_list[:]))
@@ -151,8 +151,8 @@ def tile_attend_gsink_v_kernel(tc, uT, vT, su, sv, y, offs, qoffs, out):
             for r in four:
                 nc.tensor.transpose(u_turned[t][:, r, :], u_plane[t][:, r::PACK], ident_bf[:])
 
-        def lay_u(t):
-            nc.scalar.copy(u_along_i[:, t], u_turned[t][:].rearrange("s r p -> s p r"))
+        def lay_u(t, into):
+            nc.scalar.copy(into, u_turned[t][:].rearrange("s r p -> s p r"))
 
         def quantise_ud(half):
             nc.vector.quantize_mx(
@@ -161,15 +161,15 @@ def tile_attend_gsink_v_kernel(tc, uT, vT, su, sv, y, offs, qoffs, out):
 
         gather_plane(0)
         turn_u(0, 0)
-        lay_u(0)
+        lay_u(0, u_along_i[:, 0])
         gather_plane(1)
         turn_u(1, 1)
-        lay_u(1)
+        lay_u(1, u_along_i[:, 1])
         nc.vector.tensor_copy(u_along_d[:, :, 0:2], u_pair[:].rearrange("p t i -> p i t"))
         gather_plane(2)
         nc.vector.tensor_copy(u_along_d[:, :, 2], u_plane[2])
         turn_u(2, 2)
-        lay_u(2)
+        lay_u(2, u_along_i[:, 2])
 
         scores = []
 
@@ -215,8 +215,8 @@ def tile_attend_gsink_v_kernel(tc, uT, vT, su, sv, y, offs, qoffs, out):
 
         y_turned = {}
 
-        def turn_y(n):
-            y_turned[n] = bank(4 + n, "y_turned%d" % n)
+        def turn_y(n, into):
+            y_turned[n] = bank(into, "y_turned%d" % n)
             for r in four:
                 nc.tensor.transpose(y_turned[n][:, r, :], y_sb[:, r, block(n)], ident[:])
 
@@ -228,8 +228,10 @@ def tile_attend_gsink_v_kernel(tc, uT, vT, su, sv, y, offs, qoffs, out):
         logits(0)
         soft_bound(0)
         quantise_ud(halves[1])
+        nc.scalar.copy(u_plane[3], u_along_d[:, :, 3])
         score(2)
         score(3)
+        turn_u(3, 6)
         logits(1)
         soft_bound(1)
         soft_shift(0)
@@ -244,8 +246,8 @@ def tile_attend_gsink_v_kernel(tc, uT, vT, su, sv, y, offs, qoffs, out):
         row_max(3)
         exponent(3)
         invert(1)
-        turn_y(0)
-        turn_y(1)
+        turn_y(0, 4)
+        turn_y(3, 5)
         nc.gpsimd.tensor_scalar(f[0][:], e[0][:], row_inv[0][:], 0.0, ALU.mult, ALU.add)
         invert(2)
         normalise(1)
@@ -255,15 +257,17 @@ def tile_attend_gsink_v_kernel(tc, uT, vT, su, sv, y, offs, qoffs, out):
         normalise(3, slice(P, SLOTS))
         ui = {}
 
-        def quantise_ui(first, over):
+        def quantise_ui(first, over, sources):
             codes, scales = operand("ui%d" % first, 2 * P, over)
-            nc.vector.quantize_mx(
-                codes[:].bitcast(E4M3), scales[:], u_along_i[:, first : first + 2].rearrange("s t p r -> s (t p r)")
-            )
+            at = 0
+            for source in sources:
+                cols = slice(at, at + source.shape[1] // PACK)
+                nc.vector.quantize_mx(codes[:, cols].bitcast(E4M3), scales[:, cols], source)
+                at = cols.stop
             for t in range(2):
                 ui[first + t] = (codes[:, block(t)], scales[:, block(t)])
 
-        quantise_ui(0, "e3")
+        quantise_ui(0, "e3", [u_along_i[:, 0:2].rearrange("s t p r -> s (t p r)")])
 
         f_turned = [bank(n, "f_turned%d" % n) for n in four]
 
@@ -292,25 +296,26 @@ def tile_attend_gsink_v_kernel(tc, uT, vT, su, sv, y, offs, qoffs, out):
             for n in four:
                 turn_f(n, q)
         nc.scalar.activation(f_cols[0][:, :, 0:last_rows], dealt(0)[:, :, 0:last_rows], ACT.Copy, accum_out=part_sum[:])
+        neg_y = sbuf("neg_y", [P, SLOTS], F32, over="z3")
+        nc.scalar.activation(neg_y[:], flat(y_turned[3]), ACT.Copy, scale=-1.0)
+        u_last_along_i = sbuf("u_last_along_i", [P, P, PACK], BF16, over="e2")
+        lay_u(3, u_last_along_i[:])
         for q in range(2, PACK):
             for n in four:
                 turn_f(n, q)
-        turn_y(2)
-        turn_y(3)
-        neg_y = sbuf("neg_y", [P, SLOTS], F32, over="z3")
-        nc.scalar.activation(neg_y[:], flat(y_turned[3]), ACT.Copy, scale=-1.0)
-        turn_u(3, 7)
         nc.vector.tensor_scalar(
             f_cols[0][:, :, last_rows:], dealt(0)[:, :, last_rows:], 1.0, part_sum[:], ALU.mult, ALU.add,
             accum_out=col_sum[0][:],
         )
         nc.vector.reciprocal(col_inv[0][:], col_sum[0][:])
 
-        def difference(n):
+        turn_y(1, 0)
+
+        def difference(n, into):
             nc.vector.scalar_tensor_tensor(
                 gap[n][:], flat(f_cols[n]), col_inv[n][:], flat(y_turned[n]), ALU.mult, ALU.subtract
             )
-            h = bank(n, "back%d" % n)
+            h = bank(into, "back%d" % n)
             for r in four:
                 nc.tensor.transpose(h[:, r, :], gap[n][:, block(r)], ident[:])
             back.append(h)
@@ -318,7 +323,7 @@ def tile_attend_gsink_v_kernel(tc, uT, vT, su, sv, y, offs, qoffs, out):
         def difference_in_psum(n):
             scaled = sbuf("scaled%d" % n, [P, SLOTS], F32)
             nc.scalar.activation(scaled[:], flat(f_cols[n]), ACT.Copy, scale=col_inv[n][:])
-            h = bank(4 + n, "back%d" % n)
+            h = bank(n, "back%d" % n)
             for r in four:
                 nc.tensor.matmul(h[:, r, :], neg_y[:, block(r)], ident[:], start=True, stop=False, is_transpose=True)
                 nc.tensor.matmul(h[:, r, :], scaled[:, block(r)], ident[:], start=False, stop=True, is_transpose=True)
@@ -349,13 +354,13 @@ def tile_attend_gsink_v_kernel(tc, uT, vT, su, sv, y, offs, qoffs, out):
             target = window[t % len(window)]
             nc.vector.tensor_copy(target[:].indirect(j_list[:, part.start // 16 : part.stop // 16]), dv[:])
 
-        difference(0)
         column_sum(1)
-        difference(1)
+        turn_y(2, 1)
+        difference(0, 6)
+        difference(1, 7)
         column_sum(2)
-        difference(2)
+        difference(2, 2)
         column_sum(3)
-        lay_u(3)
         difference_in_psum(3)
         gradient(0)
         gradient(1)
@@ -364,7 +369,7 @@ def tile_attend_gsink_v_kernel(tc, uT, vT, su, sv, y, offs, qoffs, out):
         gradient(2)
         gradient(3)
         quantise_gradient(halves[1])
-        quantise_ui(2, "g_along_i")
+        quantise_ui(2, "g_along_i", [u_along_i[:, 2].rearrange("s p r -> s (p r)"), flat(u_last_along_i)])
 
         place(0, halves[0], early[:, halves[1]])
         for t in four:

@@ -225,32 +225,33 @@ def tile_attend_gsink_v_kernel(tc, uT, vT, su, sv, y, offs, qoffs, out):
         score(0)
         score(1)
         gather_u(3, halves[1])
-        logits(0)
-        soft_bound(0)
         quantise_ud(halves[1])
-        nc.scalar.copy(u_plane[3], u_along_d[:, :, 3])
+        nc.scalar.copy(
+            u_plane[3].rearrange("p (r s) -> p r s", r=PACK), u_along_d[:, :, 3].rearrange("p (s r) -> p r s", r=PACK)
+        )
         score(2)
         score(3)
-        turn_u(3, 6)
+        for n in four:
+            turn_y(n, 4 + n)
+        logits(0)
+        soft_bound(0)
         logits(1)
         soft_bound(1)
+        logits(2)
         soft_shift(0)
         exponent(0)
-        logits(2)
+        logits(3)
         soft_shift(1)
         exponent(1)
-        logits(3)
         row_max(2)
         exponent(2)
         invert(0)
         row_max(3)
         exponent(3)
         invert(1)
-        turn_y(0, 4)
-        turn_y(3, 5)
-        nc.gpsimd.tensor_scalar(f[0][:], e[0][:], row_inv[0][:], 0.0, ALU.mult, ALU.add)
-        invert(2)
+        normalise(0)
         normalise(1)
+        invert(2)
         normalise(2)
         invert(3)
         normalise(3, block(0))
@@ -258,16 +259,17 @@ def tile_attend_gsink_v_kernel(tc, uT, vT, su, sv, y, offs, qoffs, out):
         ui = {}
 
         def quantise_ui(first, over, sources):
-            codes, scales = operand("ui%d" % first, 2 * P, over)
+            width = sum(source.shape[1] for source in sources) // PACK
+            codes, scales = operand("ui%d" % first, width, over)
             at = 0
             for source in sources:
                 cols = slice(at, at + source.shape[1] // PACK)
                 nc.vector.quantize_mx(codes[:, cols].bitcast(E4M3), scales[:, cols], source)
                 at = cols.stop
-            for t in range(2):
+            for t in range(width // P):
                 ui[first + t] = (codes[:, block(t)], scales[:, block(t)])
 
-        quantise_ui(0, "e3", [u_along_i[:, 0:2].rearrange("s t p r -> s (t p r)")])
+        quantise_ui(0, "e3", [u_along_i[:, 0:2].rearrange("s t p r -> s (t p r)"), u_along_i[:, 2].rearrange("s p r -> s (p r)")])
 
         f_turned = [bank(n, "f_turned%d" % n) for n in four]
 
@@ -281,35 +283,26 @@ def tile_attend_gsink_v_kernel(tc, uT, vT, su, sv, y, offs, qoffs, out):
         g_along_i = sbuf("g_along_i", [P, SLOTS, PACK], BF16)
         back = []
 
-        def column_sum(n):
-            nc.scalar.activation(
-                f_cols[n][:], flat(f_turned[n]).rearrange("j (s r) -> j r s", r=PACK), ACT.Copy, accum_out=col_sum[n][:]
-            )
-            nc.vector.reciprocal(col_inv[n][:], col_sum[n][:])
-
         def dealt(n):
             return flat(f_turned[n]).rearrange("j (s r) -> j r s", r=PACK)
 
-        last_rows = P // 2
-        part_sum = sbuf("part_sum", [P, 1], F32)
-        for q in range(2):
-            for n in four:
-                turn_f(n, q)
-        nc.scalar.activation(f_cols[0][:, :, 0:last_rows], dealt(0)[:, :, 0:last_rows], ACT.Copy, accum_out=part_sum[:])
+        def column_sum(n):
+            nc.scalar.activation(f_cols[n][:], dealt(n), ACT.Copy, accum_out=col_sum[n][:])
+
+        def column_sum_on_vector(n):
+            nc.vector.tensor_scalar(f_cols[n][:], dealt(n), 1.0, None, ALU.mult, ALU.add, accum_out=col_sum[n][:])
+
+        def invert_column(n):
+            nc.vector.reciprocal(col_inv[n][:], col_sum[n][:])
+
         neg_y = sbuf("neg_y", [P, SLOTS], F32, over="z3")
         nc.scalar.activation(neg_y[:], flat(y_turned[3]), ACT.Copy, scale=-1.0)
-        u_last_along_i = sbuf("u_last_along_i", [P, P, PACK], BF16, over="e2")
-        lay_u(3, u_last_along_i[:])
-        for q in range(2, PACK):
+        for q in four:
             for n in four:
                 turn_f(n, q)
-        nc.vector.tensor_scalar(
-            f_cols[0][:, :, last_rows:], dealt(0)[:, :, last_rows:], 1.0, part_sum[:], ALU.mult, ALU.add,
-            accum_out=col_sum[0][:],
-        )
-        nc.vector.reciprocal(col_inv[0][:], col_sum[0][:])
-
-        turn_y(1, 0)
+        last_back = bank(7, "back3")
+        for r in four:
+            nc.tensor.matmul(last_back[:, r, :], neg_y[:, block(r)], ident[:], start=r == 0, stop=False, is_transpose=True)
 
         def difference(n, into):
             nc.vector.scalar_tensor_tensor(
@@ -323,11 +316,11 @@ def tile_attend_gsink_v_kernel(tc, uT, vT, su, sv, y, offs, qoffs, out):
         def difference_in_psum(n):
             scaled = sbuf("scaled%d" % n, [P, SLOTS], F32)
             nc.scalar.activation(scaled[:], flat(f_cols[n]), ACT.Copy, scale=col_inv[n][:])
-            h = bank(n, "back%d" % n)
             for r in four:
-                nc.tensor.matmul(h[:, r, :], neg_y[:, block(r)], ident[:], start=True, stop=False, is_transpose=True)
-                nc.tensor.matmul(h[:, r, :], scaled[:, block(r)], ident[:], start=False, stop=True, is_transpose=True)
-            back.append(h)
+                nc.tensor.matmul(
+                    last_back[:, r, :], scaled[:, block(r)], ident[:], start=False, stop=r == PACK - 1, is_transpose=True
+                )
+            back.append(last_back)
 
         def gradient(n):
             nc.vector.tensor_tensor(
@@ -354,26 +347,35 @@ def tile_attend_gsink_v_kernel(tc, uT, vT, su, sv, y, offs, qoffs, out):
             target = window[t % len(window)]
             nc.vector.tensor_copy(target[:].indirect(j_list[:, part.start // 16 : part.stop // 16]), dv[:])
 
-        column_sum(1)
-        turn_y(2, 1)
-        difference(0, 6)
-        difference(1, 7)
+        column_sum(0)
+        column_sum_on_vector(1)
         column_sum(2)
-        difference(2, 2)
         column_sum(3)
+        u_turned[3] = bank(0, "u_turned3", BF16)
+        for r in four:
+            nc.tensor.transpose(u_turned[3][:, r, :], u_plane[3][:, block(r)], ident_bf[:])
+        invert_column(0)
+        invert_column(1)
+        difference(0, 4)
+        invert_column(2)
+        difference(1, 5)
+        invert_column(3)
+        difference(2, 6)
         difference_in_psum(3)
+        u_last_along_i = sbuf("u_last_along_i", [P, P, PACK], BF16)
+        lay_u(3, u_last_along_i[:])
         gradient(0)
         gradient(1)
         quantise_gradient(halves[0])
-        early = product(0, 4, slice(0, SLOTS))
+        early = product(0, 1, slice(0, SLOTS))
         gradient(2)
         gradient(3)
         quantise_gradient(halves[1])
-        quantise_ui(2, "g_along_i", [u_along_i[:, 2].rearrange("s p r -> s (p r)"), flat(u_last_along_i)])
+        quantise_ui(3, "g_along_i", [flat(u_last_along_i)])
 
         place(0, halves[0], early[:, halves[1]])
         for t in four:
-            sums = product(t, 4 + (t + 1) % PACK, slice(HALF, HALF + SLOTS))
+            sums = product(t, (t + 2) % PACK, slice(HALF, HALF + SLOTS))
             part = halves[1] if t == 0 else slice(0, SLOTS)
             place(t, part, sums[:, part])
             nc.sync.dma_start(out_rows[:, t, :], window[t % len(window)][:])

@@ -20,6 +20,7 @@ P = 128
 PACK = 4
 SLOTS = 512
 HALF = SLOTS // 2
+PAD = SLOTS - P
 POOL = 2048
 FEATURES = 512
 SOFTEN = 8.0
@@ -60,13 +61,14 @@ def tile_attend_gsink_v_kernel(tc, uT, vT, su, sv, y, offs, qoffs, out):
         v_rows = vT.rearrange("(p t) c -> p t c", t=PACK)
         out_rows = out.rearrange("(p t) c -> p t c", t=PACK)
         u_pool = [sbuf("u_pool%d" % t, [P, POOL], F32) for t in four]
-        v_pool = [sbuf("v_pool%d" % t, [P, POOL], F32) for t in four]
-        nc.sync.dma_start(i_list[:], offs)
-        nc.sync.dma_start(su_pool[P - 1 : P, :], su[0:1, :])
+        v_pair = [sbuf("v_pair%d" % h, [P, 2, POOL], F32) for h in range(2)]
+        v_pool = [v_pair[t // 2][:, t % 2, :] for t in four]
         nc.sync.dma_start(j_list[:], qoffs)
-        nc.sync.dma_start(sv_pool[P - 1 : P, :], sv[0:1, :])
-        for t in four:
-            nc.sync.dma_start(v_pool[t][:], v_rows[:, t, :])
+        nc.sync.dma_start(i_list[:], offs)
+        nc.scalar.dma_start(sv_pool[P - 1 : P, :], sv[0:1, :])
+        nc.scalar.dma_start(su_pool[P - 1 : P, :], su[0:1, :])
+        for h in range(2):
+            nc.sync.dma_start(v_pair[h][:], v_rows[:, 2 * h : 2 * h + 2, :])
         for t in four:
             nc.sync.dma_start(u_pool[t][:], u_rows[:, t, :])
         y_sb = sbuf("y_sb", [P, PACK, SLOTS], F32)
@@ -80,14 +82,16 @@ def tile_attend_gsink_v_kernel(tc, uT, vT, su, sv, y, offs, qoffs, out):
         def operand(name, width=SLOTS, over=None):
             return sbuf(name + "_codes", [P, width], U32, over), sbuf(name + "_scales", [P, width], U8)
 
-        g_codes, g_scales = operand("g", HALF + SLOTS)
-        nc.gpsimd.memset(g_codes[:, 0:HALF], 0)
-        nc.gpsimd.memset(g_scales[:, 0:HALF], 0)
+        g_codes, g_scales = operand("g", PAD + SLOTS)
+        nc.gpsimd.memset(g_codes[:, 0:PAD], 0)
+        nc.gpsimd.memset(g_scales[:, 0:PAD], 0)
+        zeros = sbuf("zeros", [P, P], F32)
+        nc.gpsimd.memset(zeros[:], 0.0)
 
         v_along_d = sbuf("v_along_d", [P, SLOTS, PACK], BF16)
 
         def gather_v(t):
-            nc.vector.tensor_copy(v_along_d[:, :, t], v_pool[t][:].indirect(j_list[:]))
+            nc.vector.tensor_copy(v_along_d[:, :, t], v_pool[t].indirect(j_list[:]))
 
         su_row = sbuf("su_row", [P, SLOTS], F32)
         sv_row = sbuf("sv_row", [P, SLOTS], F32)
@@ -121,7 +125,7 @@ def tile_attend_gsink_v_kernel(tc, uT, vT, su, sv, y, offs, qoffs, out):
 
         for t in four:
             gather_v(t)
-        window = [sbuf("window%d" % t, [P, POOL], F32, over="v_pool%d" % t) for t in range(PACK - 1)]
+        window = [sbuf("window%d" % t, [P, POOL], F32) for t in four]
         for cleared in window:
             nc.gpsimd.memset(cleared[:].bitcast(I32), 0)
 
@@ -129,7 +133,7 @@ def tile_attend_gsink_v_kernel(tc, uT, vT, su, sv, y, offs, qoffs, out):
         nc.vector.quantize_mx(v_codes[:].bitcast(E4M3), v_scales[:], flat(v_along_d))
 
         u_along_d = sbuf("u_along_d", [P, SLOTS, PACK], BF16)
-        u_along_i = sbuf("u_along_i", [P, PACK - 1, P, PACK], BF16, over="factor_planes")
+        u_along_i = sbuf("u_along_i", [P, PACK, P, PACK], BF16, over="factor_planes")
         ud_codes, ud_scales = operand("ud")
 
         def gather_u(t, part=slice(0, SLOTS)):
@@ -165,7 +169,7 @@ def tile_attend_gsink_v_kernel(tc, uT, vT, su, sv, y, offs, qoffs, out):
         gather_plane(1)
         turn_u(1, 1)
         lay_u(1, u_along_i[:, 1])
-        nc.vector.tensor_copy(u_along_d[:, :, 0:2], u_pair[:].rearrange("p t i -> p i t"))
+        nc.scalar.copy(u_along_d[:, :, 0:2], u_pair[:].rearrange("p t i -> p i t"))
         gather_plane(2)
         nc.vector.tensor_copy(u_along_d[:, :, 2], u_plane[2])
         turn_u(2, 2)
@@ -243,11 +247,15 @@ def tile_attend_gsink_v_kernel(tc, uT, vT, su, sv, y, offs, qoffs, out):
         logits(3)
         soft_shift(1)
         exponent(1)
+        u_turned[3] = bank(3, "u_turned3", BF16)
+        for r in four:
+            nc.tensor.transpose(u_turned[3][:, r, :], u_plane[3][:, block(r)], ident_bf[:])
         row_max(2)
         exponent(2)
         invert(0)
         row_max(3)
         exponent(3)
+        lay_u(3, u_along_i[:, 3])
         invert(1)
         normalise(0)
         normalise(1)
@@ -269,7 +277,7 @@ def tile_attend_gsink_v_kernel(tc, uT, vT, su, sv, y, offs, qoffs, out):
             for t in range(width // P):
                 ui[first + t] = (codes[:, block(t)], scales[:, block(t)])
 
-        quantise_ui(0, "e3", [u_along_i[:, 0:2].rearrange("s t p r -> s (t p r)"), u_along_i[:, 2].rearrange("s p r -> s (p r)")])
+        quantise_ui(0, "e3", [u_along_i[:].rearrange("s t p r -> s (t p r)")])
 
         f_turned = [bank(n, "f_turned%d" % n) for n in four]
 
@@ -304,13 +312,14 @@ def tile_attend_gsink_v_kernel(tc, uT, vT, su, sv, y, offs, qoffs, out):
         for r in four:
             nc.tensor.matmul(last_back[:, r, :], neg_y[:, block(r)], ident[:], start=r == 0, stop=False, is_transpose=True)
 
-        def difference(n, into):
-            nc.vector.scalar_tensor_tensor(
-                gap[n][:], flat(f_cols[n]), col_inv[n][:], flat(y_turned[n]), ALU.mult, ALU.subtract
-            )
+        def difference(n, into, parts=(slice(0, SLOTS),)):
             h = bank(into, "back%d" % n)
-            for r in four:
-                nc.tensor.transpose(h[:, r, :], gap[n][:, block(r)], ident[:])
+            for part in parts:
+                nc.vector.scalar_tensor_tensor(
+                    gap[n][:, part], flat(f_cols[n])[:, part], col_inv[n][:], flat(y_turned[n])[:, part], ALU.mult, ALU.subtract
+                )
+                for r in range(part.start // P, part.stop // P):
+                    nc.tensor.transpose(h[:, r, :], gap[n][:, block(r)], ident[:])
             back.append(h)
 
         def difference_in_psum(n):
@@ -328,7 +337,7 @@ def tile_attend_gsink_v_kernel(tc, uT, vT, su, sv, y, offs, qoffs, out):
             )
 
         def quantise_gradient(half):
-            cols = slice(HALF + half.start, HALF + half.stop)
+            cols = slice(PAD + half.start, PAD + half.stop)
             nc.vector.quantize_mx(
                 g_codes[:, cols].bitcast(E5M2), g_scales[:, cols], g_along_i[:, half, :].rearrange("s j r -> s (j r)")
             )
@@ -344,38 +353,40 @@ def tile_attend_gsink_v_kernel(tc, uT, vT, su, sv, y, offs, qoffs, out):
         def place(t, part, sums):
             dv = sbuf("dv_sb%d_%d" % (t, part.start), [P, part.stop - part.start], F32)
             nc.scalar.copy(dv[:], sums)
-            target = window[t % len(window)]
-            nc.vector.tensor_copy(target[:].indirect(j_list[:, part.start // 16 : part.stop // 16]), dv[:])
+            target = window[t]
+            listed = target[:].indirect(j_list[:, part.start // 16 : part.stop // 16])
+            if part.stop - part.start == P:
+                nc.vector.tensor_tensor(listed, dv[:], zeros[:], ALU.add)
+            else:
+                nc.vector.tensor_copy(listed, dv[:])
 
         column_sum(0)
         column_sum_on_vector(1)
         column_sum(2)
         column_sum(3)
-        u_turned[3] = bank(0, "u_turned3", BF16)
-        for r in four:
-            nc.tensor.transpose(u_turned[3][:, r, :], u_plane[3][:, block(r)], ident_bf[:])
         invert_column(0)
         invert_column(1)
-        difference(0, 4)
+        difference(0, 1, halves)
         invert_column(2)
-        difference(1, 5)
+        difference(1, 4)
         invert_column(3)
-        difference(2, 6)
+        difference(2, 5)
         difference_in_psum(3)
-        u_last_along_i = sbuf("u_last_along_i", [P, P, PACK], BF16)
-        lay_u(3, u_last_along_i[:])
         gradient(0)
         gradient(1)
-        quantise_gradient(halves[0])
-        early = product(0, 1, slice(0, SLOTS))
+        quantise_gradient(block(0))
+        early = [product(0, 6, slice(0, SLOTS))]
         gradient(2)
+        quantise_gradient(block(1))
+        early.append(product(1, 2, slice(P, P + SLOTS)))
         gradient(3)
-        quantise_gradient(halves[1])
-        quantise_ui(3, "g_along_i", [flat(u_last_along_i)])
+        quantise_gradient(block(2))
+        quantise_gradient(block(3))
 
-        place(0, halves[0], early[:, halves[1]])
+        place(0, block(0), early[0][:, PAD:])
+        place(1, halves[0], early[1][:, HALF:])
+        left = [slice(P, SLOTS), halves[1], slice(0, SLOTS), slice(0, SLOTS)]
         for t in four:
-            sums = product(t, (t + 2) % PACK, slice(HALF, HALF + SLOTS))
-            part = halves[1] if t == 0 else slice(0, SLOTS)
-            place(t, part, sums[:, part])
-            nc.sync.dma_start(out_rows[:, t, :], window[t % len(window)][:])
+            sums = product(t, (t + 3) % PACK, slice(PAD, PAD + SLOTS))
+            place(t, left[t], sums[:, left[t]])
+            nc.sync.dma_start(out_rows[:, t, :], window[t][:])

@@ -145,8 +145,8 @@ def tile_attend_gsink_v_kernel(tc, uT, vT, su, sv, y, offs, qoffs, out):
         u_plane = [u_pair[:, 0, :], u_pair[:, 1, :]]
         u_plane += [sbuf("u_plane%d" % t, [P, SLOTS], BF16)[:] for t in range(2, PACK)]
 
-        def gather_plane(t):
-            nc.vector.tensor_copy(u_plane[t], u_pool[t][:].indirect(i_list[:]))
+        def gather_plane(t, part=slice(0, SLOTS)):
+            nc.vector.tensor_copy(u_plane[t][:, part], u_pool[t][:].indirect(i_list[:, part.start // 16 : part.stop // 16]))
 
         u_turned = {}
 
@@ -170,8 +170,10 @@ def tile_attend_gsink_v_kernel(tc, uT, vT, su, sv, y, offs, qoffs, out):
         turn_u(1, 1)
         lay_u(1, u_along_i[:, 1])
         nc.scalar.copy(u_along_d[:, :, 0:2], u_pair[:].rearrange("p t i -> p i t"))
-        gather_plane(2)
-        nc.vector.tensor_copy(u_along_d[:, :, 2], u_plane[2])
+        for half in halves:
+            gather_plane(2, half)
+        for half in halves:
+            nc.vector.tensor_copy(u_along_d[:, half, 2], u_plane[2][:, half])
         turn_u(2, 2)
         lay_u(2, u_along_i[:, 2])
 
@@ -235,7 +237,7 @@ def tile_attend_gsink_v_kernel(tc, uT, vT, su, sv, y, offs, qoffs, out):
         )
         score(2)
         score(3)
-        for n in four:
+        for n in (0, 1, 3):
             turn_y(n, 4 + n)
         logits(0)
         soft_bound(0)
@@ -255,12 +257,12 @@ def tile_attend_gsink_v_kernel(tc, uT, vT, su, sv, y, offs, qoffs, out):
         invert(0)
         row_max(3)
         exponent(3)
-        lay_u(3, u_along_i[:, 3])
         invert(1)
         normalise(0)
         normalise(1)
         invert(2)
         normalise(2)
+        lay_u(3, u_along_i[:, 3])
         invert(3)
         normalise(3, block(0))
         normalise(3, slice(P, SLOTS))
@@ -362,20 +364,21 @@ def tile_attend_gsink_v_kernel(tc, uT, vT, su, sv, y, offs, qoffs, out):
 
         column_sum(0)
         column_sum_on_vector(1)
+        turn_y(2, 0)
         column_sum(2)
         column_sum(3)
         invert_column(0)
         invert_column(1)
-        difference(0, 1, halves)
+        difference(0, 6, halves)
         invert_column(2)
-        difference(1, 4)
+        difference(1, 1)
         invert_column(3)
-        difference(2, 5)
+        difference(2, 4)
         difference_in_psum(3)
         gradient(0)
         gradient(1)
         quantise_gradient(block(0))
-        early = [product(0, 6, slice(0, SLOTS))]
+        early = [product(0, 5, slice(0, SLOTS))]
         gradient(2)
         quantise_gradient(block(1))
         early.append(product(1, 2, slice(P, P + SLOTS)))

@@ -133,7 +133,7 @@ def tile_attend_gsink_v_kernel(tc, uT, vT, su, sv, y, offs, qoffs, out):
         nc.vector.quantize_mx(v_codes[:].bitcast(E4M3), v_scales[:], flat(v_along_d))
 
         u_along_d = sbuf("u_along_d", [P, SLOTS, PACK], BF16)
-        u_along_i = sbuf("u_along_i", [P, PACK, P, PACK], BF16, over="factor_planes")
+        u_along_i = sbuf("u_along_i", [P, PACK - 1, P, PACK], BF16, over="factor_planes")
         ud_codes, ud_scales = operand("ud")
 
         def gather_u(t, part=slice(0, SLOTS)):
@@ -262,7 +262,8 @@ def tile_attend_gsink_v_kernel(tc, uT, vT, su, sv, y, offs, qoffs, out):
         normalise(1)
         invert(2)
         normalise(2)
-        lay_u(3, u_along_i[:, 3])
+        u_last_along_i = sbuf("u_last_along_i", [P, P, PACK], BF16, over="neg_shift3")
+        lay_u(3, u_last_along_i[:])
         invert(3)
         normalise(3, block(0))
         normalise(3, slice(P, SLOTS))
@@ -279,9 +280,9 @@ def tile_attend_gsink_v_kernel(tc, uT, vT, su, sv, y, offs, qoffs, out):
             for t in range(width // P):
                 ui[first + t] = (codes[:, block(t)], scales[:, block(t)])
 
-        quantise_ui(0, "e3", [u_along_i[:].rearrange("s t p r -> s (t p r)")])
+        quantise_ui(0, "e3", [u_along_i[:, 0:2].rearrange("s t p r -> s (t p r)"), u_along_i[:, 2].rearrange("s p r -> s (p r)"), flat(u_last_along_i)])
 
-        f_turned = [bank(n, "f_turned%d" % n) for n in four]
+        f_turned = [bank(n, "f_turned%d" % n) for n in range(PACK - 1)]
 
         def turn_f(n, q):
             nc.tensor.transpose(f_turned[n][:, q, :], f[q][:, block(n)], ident[:])
@@ -307,10 +308,11 @@ def tile_attend_gsink_v_kernel(tc, uT, vT, su, sv, y, offs, qoffs, out):
 
         neg_y = sbuf("neg_y", [P, SLOTS], F32, over="z3")
         nc.scalar.activation(neg_y[:], flat(y_turned[3]), ACT.Copy, scale=-1.0)
+        f_turned.append(bank(7, "f_turned3"))
         for q in four:
             for n in four:
                 turn_f(n, q)
-        last_back = bank(7, "back3")
+        last_back = bank(3, "back3")
         for r in four:
             nc.tensor.matmul(last_back[:, r, :], neg_y[:, block(r)], ident[:], start=r == 0, stop=False, is_transpose=True)
 

@@ -69,7 +69,7 @@ def tile_attend_gsink_v_kernel(tc, uT, vT, su, sv, y, offs, qoffs, out):
         nc.scalar.dma_start(su_pool[P - 1 : P, :], su[0:1, :])
         for h in range(2):
             nc.sync.dma_start(v_pair[h][:], v_rows[:, 2 * h : 2 * h + 2, :])
-        for t in four:
+        for t in (2, 0, 1, 3):
             nc.sync.dma_start(u_pool[t][:], u_rows[:, t, :])
         y_sb = sbuf("y_sb", [P, PACK, SLOTS], F32)
         nc.sync.dma_start(y_sb[:], y.rearrange("(p r) j -> p r j", r=PACK))
@@ -163,19 +163,18 @@ def tile_attend_gsink_v_kernel(tc, uT, vT, su, sv, y, offs, qoffs, out):
                 ud_codes[:, half].bitcast(E4M3), ud_scales[:, half], u_along_d[:, half, :].rearrange("p n t -> p (n t)")
             )
 
+        gather_plane(2)
+        nc.vector.tensor_copy(u_along_d[:, :, 2], u_plane[2])
+        turn_u(2, 2)
+        lay_u(2, u_along_i[:, 2])
         gather_plane(0)
         turn_u(0, 0)
         lay_u(0, u_along_i[:, 0])
-        gather_plane(1)
+        for half in halves:
+            gather_plane(1, half)
+            nc.scalar.copy(u_along_d[:, half, 0:2], u_pair[:, :, half].rearrange("p t i -> p i t"))
         turn_u(1, 1)
         lay_u(1, u_along_i[:, 1])
-        nc.scalar.copy(u_along_d[:, :, 0:2], u_pair[:].rearrange("p t i -> p i t"))
-        for half in halves:
-            gather_plane(2, half)
-        for half in halves:
-            nc.vector.tensor_copy(u_along_d[:, half, 2], u_plane[2][:, half])
-        turn_u(2, 2)
-        lay_u(2, u_along_i[:, 2])
 
         scores = []
 

@@ -61,14 +61,15 @@ def tile_attend_gsink_v_kernel(tc, uT, vT, su, sv, y, offs, qoffs, out):
         v_rows = vT.rearrange("(p t) c -> p t c", t=PACK)
         out_rows = out.rearrange("(p t) c -> p t c", t=PACK)
         u_pool = [sbuf("u_pool%d" % t, [P, POOL], F32) for t in four]
-        v_pair = [sbuf("v_pair%d" % h, [P, 2, POOL], F32) for h in range(2)]
-        v_pool = [v_pair[t // 2][:, t % 2, :] for t in four]
+        v_pair = sbuf("v_pair", [P, 2, POOL], F32)
+        v_pool = [v_pair[:, t, :] for t in range(2)] + [sbuf("v_pool%d" % t, [P, POOL], F32)[:] for t in range(2, PACK)]
         nc.sync.dma_start(j_list[:], qoffs)
         nc.sync.dma_start(i_list[:], offs)
         nc.scalar.dma_start(sv_pool[P - 1 : P, :], sv[0:1, :])
         nc.scalar.dma_start(su_pool[P - 1 : P, :], su[0:1, :])
-        for h in range(2):
-            nc.sync.dma_start(v_pair[h][:], v_rows[:, 2 * h : 2 * h + 2, :])
+        nc.sync.dma_start(v_pair[:], v_rows[:, 0:2, :])
+        for t in range(2, PACK):
+            nc.sync.dma_start(v_pool[t], v_rows[:, t, :])
         for t in (2, 0, 1, 3):
             nc.sync.dma_start(u_pool[t][:], u_rows[:, t, :])
         y_sb = sbuf("y_sb", [P, PACK, SLOTS], F32)
@@ -260,10 +261,11 @@ def tile_attend_gsink_v_kernel(tc, uT, vT, su, sv, y, offs, qoffs, out):
         normalise(0)
         normalise(1)
         invert(2)
-        normalise(2)
+        normalise(2, halves[0])
         u_last_along_i = sbuf("u_last_along_i", [P, P, PACK], BF16, over="neg_shift3")
         lay_u(3, u_last_along_i[:])
         invert(3)
+        normalise(2, halves[1])
         normalise(3, block(0))
         normalise(3, slice(P, SLOTS))
         ui = {}

@@ -70,15 +70,13 @@ def tile_attend_gsink_v_kernel(tc, uT, vT, su, sv, y, offs, qoffs, out):
         nc.sync.dma_start(v_pair[:], v_rows[:, 0:2, :])
         for t in range(2, PACK):
             nc.sync.dma_start(v_pool[t], v_rows[:, t, :])
-        for t in (2, 0, 1, 3):
+        for t in four:
             nc.sync.dma_start(u_pool[t][:], u_rows[:, t, :])
         y_sb = sbuf("y_sb", [P, PACK, SLOTS], F32)
         nc.sync.dma_start(y_sb[:], y.rearrange("(p r) j -> p r j", r=PACK))
 
         ident = sbuf("ident", [P, P], F32)
-        ident_bf = sbuf("ident_bf", [P, P], BF16)
         make_identity(nc, ident[:])
-        make_identity(nc, ident_bf[:])
 
         def operand(name, width=SLOTS, over=None):
             return sbuf(name + "_codes", [P, width], U32, over), sbuf(name + "_scales", [P, width], U8)
@@ -133,49 +131,48 @@ def tile_attend_gsink_v_kernel(tc, uT, vT, su, sv, y, offs, qoffs, out):
         v_codes, v_scales = operand("v")
         nc.vector.quantize_mx(v_codes[:].bitcast(E4M3), v_scales[:], flat(v_along_d))
 
-        u_along_d = sbuf("u_along_d", [P, SLOTS, PACK], BF16)
+        u_along_d = [sbuf("u_along_d%d" % q, [P, P, PACK], BF16) for q in four]
         u_along_i = sbuf("u_along_i", [P, PACK - 1, P, PACK], BF16, over="factor_planes")
         ud_codes, ud_scales = operand("ud")
 
-        def gather_u(t, part=slice(0, SLOTS)):
-            nc.vector.tensor_copy(
-                u_along_d[:, part, t], u_pool[t][:].indirect(i_list[:, part.start // 16 : part.stop // 16])
-            )
-
-        u_pair = sbuf("u_pair", [P, 2, SLOTS], BF16)
-        u_plane = [u_pair[:, 0, :], u_pair[:, 1, :]]
-        u_plane += [sbuf("u_plane%d" % t, [P, SLOTS], BF16)[:] for t in range(2, PACK)]
+        u_pair = [sbuf("u_pair%d" % h, [P, 2, SLOTS], BF16) for h in range(2)]
+        u_plane = [u_pair[t // 2][:, t % 2, :] for t in four]
 
         def gather_plane(t, part=slice(0, SLOTS)):
             nc.vector.tensor_copy(u_plane[t][:, part], u_pool[t][:].indirect(i_list[:, part.start // 16 : part.stop // 16]))
 
+        def weave(h, q):
+            nc.scalar.copy(u_along_d[q][:, :, 2 * h : 2 * h + 2], u_pair[h][:, :, block(q)].rearrange("p t i -> p i t"))
+
         u_turned = {}
 
         def turn_u(t, n):
-            u_turned[t] = bank(n, "u_turned%d" % t, BF16)
-            for r in four:
-                nc.tensor.transpose(u_turned[t][:, r, :], u_plane[t][:, r::PACK], ident_bf[:])
+            u_turned[t] = ps.tile([P, 2, P], F32, name="u_turned%d" % t, tag="bank%d" % n)
+            words = u_plane[t].bitcast(F32)
+            for w in range(2):
+                nc.tensor.transpose(u_turned[t][:, w, :], words[:, w::2], ident[:])
 
         def lay_u(t, into):
-            nc.scalar.copy(into, u_turned[t][:].rearrange("s r p -> s p r"))
+            words = into.rearrange("s p r -> s (p r)").bitcast(F32).rearrange("s (p w) -> s p w", w=2)
+            nc.scalar.copy(words, u_turned[t][:].rearrange("s w p -> s p w"))
 
-        def quantise_ud(half):
-            nc.vector.quantize_mx(
-                ud_codes[:, half].bitcast(E4M3), ud_scales[:, half], u_along_d[:, half, :].rearrange("p n t -> p (n t)")
-            )
+        def quantise_ud(q):
+            nc.vector.quantize_mx(ud_codes[:, block(q)].bitcast(E4M3), ud_scales[:, block(q)], flat(u_along_d[q]))
 
-        gather_plane(2)
-        nc.vector.tensor_copy(u_along_d[:, :, 2], u_plane[2])
-        turn_u(2, 2)
-        lay_u(2, u_along_i[:, 2])
-        gather_plane(0)
-        turn_u(0, 0)
-        lay_u(0, u_along_i[:, 0])
-        for half in halves:
-            gather_plane(1, half)
-            nc.scalar.copy(u_along_d[:, half, 0:2], u_pair[:, :, half].rearrange("p t i -> p i t"))
-        turn_u(1, 1)
-        lay_u(1, u_along_i[:, 1])
+        ui = {}
+
+        def quantise_ui(t, over, source):
+            codes, scales = operand("ui%d" % t, P, over)
+            nc.vector.quantize_mx(codes[:].bitcast(E4M3), scales[:], source)
+            ui[t] = (codes[:], scales[:])
+
+        for t in range(PACK - 1):
+            gather_plane(t)
+            if t == 1:
+                for q in four:
+                    weave(0, q)
+            turn_u(t, t)
+            lay_u(t, u_along_i[:, t])
 
         scores = []
 
@@ -226,17 +223,14 @@ def tile_attend_gsink_v_kernel(tc, uT, vT, su, sv, y, offs, qoffs, out):
             for r in four:
                 nc.tensor.transpose(y_turned[n][:, r, :], y_sb[:, r, block(n)], ident[:])
 
-        gather_u(3, halves[0])
-        quantise_ud(halves[0])
-        score(0)
-        score(1)
-        gather_u(3, halves[1])
-        quantise_ud(halves[1])
-        nc.scalar.copy(
-            u_plane[3].rearrange("p (r s) -> p r s", r=PACK), u_along_d[:, :, 3].rearrange("p (s r) -> p r s", r=PACK)
-        )
-        score(2)
-        score(3)
+        for q in four:
+            gather_plane(3, block(q))
+            weave(1, q)
+        for q in four:
+            quantise_ud(q)
+            score(q)
+            if q < PACK - 1:
+                quantise_ui(q, "u_along_d%d" % q, u_along_i[:, q].rearrange("s p r -> s (p r)"))
         for n in (0, 1, 3):
             turn_y(n, 4 + n)
         logits(0)
@@ -249,9 +243,7 @@ def tile_attend_gsink_v_kernel(tc, uT, vT, su, sv, y, offs, qoffs, out):
         logits(3)
         soft_shift(1)
         exponent(1)
-        u_turned[3] = bank(3, "u_turned3", BF16)
-        for r in four:
-            nc.tensor.transpose(u_turned[3][:, r, :], u_plane[3][:, block(r)], ident_bf[:])
+        turn_u(3, 3)
         row_max(2)
         exponent(2)
         invert(0)
@@ -268,20 +260,7 @@ def tile_attend_gsink_v_kernel(tc, uT, vT, su, sv, y, offs, qoffs, out):
         normalise(2, halves[1])
         normalise(3, block(0))
         normalise(3, slice(P, SLOTS))
-        ui = {}
-
-        def quantise_ui(first, over, sources):
-            width = sum(source.shape[1] for source in sources) // PACK
-            codes, scales = operand("ui%d" % first, width, over)
-            at = 0
-            for source in sources:
-                cols = slice(at, at + source.shape[1] // PACK)
-                nc.vector.quantize_mx(codes[:, cols].bitcast(E4M3), scales[:, cols], source)
-                at = cols.stop
-            for t in range(width // P):
-                ui[first + t] = (codes[:, block(t)], scales[:, block(t)])
-
-        quantise_ui(0, "e3", [u_along_i[:, 0:2].rearrange("s t p r -> s (t p r)"), u_along_i[:, 2].rearrange("s p r -> s (p r)"), flat(u_last_along_i)])
+        quantise_ui(3, "e3", flat(u_last_along_i))
 
         f_turned = [bank(n, "f_turned%d" % n) for n in range(PACK - 1)]
 

@@ -24,6 +24,8 @@ PAD = SLOTS - P
 POOL = 2048
 FEATURES = 512
 SOFTEN = 8.0
+SOFT_TILES = 3
+LARGE = 2.0**100
 
 FLOPS = 2 * 2 * SLOTS * SLOTS * FEATURES
 BYTES = 4 * (3 * FEATURES * POOL + SLOTS * SLOTS + 2 * POOL) + 2 * 2 * P * (SLOTS // 16)
@@ -111,17 +113,15 @@ def tile_attend_gsink_v_kernel(tc, uT, vT, su, sv, y, offs, qoffs, out):
         nc.scalar.copy(su_col[:], su_turned[:, :, P - 1])
         nc.scalar.copy(su_dealt[:], su_dealt_turned[:, :, P - 1])
         nc.scalar.copy(sv_col[:], sv_turned[:, :, P - 1])
+        sv_inv = sbuf("sv_inv", [P, PACK], F32)
+        sv_inv_col = sbuf("sv_inv_col", [P, PACK], F32)
+        nc.vector.reciprocal(sv_inv[:], sv_col[:])
+        nc.vector.tensor_scalar(sv_inv_col[:], sv_inv[:], LARGE, -LARGE, ALU.min, ALU.max)
         sv_spread = bank(7, "sv_spread")
         for n in four:
             nc.tensor.transpose(sv_spread[:, n, :], sv_col[:, n : n + 1].to_broadcast([P, P]), ident[:])
         sv_all = sbuf("sv_all", [P, SLOTS], F32)
         nc.scalar.copy(sv_all[:], flat(sv_spread))
-        factor_planes = sbuf("factor_planes", [P, PACK, SLOTS], F32)
-        for r in four:
-            nc.scalar.activation(factor_planes[:, r, :], sv_all[:], ACT.Copy, scale=su_dealt[:, r : r + 1])
-        factor = sbuf("factor", [P, SLOTS, PACK], F32)
-        nc.scalar.copy(factor[:], factor_planes[:].rearrange("s r j -> s j r"))
-
         for t in four:
             gather_v(t)
         window = [sbuf("window%d" % t, [P, POOL], F32) for t in four]
@@ -132,9 +132,7 @@ def tile_attend_gsink_v_kernel(tc, uT, vT, su, sv, y, offs, qoffs, out):
         nc.vector.quantize_mx(v_codes[:].bitcast(E4M3), v_scales[:], flat(v_along_d))
 
         u_along_d = [sbuf("u_along_d%d" % q, [P, P, PACK], BF16) for q in four]
-        u_along_i = sbuf("u_along_i", [P, PACK - 1, P, PACK], BF16, over="factor_planes")
         ud_codes, ud_scales = operand("ud")
-
         u_pair = [sbuf("u_pair%d" % h, [P, 2, SLOTS], BF16) for h in range(2)]
         u_plane = [u_pair[t // 2][:, t % 2, :] for t in four]
 
@@ -144,26 +142,28 @@ def tile_attend_gsink_v_kernel(tc, uT, vT, su, sv, y, offs, qoffs, out):
         def weave(h, q):
             nc.scalar.copy(u_along_d[q][:, :, 2 * h : 2 * h + 2], u_pair[h][:, :, block(q)].rearrange("p t i -> p i t"))
 
-        u_turned = {}
-
-        def turn_u(t, n):
-            u_turned[t] = ps.tile([P, 2, P], F32, name="u_turned%d" % t, tag="bank%d" % n)
-            words = u_plane[t].bitcast(F32)
+        def turn_words(name, rows, n):
+            turned = ps.tile([P, 2, P], F32, name=name + "_turned", tag="bank%d" % n)
+            words = rows.bitcast(F32)
             for w in range(2):
-                nc.tensor.transpose(u_turned[t][:, w, :], words[:, w::2], ident[:])
+                nc.tensor.transpose(turned[:, w, :], words[:, w::2], ident[:])
+            return turned
 
-        def lay_u(t, into):
-            words = into.rearrange("s p r -> s (p r)").bitcast(F32).rearrange("s (p w) -> s p w", w=2)
-            nc.scalar.copy(words, u_turned[t][:].rearrange("s w p -> s p w"))
+        def lay_words(name, turned, over=None):
+            along_i = sbuf(name + "_along_i", [P, P, PACK], BF16, over)
+            words = flat(along_i).bitcast(F32).rearrange("s (x w) -> s x w", w=2)
+            nc.scalar.copy(words, turned[:].rearrange("s w x -> s x w"))
+            return along_i
 
         def quantise_ud(q):
             nc.vector.quantize_mx(ud_codes[:, block(q)].bitcast(E4M3), ud_scales[:, block(q)], flat(u_along_d[q]))
 
+        u_along_i = {}
         ui = {}
 
-        def quantise_ui(t, over, source):
+        def quantise_ui(t, over):
             codes, scales = operand("ui%d" % t, P, over)
-            nc.vector.quantize_mx(codes[:].bitcast(E4M3), scales[:], source)
+            nc.vector.quantize_mx(codes[:].bitcast(E4M3), scales[:], flat(u_along_i[t]))
             ui[t] = (codes[:], scales[:])
 
         for t in range(PACK - 1):
@@ -171,8 +171,9 @@ def tile_attend_gsink_v_kernel(tc, uT, vT, su, sv, y, offs, qoffs, out):
             if t == 1:
                 for q in four:
                     weave(0, q)
-            turn_u(t, t)
-            lay_u(t, u_along_i[:, t])
+            u_along_i[t] = lay_words("u%d" % t, turn_words("u%d" % t, u_plane[t], t))
+            if t > 0:
+                quantise_ui(t - 1, "u_pool%d" % t)
 
         scores = []
 
@@ -187,7 +188,8 @@ def tile_attend_gsink_v_kernel(tc, uT, vT, su, sv, y, offs, qoffs, out):
         z = [sbuf("z%d" % q, [P, SLOTS], F32) for q in four]
         e = [sbuf("e%d" % q, [P, SLOTS], F32) for q in four]
         f = [sbuf("f%d" % q, [P, SLOTS], F32) for q in four]
-        soft_sum = [sbuf("soft_sum%d" % q, [P, 1], F32) for q in range(2)]
+        x = [[sbuf("x%d_%d" % (q, h), [P, HALF], F32) for h in range(2)] for q in four]
+        soft_sum = [sbuf("soft_sum%d" % q, [P, 1], F32) for q in range(SOFT_TILES)]
         neg_shift = [sbuf("neg_shift%d" % q, [P, 1], F32) for q in four]
         row_sum = [sbuf("row_sum%d" % q, [P, 1], F32) for q in four]
         row_inv = [sbuf("row_inv%d" % q, [P, 1], F32) for q in four]
@@ -216,12 +218,8 @@ def tile_attend_gsink_v_kernel(tc, uT, vT, su, sv, y, offs, qoffs, out):
         def normalise(q, cols=slice(0, SLOTS)):
             nc.vector.tensor_scalar(f[q][:, cols], e[q][:, cols], row_inv[q][:], None, ALU.mult)
 
-        y_turned = {}
-
-        def turn_y(n, into):
-            y_turned[n] = bank(into, "y_turned%d" % n)
-            for r in four:
-                nc.tensor.transpose(y_turned[n][:, r, :], y_sb[:, r, block(n)], ident[:])
+        def weigh(engine, q, cols):
+            engine.tensor_scalar(x[q][cols.start // HALF][:], e[q][:, cols], row_inv[q][:], su_col[:, q : q + 1], ALU.mult, ALU.mult)
 
         for q in four:
             gather_plane(3, block(q))
@@ -229,102 +227,93 @@ def tile_attend_gsink_v_kernel(tc, uT, vT, su, sv, y, offs, qoffs, out):
         for q in four:
             quantise_ud(q)
             score(q)
-            if q < PACK - 1:
-                quantise_ui(q, "u_along_d%d" % q, u_along_i[:, q].rearrange("s p r -> s (p r)"))
-        for n in (0, 1, 3):
-            turn_y(n, 4 + n)
-        logits(0)
-        soft_bound(0)
-        logits(1)
-        soft_bound(1)
-        logits(2)
-        soft_shift(0)
-        exponent(0)
-        logits(3)
-        soft_shift(1)
-        exponent(1)
-        turn_u(3, 3)
-        row_max(2)
-        exponent(2)
-        invert(0)
-        row_max(3)
-        exponent(3)
-        invert(1)
-        normalise(0)
-        normalise(1)
-        invert(2)
-        normalise(2, halves[0])
-        u_last_along_i = sbuf("u_last_along_i", [P, P, PACK], BF16, over="neg_shift3")
-        lay_u(3, u_last_along_i[:])
+        for q in range(SOFT_TILES):
+            logits(q)
+            soft_bound(q)
+        for q in range(SOFT_TILES):
+            soft_shift(q)
+        for q in range(SOFT_TILES, PACK):
+            logits(q)
+            row_max(q)
+        for q in four:
+            exponent(q)
+        u_last_turned = turn_words("u3", u_plane[3], 0)
+
+        column_banks = (4, 5, 6, 3)
+        y_su = [sbuf("y_su%d" % r, [P, SLOTS], F32) for r in four]
+        y_turned = [bank(column_banks[n], "y_turned%d" % n) for n in four]
+        for r in four:
+            nc.gpsimd.tensor_scalar(y_su[r][:], y_sb[:, r, :], su_dealt[:, r : r + 1], 0.0, ALU.mult, ALU.add)
+            for n in four:
+                nc.tensor.transpose(y_turned[n][:, r, :], y_su[r][:, block(n)], ident[:])
+
+        groups = ((0,), (1,), (2, 3))
+        sums = [ps.tile([P, len(groups[h]), P], F32, name="sums%d" % h, tag="bank%d" % (7, 2, 1)[h]) for h in range(3)]
+
+        def add_columns(q, h):
+            for k, n in enumerate(groups[h]):
+                nc.tensor.matmul(
+                    sums[h][:, k, :], f[q][:, block(n)], ident[:],
+                    start=q == 0 and k == 0, stop=q == PACK - 1 and n == groups[h][-1], is_transpose=True,
+                )
+
+        for q in range(PACK - 1):
+            invert(q)
+            normalise(q)
+            for h in range(3):
+                add_columns(q, h)
         invert(3)
-        normalise(2, halves[1])
-        normalise(3, block(0))
-        normalise(3, slice(P, SLOTS))
-        quantise_ui(3, "e3", flat(u_last_along_i))
+        for n in range(2):
+            normalise(3, block(n))
+            add_columns(3, n)
+        for q in four:
+            weigh(nc.vector, q, halves[0])
+        u_along_i[3] = lay_words("u3", u_last_turned, "neg_shift3")
+        y_terms = sbuf("y_terms", [P, PACK, P, PACK], F32, "z3")
+        y_term = []
+        for n in four:
+            w = y_terms[:, n]
+            nc.scalar.activation(w, y_turned[n][:].rearrange("j r s -> j s r"), ACT.Copy, scale=sv_col[:, n : n + 1])
+            y_term.append(w)
 
-        f_turned = [bank(n, "f_turned%d" % n) for n in range(PACK - 1)]
+        x_turned = []
 
-        def turn_f(n, q):
-            nc.tensor.transpose(f_turned[n][:, q, :], f[q][:, block(n)], ident[:])
+        def turn_x(n):
+            t = bank(column_banks[n], "x_turned%d" % n)
+            for q in four:
+                nc.tensor.transpose(t[:, q, :], x[q][n // 2][:, block(n % 2)], ident[:])
+            x_turned.append(t)
 
         col_sum = [sbuf("col_sum%d" % n, [P, 1], F32) for n in four]
-        col_inv = [sbuf("col_inv%d" % n, [P, 1], F32) for n in four]
-        f_cols = [sbuf("f_cols%d" % n, [P, PACK, P], F32) for n in four]
-        gap = [sbuf("gap%d" % n, [P, SLOTS], F32) for n in four]
-        g_along_i = sbuf("g_along_i", [P, SLOTS, PACK], BF16)
-        back = []
-
-        def dealt(n):
-            return flat(f_turned[n]).rearrange("j (s r) -> j r s", r=PACK)
+        col_scale = [sbuf("col_scale%d" % n, [P, 1], F32) for n in four]
+        spent = [sbuf("spent%d" % n, [P, P], F32) for n in four]
 
         def column_sum(n):
-            nc.scalar.activation(f_cols[n][:], dealt(n), ACT.Copy, accum_out=col_sum[n][:])
-
-        def column_sum_on_vector(n):
-            nc.vector.tensor_scalar(f_cols[n][:], dealt(n), 1.0, None, ALU.mult, ALU.add, accum_out=col_sum[n][:])
-
-        def invert_column(n):
-            nc.vector.reciprocal(col_inv[n][:], col_sum[n][:])
-
-        neg_y = sbuf("neg_y", [P, SLOTS], F32, over="z3")
-        nc.scalar.activation(neg_y[:], flat(y_turned[3]), ACT.Copy, scale=-1.0)
-        f_turned.append(bank(7, "f_turned3"))
-        for q in four:
-            for n in four:
-                turn_f(n, q)
-        last_back = bank(3, "back3")
-        for r in four:
-            nc.tensor.matmul(last_back[:, r, :], neg_y[:, block(r)], ident[:], start=r == 0, stop=False, is_transpose=True)
-
-        def difference(n, into, parts=(slice(0, SLOTS),)):
-            h = bank(into, "back%d" % n)
-            for part in parts:
-                nc.vector.scalar_tensor_tensor(
-                    gap[n][:, part], flat(f_cols[n])[:, part], col_inv[n][:], flat(y_turned[n])[:, part], ALU.mult, ALU.subtract
+            if n < 2:
+                nc.vector.tensor_scalar(
+                    spent[n][:], sums[n][:, 0, :], sv_inv_col[:, n : n + 1], None, ALU.mult, ALU.add, accum_out=col_sum[n][:]
                 )
-                for r in range(part.start // P, part.stop // P):
-                    nc.tensor.transpose(h[:, r, :], gap[n][:, block(r)], ident[:])
-            back.append(h)
-
-        def difference_in_psum(n):
-            scaled = sbuf("scaled%d" % n, [P, SLOTS], F32)
-            nc.scalar.activation(scaled[:], flat(f_cols[n]), ACT.Copy, scale=col_inv[n][:])
-            for r in four:
-                nc.tensor.matmul(
-                    last_back[:, r, :], scaled[:, block(r)], ident[:], start=False, stop=r == PACK - 1, is_transpose=True
+            else:
+                nc.scalar.activation(
+                    spent[n][:], sums[2][:, n - 2, :], ACT.Copy, scale=sv_inv_col[:, n : n + 1], accum_out=col_sum[n][:]
                 )
-            back.append(last_back)
 
-        def gradient(n):
-            nc.vector.tensor_tensor(
-                g_along_i[:, block(n), :], back[n][:].rearrange("s r j -> s j r"), factor[:, block(n), :], ALU.mult
-            )
+        def column_scale(n):
+            nc.vector.reciprocal(col_scale[n][:], col_sum[n][:])
 
-        def quantise_gradient(half):
-            cols = slice(PAD + half.start, PAD + half.stop)
-            nc.vector.quantize_mx(
-                g_codes[:, cols].bitcast(E5M2), g_scales[:, cols], g_along_i[:, half, :].rearrange("s j r -> s (j r)")
-            )
+        g_along_i = {}
+        g_rows = {}
+
+        def gradient(n, into):
+            g = sbuf("g%d" % n, [P, SLOTS], BF16)
+            g_rows[n] = g
+            scale = col_scale[n][:]
+            nc.vector.scalar_tensor_tensor(g[:], flat(x_turned[n]), scale, y_term[n].rearrange("j s r -> j (s r)"), ALU.mult, ALU.subtract)
+            g_along_i[n] = lay_words("g%d" % n, turn_words("g%d" % n, g[:], into))
+
+        def quantise_gradient(n):
+            cols = slice(PAD + n * P, PAD + (n + 1) * P)
+            nc.vector.quantize_mx(g_codes[:, cols].bitcast(E5M2), g_scales[:, cols], flat(g_along_i[n]))
 
         def product(t, n, cols):
             acc = bank(n, "dv%d_%d" % (t, cols.start))
@@ -344,34 +333,39 @@ def tile_attend_gsink_v_kernel(tc, uT, vT, su, sv, y, offs, qoffs, out):
             else:
                 nc.vector.tensor_copy(listed, dv[:])
 
+        turn_x(0)
         column_sum(0)
-        column_sum_on_vector(1)
-        turn_y(2, 0)
+        column_sum(1)
+        column_scale(0)
+        column_scale(1)
+        turn_x(1)
+        gradient(0, 0)
+        normalise(3, halves[1])
+        add_columns(3, 2)
+        for q in four:
+            weigh(nc.vector, q, halves[1])
+        turn_x(2)
+        gradient(1, 7)
+        turn_x(3)
         column_sum(2)
         column_sum(3)
-        invert_column(0)
-        invert_column(1)
-        difference(0, 6, halves)
-        invert_column(2)
-        difference(1, 1)
-        invert_column(3)
-        difference(2, 4)
-        difference_in_psum(3)
-        gradient(0)
-        gradient(1)
-        quantise_gradient(block(0))
-        early = [product(0, 5, slice(0, SLOTS))]
-        gradient(2)
-        quantise_gradient(block(1))
-        early.append(product(1, 2, slice(P, P + SLOTS)))
-        gradient(3)
-        quantise_gradient(block(2))
-        quantise_gradient(block(3))
+        column_scale(2)
+        column_scale(3)
+        quantise_gradient(0)
+        early = [product(0, 2, slice(0, SLOTS))]
+        gradient(2, 4)
+        quantise_gradient(1)
+        gradient(3, 5)
+        early.append(product(1, 3, slice(P, P + SLOTS)))
+        quantise_gradient(2)
+        quantise_gradient(3)
+        quantise_ui(2, "e3")
+        quantise_ui(3, None)
 
         place(0, block(0), early[0][:, PAD:])
         place(1, halves[0], early[1][:, HALF:])
         left = [slice(P, SLOTS), halves[1], slice(0, SLOTS), slice(0, SLOTS)]
         for t in four:
-            sums = product(t, (t + 3) % PACK, slice(PAD, PAD + SLOTS))
-            place(t, left[t], sums[:, left[t]])
+            whole = product(t, (0, 6, 7, 1)[t], slice(PAD, PAD + SLOTS))
+            place(t, left[t], whole[:, left[t]])
             nc.sync.dma_start(out_rows[:, t, :], window[t][:])

@@ -63,15 +63,13 @@ def tile_attend_gsink_v_kernel(tc, uT, vT, su, sv, y, offs, qoffs, out):
         v_rows = vT.rearrange("(p t) c -> p t c", t=PACK)
         out_rows = out.rearrange("(p t) c -> p t c", t=PACK)
         u_pool = [sbuf("u_pool%d" % t, [P, POOL], F32) for t in four]
-        v_pair = sbuf("v_pair", [P, 2, POOL], F32)
-        v_pool = [v_pair[:, t, :] for t in range(2)] + [sbuf("v_pool%d" % t, [P, POOL], F32)[:] for t in range(2, PACK)]
+        v_pool = [sbuf("v_pool%d" % h, [P, 2, POOL], F32) for h in range(2)]
         nc.sync.dma_start(j_list[:], qoffs)
         nc.sync.dma_start(i_list[:], offs)
         nc.scalar.dma_start(sv_pool[P - 1 : P, :], sv[0:1, :])
         nc.scalar.dma_start(su_pool[P - 1 : P, :], su[0:1, :])
-        nc.sync.dma_start(v_pair[:], v_rows[:, 0:2, :])
-        for t in range(2, PACK):
-            nc.sync.dma_start(v_pool[t], v_rows[:, t, :])
+        for h in range(2):
+            nc.sync.dma_start(v_pool[h][:], v_rows[:, 2 * h : 2 * h + 2, :])
         for t in four:
             nc.sync.dma_start(u_pool[t][:], u_rows[:, t, :])
         y_sb = sbuf("y_sb", [P, PACK, SLOTS], F32)
@@ -91,8 +89,10 @@ def tile_attend_gsink_v_kernel(tc, uT, vT, su, sv, y, offs, qoffs, out):
 
         v_along_d = sbuf("v_along_d", [P, SLOTS, PACK], BF16)
 
+        v_pairs = sbuf("v_pairs", [P, 2, SLOTS, 2], BF16)
+
         def gather_v(t):
-            nc.vector.tensor_copy(v_along_d[:, :, t], v_pool[t].indirect(j_list[:]))
+            nc.vector.tensor_copy(v_pairs[:, t // 2, :, t % 2], v_pool[t // 2][:, t % 2, :].indirect(j_list[:]))
 
         su_row = sbuf("su_row", [P, SLOTS], F32)
         sv_row = sbuf("sv_row", [P, SLOTS], F32)
@@ -124,12 +124,14 @@ def tile_attend_gsink_v_kernel(tc, uT, vT, su, sv, y, offs, qoffs, out):
         nc.scalar.copy(sv_all[:], flat(sv_spread))
         for t in four:
             gather_v(t)
+        nc.scalar.copy(
+            flat(v_along_d).bitcast(U32).rearrange("p (j h) -> p j h", h=2),
+            v_pairs[:].rearrange("p h j e -> p (h j e)").bitcast(U32).rearrange("p (h j) -> p j h", h=2),
+        )
         window = [sbuf("window%d" % t, [P, POOL], F32) for t in four]
         for cleared in window:
             nc.gpsimd.memset(cleared[:].bitcast(I32), 0)
 
-        v_codes, v_scales = operand("v")
-        nc.vector.quantize_mx(v_codes[:].bitcast(E4M3), v_scales[:], flat(v_along_d))
 
         u_along_d = [sbuf("u_along_d%d" % q, [P, P, PACK], BF16) for q in four]
         ud_codes, ud_scales = operand("ud")
@@ -175,6 +177,9 @@ def tile_attend_gsink_v_kernel(tc, uT, vT, su, sv, y, offs, qoffs, out):
             if t > 0:
                 quantise_ui(t - 1, "u_pool%d" % t)
 
+        v_codes, v_scales = operand("v", SLOTS, "u_pool0")
+        nc.vector.quantize_mx(v_codes[:].bitcast(E4M3), v_scales[:], flat(v_along_d))
+
         scores = []
 
         def score(q):
@@ -202,8 +207,10 @@ def tile_attend_gsink_v_kernel(tc, uT, vT, su, sv, y, offs, qoffs, out):
 
         def soft_shift(q):
             per_bit = SOFTEN * math.log(2.0)
+            slope = sbuf("slope%d" % q, [P, 1], F32)
             nc.vector.tensor_scalar(
-                neg_shift[q][:], soft_sum[q][:].bitcast(I32), -per_bit / 2.0**23, per_bit * (127 + 9), ALU.mult, ALU.add
+                slope[:], soft_sum[q][:].bitcast(I32), -per_bit / 2.0**23, per_bit * (127 + 9), ALU.mult, ALU.add,
+                accum_out=neg_shift[q][:],
             )
 
         def row_max(q):
@@ -240,10 +247,11 @@ def tile_attend_gsink_v_kernel(tc, uT, vT, su, sv, y, offs, qoffs, out):
         u_last_turned = turn_words("u3", u_plane[3], 0)
 
         column_banks = (4, 5, 6, 3)
-        y_su = [sbuf("y_su%d" % r, [P, SLOTS], F32) for r in four]
+        y_scaled = sbuf("y_scaled", [P, PACK, SLOTS], F32, "u_along_d3")
+        y_su = [y_scaled[:, r, :] for r in four]
         y_turned = [bank(column_banks[n], "y_turned%d" % n) for n in four]
         for r in four:
-            nc.gpsimd.tensor_scalar(y_su[r][:], y_sb[:, r, :], su_dealt[:, r : r + 1], 0.0, ALU.mult, ALU.add)
+            nc.gpsimd.tensor_scalar(y_su[r], y_sb[:, r, :], su_dealt[:, r : r + 1], 0.0, ALU.mult, ALU.add)
             for n in four:
                 nc.tensor.transpose(y_turned[n][:, r, :], y_su[r][:, block(n)], ident[:])
 

@@ -146,10 +146,12 @@ def tile_attend_gsink_v_kernel(tc, uT, vT, su, sv, y, offs, qoffs, out):
 
         def turn_words(name, rows, n):
             turned = ps.tile([P, 2, P], F32, name=name + "_turned", tag="bank%d" % n)
-            words = rows.bitcast(F32)
             for w in range(2):
-                nc.tensor.transpose(turned[:, w, :], words[:, w::2], ident[:])
+                nc.tensor.transpose(turned[:, w, :], rows[w], ident[:])
             return turned
+
+        def every_second_word(plane):
+            return [plane.bitcast(F32)[:, w::2] for w in range(2)]
 
         def lay_words(name, turned, over=None):
             along_i = sbuf(name + "_along_i", [P, P, PACK], BF16, over)
@@ -173,7 +175,7 @@ def tile_attend_gsink_v_kernel(tc, uT, vT, su, sv, y, offs, qoffs, out):
             if t == 1:
                 for q in four:
                     weave(0, q)
-            u_along_i[t] = lay_words("u%d" % t, turn_words("u%d" % t, u_plane[t], t))
+            u_along_i[t] = lay_words("u%d" % t, turn_words("u%d" % t, every_second_word(u_plane[t]), t))
             if t > 0:
                 quantise_ui(t - 1, "u_pool%d" % t)
 
@@ -244,7 +246,7 @@ def tile_attend_gsink_v_kernel(tc, uT, vT, su, sv, y, offs, qoffs, out):
             row_max(q)
         for q in four:
             exponent(q)
-        u_last_turned = turn_words("u3", u_plane[3], 0)
+        u_last_turned = turn_words("u3", every_second_word(u_plane[3]), 0)
 
         column_banks = (4, 5, 6, 3)
         y_scaled = sbuf("y_scaled", [P, PACK, SLOTS], F32, "u_along_d3")
@@ -277,11 +279,11 @@ def tile_attend_gsink_v_kernel(tc, uT, vT, su, sv, y, offs, qoffs, out):
         for q in four:
             weigh(nc.vector, q, halves[0])
         u_along_i[3] = lay_words("u3", u_last_turned, "neg_shift3")
-        y_terms = sbuf("y_terms", [P, PACK, P, PACK], F32, "z3")
+        y_terms = sbuf("y_terms", [P, PACK, 2, P, 2], F32, "z3")
         y_term = []
         for n in four:
             w = y_terms[:, n]
-            nc.scalar.activation(w, y_turned[n][:].rearrange("j r s -> j s r"), ACT.Copy, scale=sv_col[:, n : n + 1])
+            nc.scalar.activation(w, y_turned[n][:].rearrange("j (w e) s -> j w s e", w=2), ACT.Copy, scale=sv_col[:, n : n + 1])
             y_term.append(w)
 
         x_turned = []
@@ -310,14 +312,15 @@ def tile_attend_gsink_v_kernel(tc, uT, vT, su, sv, y, offs, qoffs, out):
             nc.vector.reciprocal(col_scale[n][:], col_sum[n][:])
 
         g_along_i = {}
-        g_rows = {}
 
         def gradient(n, into):
-            g = sbuf("g%d" % n, [P, SLOTS], BF16)
-            g_rows[n] = g
-            scale = col_scale[n][:]
-            nc.vector.scalar_tensor_tensor(g[:], flat(x_turned[n]), scale, y_term[n].rearrange("j s r -> j (s r)"), ALU.mult, ALU.subtract)
-            g_along_i[n] = lay_words("g%d" % n, turn_words("g%d" % n, g[:], into))
+            g = [sbuf("g%d_%d" % (n, w), [P, P, 2], BF16) for w in range(2)]
+            x_words = flat(x_turned[n]).rearrange("j (s w e) -> j w s e", w=2, e=2)
+            for w in range(2):
+                nc.vector.scalar_tensor_tensor(
+                    g[w][:], x_words[:, w], col_scale[n][:], y_term[n][:, w], ALU.mult, ALU.subtract
+                )
+            g_along_i[n] = lay_words("g%d" % n, turn_words("g%d" % n, [flat(t).bitcast(F32) for t in g], into))
 
         def quantise_gradient(n):
             cols = slice(PAD + n * P, PAD + (n + 1) * P)

@@ -289,7 +289,7 @@ def tile_attend_gsink_v_kernel(tc, uT, vT, su, sv, y, offs, qoffs, out):
         x_turned = []
 
         def turn_x(n):
-            t = bank(column_banks[n], "x_turned%d" % n)
+            t = bank(column_banks[n % 2], "x_turned%d" % n)
             for q in four:
                 nc.tensor.transpose(t[:, q, :], x[q][n // 2][:, block(n % 2)], ident[:])
             x_turned.append(t)
@@ -364,10 +364,10 @@ def tile_attend_gsink_v_kernel(tc, uT, vT, su, sv, y, offs, qoffs, out):
         column_scale(3)
         quantise_gradient(0)
         early = [product(0, 2, slice(0, SLOTS))]
-        gradient(2, 4)
+        gradient(2, 6)
         quantise_gradient(1)
-        gradient(3, 5)
-        early.append(product(1, 3, slice(P, P + SLOTS)))
+        gradient(3, 3)
+        early.append(product(1, 5, slice(P, P + SLOTS)))
         quantise_gradient(2)
         quantise_gradient(3)
         quantise_ui(2, "e3")
@@ -377,6 +377,6 @@ def tile_attend_gsink_v_kernel(tc, uT, vT, su, sv, y, offs, qoffs, out):
         place(1, halves[0], early[1][:, HALF:])
         left = [slice(P, SLOTS), halves[1], slice(0, SLOTS), slice(0, SLOTS)]
         for t in four:
-            whole = product(t, (0, 6, 7, 1)[t], slice(PAD, PAD + SLOTS))
+            whole = product(t, (0, 7, 4, 1)[t], slice(PAD, PAD + SLOTS))
             place(t, left[t], whole[:, left[t]])
             nc.sync.dma_start(out_rows[:, t, :], window[t][:])

@@ -195,11 +195,12 @@ def tile_attend_gsink_v_kernel(tc, uT, vT, su, sv, y, offs, qoffs, out):
         z = [sbuf("z%d" % q, [P, SLOTS], F32) for q in four]
         e = [sbuf("e%d" % q, [P, SLOTS], F32) for q in four]
         f = [sbuf("f%d" % q, [P, SLOTS], F32) for q in four]
-        x = [[sbuf("x%d_%d" % (q, h), [P, HALF], F32) for h in range(2)] for q in four]
+        x = [[sbuf("x%d" % q, [P, HALF], F32)[:]] for q in four]
         soft_sum = [sbuf("soft_sum%d" % q, [P, 1], F32) for q in range(SOFT_TILES)]
         neg_shift = [sbuf("neg_shift%d" % q, [P, 1], F32) for q in four]
         row_sum = [sbuf("row_sum%d" % q, [P, 1], F32) for q in four]
-        row_inv = [sbuf("row_inv%d" % q, [P, 1], F32) for q in four]
+        row_inv_all = sbuf("row_inv_all", [P, PACK], F32)
+        row_inv = [row_inv_all[:, q : q + 1] for q in four]
 
         def logits(q):
             nc.vector.scalar_tensor_tensor(z[q][:], flat(scores[q]), su_col[:, q : q + 1], sv_all[:], ALU.mult, ALU.mult)
@@ -222,13 +223,13 @@ def tile_attend_gsink_v_kernel(tc, uT, vT, su, sv, y, offs, qoffs, out):
             nc.scalar.activation(e[q][:], z[q][:], ACT.Exp, bias=neg_shift[q][:], accum_out=row_sum[q][:])
 
         def invert(q):
-            nc.vector.reciprocal(row_inv[q][:], row_sum[q][:])
+            nc.vector.reciprocal(row_inv[q], row_sum[q][:])
 
         def normalise(q, cols=slice(0, SLOTS)):
-            nc.vector.tensor_scalar(f[q][:, cols], e[q][:, cols], row_inv[q][:], None, ALU.mult)
+            nc.vector.tensor_scalar(f[q][:, cols], e[q][:, cols], row_inv[q], None, ALU.mult)
 
-        def weigh(engine, q, cols):
-            engine.tensor_scalar(x[q][cols.start // HALF][:], e[q][:, cols], row_inv[q][:], su_col[:, q : q + 1], ALU.mult, ALU.mult)
+        def weigh(q):
+            nc.vector.tensor_scalar(x[q][0], e[q][:, halves[0]], row_inv[q], su_col[:, q : q + 1], ALU.mult, ALU.mult)
 
         for q in four:
             gather_plane(3, block(q))
@@ -260,31 +261,43 @@ def tile_attend_gsink_v_kernel(tc, uT, vT, su, sv, y, offs, qoffs, out):
         groups = ((0,), (1,), (2, 3))
         sums = [ps.tile([P, len(groups[h]), P], F32, name="sums%d" % h, tag="bank%d" % (7, 2, 1)[h]) for h in range(3)]
 
-        def add_columns(q, h):
+        def add_tile(q, cols=slice(0, SLOTS)):
+            nc.vector.scalar_tensor_tensor(f[q][:, cols], e[q][:, cols], row_inv[q], f[q - 1][:, cols], ALU.mult, ALU.add)
+
+        def turn_sums(q, h):
             for k, n in enumerate(groups[h]):
                 nc.tensor.matmul(
                     sums[h][:, k, :], f[q][:, block(n)], ident[:],
-                    start=q == 0 and k == 0, stop=q == PACK - 1 and n == groups[h][-1], is_transpose=True,
+                    start=q == h // 2 and k == 0, stop=q == PACK - 1 and n == groups[h][-1], is_transpose=True,
                 )
 
-        for q in range(PACK - 1):
-            invert(q)
-            normalise(q)
-            for h in range(3):
-                add_columns(q, h)
+        invert(0)
+        normalise(0)
+        invert(1)
+        normalise(1, halves[0])
+        for q in range(2):
+            for h in range(2):
+                turn_sums(q, h)
+        invert(2)
+        normalise(2)
         invert(3)
         for n in range(2):
-            normalise(3, block(n))
-            add_columns(3, n)
+            add_tile(3, block(n))
+            turn_sums(3, n)
         for q in four:
-            weigh(nc.vector, q, halves[0])
+            weigh(q)
+        row_scale = sbuf("row_scale", [P, PACK], F32)
+        nc.vector.tensor_tensor(row_scale[:], row_inv_all[:], su_col[:], ALU.mult)
         u_along_i[3] = lay_words("u3", u_last_turned, "neg_shift3")
         y_terms = sbuf("y_terms", [P, PACK, 2, P, 2], F32, "z3")
-        y_term = []
-        for n in four:
-            w = y_terms[:, n]
-            nc.scalar.activation(w, y_turned[n][:].rearrange("j (w e) s -> j w s e", w=2), ACT.Copy, scale=sv_col[:, n : n + 1])
-            y_term.append(w)
+        y_term = [y_terms[:, n] for n in four]
+
+        def lay_y_term(n):
+            dealt = y_turned[n][:].rearrange("j (w e) s -> j w s e", w=2)
+            nc.scalar.activation(y_term[n], dealt, ACT.Copy, scale=sv_col[:, n : n + 1])
+
+        lay_y_term(0)
+        lay_y_term(1)
 
         x_turned = []
 
@@ -294,22 +307,24 @@ def tile_attend_gsink_v_kernel(tc, uT, vT, su, sv, y, offs, qoffs, out):
                 nc.tensor.transpose(t[:, q, :], x[q][n // 2][:, block(n % 2)], ident[:])
             x_turned.append(t)
 
-        col_sum = [sbuf("col_sum%d" % n, [P, 1], F32) for n in four]
-        col_scale = [sbuf("col_scale%d" % n, [P, 1], F32) for n in four]
+        sum_tiles = [sbuf("col_sum%d" % h, [P, len(groups[h])], F32) for h in range(3)]
+        scale_tiles = [sbuf("col_scale%d" % h, [P, len(groups[h])], F32) for h in range(3)]
+        col_sum = [sum_tiles[h][:, k : k + 1] for h in range(3) for k in range(len(groups[h]))]
+        col_scale = [scale_tiles[h][:, k : k + 1] for h in range(3) for k in range(len(groups[h]))]
         spent = [sbuf("spent%d" % n, [P, P], F32) for n in four]
 
         def column_sum(n):
-            if n < 2:
+            if n == 0:
                 nc.vector.tensor_scalar(
-                    spent[n][:], sums[n][:, 0, :], sv_inv_col[:, n : n + 1], None, ALU.mult, ALU.add, accum_out=col_sum[n][:]
+                    spent[n][:], sums[0][:, 0, :], sv_inv_col[:, n : n + 1], None, ALU.mult, ALU.add, accum_out=col_sum[n]
                 )
             else:
                 nc.scalar.activation(
-                    spent[n][:], sums[2][:, n - 2, :], ACT.Copy, scale=sv_inv_col[:, n : n + 1], accum_out=col_sum[n][:]
+                    spent[n][:], sums[min(n, 2)][:, max(n - 2, 0), :], ACT.Copy, scale=sv_inv_col[:, n : n + 1], accum_out=col_sum[n]
                 )
 
-        def column_scale(n):
-            nc.vector.reciprocal(col_scale[n][:], col_sum[n][:])
+        def column_scale(h):
+            nc.vector.reciprocal(scale_tiles[h][:], sum_tiles[h][:])
 
         g_along_i = {}
 
@@ -318,7 +333,7 @@ def tile_attend_gsink_v_kernel(tc, uT, vT, su, sv, y, offs, qoffs, out):
             x_words = flat(x_turned[n]).rearrange("j (s w e) -> j w s e", w=2, e=2)
             for w in range(2):
                 nc.vector.scalar_tensor_tensor(
-                    g[w][:], x_words[:, w], col_scale[n][:], y_term[n][:, w], ALU.mult, ALU.subtract
+                    g[w][:], x_words[:, w], col_scale[n], y_term[n][:, w], ALU.mult, ALU.subtract
                 )
             g_along_i[n] = lay_words("g%d" % n, turn_words("g%d" % n, [flat(t).bitcast(F32) for t in g], into))
 
@@ -346,22 +361,26 @@ def tile_attend_gsink_v_kernel(tc, uT, vT, su, sv, y, offs, qoffs, out):
 
         turn_x(0)
         column_sum(0)
-        column_sum(1)
         column_scale(0)
-        column_scale(1)
+        column_sum(1)
+        lay_y_term(2)
+        lay_y_term(3)
         turn_x(1)
         gradient(0, 0)
-        normalise(3, halves[1])
-        add_columns(3, 2)
+        for q in (1, 3):
+            add_tile(q, halves[1])
+            turn_sums(q, 2)
+        x_late = sbuf("x_late", [P, PACK, HALF], F32, "row_inv_all")
         for q in four:
-            weigh(nc.vector, q, halves[1])
+            x[q].append(x_late[:, q, :])
+            nc.gpsimd.tensor_scalar(x[q][1], e[q][:, halves[1]], row_scale[:, q : q + 1], 0.0, ALU.mult, ALU.add)
         turn_x(2)
+        column_scale(1)
         gradient(1, 7)
         turn_x(3)
         column_sum(2)
         column_sum(3)
         column_scale(2)
-        column_scale(3)
         quantise_gradient(0)
         early = [product(0, 2, slice(0, SLOTS))]
         gradient(2, 6)
@@ -370,8 +389,8 @@ def tile_attend_gsink_v_kernel(tc, uT, vT, su, sv, y, offs, qoffs, out):
         early.append(product(1, 5, slice(P, P + SLOTS)))
         quantise_gradient(2)
         quantise_gradient(3)
-        quantise_ui(2, "e3")
-        quantise_ui(3, None)
+        quantise_ui(2, "g0_along_i")
+        quantise_ui(3, "g1_along_i")
 
         place(0, block(0), early[0][:, PAD:])
         place(1, halves[0], early[1][:, HALF:])

@@ -122,6 +122,9 @@ def tile_attend_gsink_v_kernel(tc, uT, vT, su, sv, y, offs, qoffs, out):
             nc.tensor.transpose(sv_spread[:, n, :], sv_col[:, n : n + 1].to_broadcast([P, P]), ident[:])
         sv_all = sbuf("sv_all", [P, SLOTS], F32)
         nc.scalar.copy(sv_all[:], flat(sv_spread))
+        last_factor = sbuf("last_factor", [P, PACK, P], F32)
+        for r in four:
+            nc.scalar.activation(last_factor[:, r, :], sv_all[:, block(3)], ACT.Copy, scale=su_dealt[:, r : r + 1])
         for t in four:
             gather_v(t)
         nc.scalar.copy(
@@ -249,14 +252,12 @@ def tile_attend_gsink_v_kernel(tc, uT, vT, su, sv, y, offs, qoffs, out):
             exponent(q)
         u_last_turned = turn_words("u3", every_second_word(u_plane[3]), 0)
 
-        column_banks = (4, 5, 6, 3)
-        y_scaled = sbuf("y_scaled", [P, PACK, SLOTS], F32, "u_along_d3")
-        y_su = [y_scaled[:, r, :] for r in four]
-        y_turned = [bank(column_banks[n], "y_turned%d" % n) for n in four]
+        y_scaled = sbuf("y_scaled", [P, PACK, PAD], F32, "u_along_d3")
+        y_turned = [bank(4 + n, "y_turned%d" % n) for n in range(PACK - 1)]
         for r in four:
-            nc.gpsimd.tensor_scalar(y_su[r], y_sb[:, r, :], su_dealt[:, r : r + 1], 0.0, ALU.mult, ALU.add)
-            for n in four:
-                nc.tensor.transpose(y_turned[n][:, r, :], y_su[r][:, block(n)], ident[:])
+            nc.gpsimd.tensor_scalar(y_scaled[:, r, :], y_sb[:, r, 0:PAD], su_dealt[:, r : r + 1], 0.0, ALU.mult, ALU.add)
+            for n in range(PACK - 1):
+                nc.tensor.transpose(y_turned[n][:, r, :], y_scaled[:, r, block(n)], ident[:])
 
         groups = ((0,), (1,), (2, 3))
         sums = [ps.tile([P, len(groups[h]), P], F32, name="sums%d" % h, tag="bank%d" % (7, 2, 1)[h]) for h in range(3)]
@@ -286,11 +287,9 @@ def tile_attend_gsink_v_kernel(tc, uT, vT, su, sv, y, offs, qoffs, out):
             turn_sums(3, n)
         for q in four:
             weigh(q)
-        row_scale = sbuf("row_scale", [P, PACK], F32)
-        nc.vector.tensor_tensor(row_scale[:], row_inv_all[:], su_col[:], ALU.mult)
         u_along_i[3] = lay_words("u3", u_last_turned, "neg_shift3")
-        y_terms = sbuf("y_terms", [P, PACK, 2, P, 2], F32, "z3")
-        y_term = [y_terms[:, n] for n in four]
+        y_terms = sbuf("y_terms", [P, PACK - 1, 2, P, 2], F32, "z3")
+        y_term = [y_terms[:, n] for n in range(PACK - 1)]
 
         def lay_y_term(n):
             dealt = y_turned[n][:].rearrange("j (w e) s -> j w s e", w=2)
@@ -299,13 +298,13 @@ def tile_attend_gsink_v_kernel(tc, uT, vT, su, sv, y, offs, qoffs, out):
         lay_y_term(0)
         lay_y_term(1)
 
-        x_turned = []
+        x_turned = {}
 
         def turn_x(n):
-            t = bank(column_banks[n % 2], "x_turned%d" % n)
+            t = bank((4, 5, 4, 3)[n], "x_turned%d" % n)
             for q in four:
                 nc.tensor.transpose(t[:, q, :], x[q][n // 2][:, block(n % 2)], ident[:])
-            x_turned.append(t)
+            x_turned[n] = t
 
         sum_tiles = [sbuf("col_sum%d" % h, [P, len(groups[h])], F32) for h in range(3)]
         scale_tiles = [sbuf("col_scale%d" % h, [P, len(groups[h])], F32) for h in range(3)]
@@ -364,38 +363,46 @@ def tile_attend_gsink_v_kernel(tc, uT, vT, su, sv, y, offs, qoffs, out):
         column_scale(0)
         column_sum(1)
         lay_y_term(2)
-        lay_y_term(3)
         turn_x(1)
         gradient(0, 0)
         for q in (1, 3):
             add_tile(q, halves[1])
             turn_sums(q, 2)
-        x_late = sbuf("x_late", [P, PACK, HALF], F32, "row_inv_all")
         for q in four:
-            x[q].append(x_late[:, q, :])
-            nc.gpsimd.tensor_scalar(x[q][1], e[q][:, halves[1]], row_scale[:, q : q + 1], 0.0, ALU.mult, ALU.add)
+            x[q].append(sbuf("x_late%d" % q, [P, HALF], F32)[:])
+            nc.vector.tensor_scalar(x[q][1], e[q][:, halves[1]], row_inv[q], su_col[:, q : q + 1], ALU.mult, ALU.mult)
+        last_y_term = sbuf("last_y_term", [P, PACK, P], F32, "row_inv_all")
+        nc.gpsimd.tensor_tensor(last_y_term[:], y_sb[:, :, block(3)], last_factor[:], ALU.mult)
+        turn_x(3)
         turn_x(2)
         column_scale(1)
         gradient(1, 7)
-        turn_x(3)
-        column_sum(2)
         column_sum(3)
+        column_sum(2)
         column_scale(2)
         quantise_gradient(0)
         early = [product(0, 2, slice(0, SLOTS))]
-        gradient(2, 6)
+        scaled = sbuf("scaled", [P, PACK, P], F32)
+        nc.scalar.activation(scaled[:], flat(x_turned[3]).rearrange("j (s r) -> j r s", r=PACK), ACT.Copy, scale=col_scale[3])
+        gradient(2, 1)
+        last_back = bank(6, "last_back")
+        for r in four:
+            nc.tensor.transpose(last_back[:, r, :], scaled[:, r, :], ident[:])
         quantise_gradient(1)
-        gradient(3, 3)
-        early.append(product(1, 5, slice(P, P + SLOTS)))
+        g_along_i[3] = sbuf("g3_along_i", [P, P, PACK], BF16)
+        nc.vector.tensor_tensor(
+            g_along_i[3][:], last_back[:].rearrange("s r j -> s j r"), last_y_term[:].rearrange("s r j -> s j r"), ALU.subtract
+        )
+        early.append(product(1, 4, slice(P, P + SLOTS)))
         quantise_gradient(2)
         quantise_gradient(3)
-        quantise_ui(2, "g0_along_i")
-        quantise_ui(3, "g1_along_i")
+        quantise_ui(2, "e3")
+        quantise_ui(3, None)
 
         place(0, block(0), early[0][:, PAD:])
         place(1, halves[0], early[1][:, HALF:])
         left = [slice(P, SLOTS), halves[1], slice(0, SLOTS), slice(0, SLOTS)]
         for t in four:
-            whole = product(t, (0, 7, 4, 1)[t], slice(PAD, PAD + SLOTS))
+            whole = product(t, (0, 7, 3, 5)[t], slice(PAD, PAD + SLOTS))
             place(t, left[t], whole[:, left[t]])
             nc.sync.dma_start(out_rows[:, t, :], window[t][:])

@@ -20,7 +20,6 @@ P = 128
 PACK = 4
 SLOTS = 512
 HALF = SLOTS // 2
-PAD = SLOTS - P
 POOL = 2048
 FEATURES = 512
 SOFTEN = 8.0
@@ -34,6 +33,7 @@ BYTES = 4 * (3 * FEATURES * POOL + SLOTS * SLOTS + 2 * POOL) + 2 * 2 * P * (SLOT
 def tile_attend_gsink_v_kernel(tc, uT, vT, su, sv, y, offs, qoffs, out):
     nc = tc.nc
     four = range(PACK)
+    whole = slice(0, SLOTS)
     halves = (slice(0, HALF), slice(HALF, SLOTS))
 
     def block(n):
@@ -42,6 +42,9 @@ def tile_attend_gsink_v_kernel(tc, uT, vT, su, sv, y, offs, qoffs, out):
     def flat(t):
         return t[:].rearrange("p a b -> p (a b)")
 
+    def entries(listed, part):
+        return listed[:, part.start // 16 : part.stop // 16]
+
     with ExitStack() as ctx:
         sb = ctx.enter_context(tc.tile_pool(name="sb", bufs=1))
         ps = ctx.enter_context(tc.psum_pool(name="ps", bufs=1))
@@ -49,16 +52,18 @@ def tile_attend_gsink_v_kernel(tc, uT, vT, su, sv, y, offs, qoffs, out):
         def sbuf(name, shape, dtype, over=None):
             return sb.tile(shape, dtype, name=name, tag=over or name, align_bytes=64)
 
-        def bank(n, name, dtype=F32):
-            return ps.tile([P, PACK, P], dtype, name=name, tag="bank%d" % n)
+        def bank(n, name, parts=PACK):
+            return ps.tile([P, parts, P], F32, name=name, tag="bank%d" % n)
+
+        def operand(name, width, over=None):
+            return sbuf(name + "_codes", [P, width], U32, over), sbuf(name + "_scales", [P, width], U8)
 
         i_list = sb.tile([P, SLOTS // 16], U16, name="i_list")
         j_list = sb.tile([P, SLOTS // 16], U16, name="j_list")
-
         su_pool = sbuf("su_pool", [P, POOL], F32)
         sv_pool = sbuf("sv_pool", [P, POOL], F32)
-        nc.vector.memset(su_pool[0 : P - 1, :].bitcast(I32), 0)
         nc.vector.memset(sv_pool[0 : P - 1, :].bitcast(I32), 0)
+        nc.vector.memset(su_pool[0 : P - 1, :].bitcast(I32), 0)
         u_rows = uT.rearrange("(p t) c -> p t c", t=PACK)
         v_rows = vT.rearrange("(p t) c -> p t c", t=PACK)
         out_rows = out.rearrange("(p t) c -> p t c", t=PACK)
@@ -77,84 +82,59 @@ def tile_attend_gsink_v_kernel(tc, uT, vT, su, sv, y, offs, qoffs, out):
 
         ident = sbuf("ident", [P, P], F32)
         make_identity(nc, ident[:])
-
-        def operand(name, width=SLOTS, over=None):
-            return sbuf(name + "_codes", [P, width], U32, over), sbuf(name + "_scales", [P, width], U8)
-
-        g_codes, g_scales = operand("g", PAD + SLOTS)
-        nc.gpsimd.memset(g_codes[:, 0:PAD], 0)
-        nc.gpsimd.memset(g_scales[:, 0:PAD], 0)
         zeros = sbuf("zeros", [P, P], F32)
         nc.gpsimd.memset(zeros[:], 0.0)
-
-        v_along_d = sbuf("v_along_d", [P, SLOTS, PACK], BF16)
-
-        v_pairs = sbuf("v_pairs", [P, 2, SLOTS, 2], BF16)
-
-        def gather_v(t):
-            nc.vector.tensor_copy(v_pairs[:, t // 2, :, t % 2], v_pool[t // 2][:, t % 2, :].indirect(j_list[:]))
+        window = [sbuf("window%d" % t, [P, POOL], F32) for t in four]
+        for cleared in window:
+            nc.gpsimd.memset(cleared[:].bitcast(I32), 0)
 
         su_row = sbuf("su_row", [P, SLOTS], F32)
         sv_row = sbuf("sv_row", [P, SLOTS], F32)
-        nc.vector.tensor_copy(su_row[:], su_pool[:].indirect(i_list[:]))
-        nc.vector.tensor_copy(sv_row[:], sv_pool[:].indirect(j_list[:]))
-        su_turned = bank(4, "su_turned")
-        su_dealt_turned = bank(5, "su_dealt_turned")
-        sv_turned = bank(6, "sv_turned")
-        for n in four:
-            nc.tensor.transpose(su_turned[:, n, :], su_row[:, block(n)], ident[:])
-        for n in four:
-            nc.tensor.transpose(su_dealt_turned[:, n, :], su_row[:, n::PACK], ident[:])
-        for n in four:
-            nc.tensor.transpose(sv_turned[:, n, :], sv_row[:, block(n)], ident[:])
-        su_col = sbuf("su_col", [P, PACK], F32)
-        su_dealt = sbuf("su_dealt", [P, PACK], F32)
-        sv_col = sbuf("sv_col", [P, PACK], F32)
-        nc.scalar.copy(su_col[:], su_turned[:, :, P - 1])
-        nc.scalar.copy(su_dealt[:], su_dealt_turned[:, :, P - 1])
-        nc.scalar.copy(sv_col[:], sv_turned[:, :, P - 1])
-        sv_inv = sbuf("sv_inv", [P, PACK], F32)
-        sv_inv_col = sbuf("sv_inv_col", [P, PACK], F32)
-        nc.vector.reciprocal(sv_inv[:], sv_col[:])
-        nc.vector.tensor_scalar(sv_inv_col[:], sv_inv[:], LARGE, -LARGE, ALU.min, ALU.max)
+        nc.scalar.activation(sv_row[:], sv_pool[:].indirect(j_list[:]), ACT.Copy)
+        nc.scalar.activation(su_row[:], su_pool[:].indirect(i_list[:]), ACT.Copy)
+
+        def as_columns(name, n, rows):
+            turned = bank(n, name + "_turned")
+            for k in four:
+                nc.tensor.transpose(turned[:, k, :], rows[k], ident[:])
+            columns = sbuf(name, [P, PACK], F32)
+            nc.scalar.copy(columns[:], turned[:, :, P - 1])
+            return columns
+
+        sv_col = as_columns("sv_col", 4, [sv_row[:, block(n)] for n in four])
+        su_col = as_columns("su_col", 5, [su_row[:, block(n)] for n in four])
+        su_dealt = as_columns("su_dealt", 6, [su_row[:, r::PACK] for r in four])
         sv_spread = bank(7, "sv_spread")
         for n in four:
             nc.tensor.transpose(sv_spread[:, n, :], sv_col[:, n : n + 1].to_broadcast([P, P]), ident[:])
         sv_all = sbuf("sv_all", [P, SLOTS], F32)
         nc.scalar.copy(sv_all[:], flat(sv_spread))
-        last_factor = sbuf("last_factor", [P, PACK, P], F32)
-        for r in four:
-            nc.scalar.activation(last_factor[:, r, :], sv_all[:, block(3)], ACT.Copy, scale=su_dealt[:, r : r + 1])
-        for t in four:
-            gather_v(t)
-        nc.scalar.copy(
-            flat(v_along_d).bitcast(U32).rearrange("p (j h) -> p j h", h=2),
-            v_pairs[:].rearrange("p h j e -> p (h j e)").bitcast(U32).rearrange("p (h j) -> p j h", h=2),
-        )
-        window = [sbuf("window%d" % t, [P, POOL], F32) for t in four]
-        for cleared in window:
-            nc.gpsimd.memset(cleared[:].bitcast(I32), 0)
 
+        v_along_d = sbuf("v_along_d", [P, SLOTS, PACK], BF16)
+        for t in four:
+            nc.vector.tensor_copy(v_along_d[:, :, t], v_pool[t // 2][:, t % 2, :].indirect(j_list[:]))
+        v_codes, v_scales = operand("v", SLOTS)
+        nc.vector.quantize_mx(v_codes[:].bitcast(E4M3), v_scales[:], flat(v_along_d))
+        sv_inv = sbuf("sv_inv", [P, PACK], F32)
+        sv_inv_col = sbuf("sv_inv_col", [P, PACK], F32)
+        nc.vector.reciprocal(sv_inv[:], sv_col[:])
+        nc.vector.tensor_scalar(sv_inv_col[:], sv_inv[:], LARGE, -LARGE, ALU.min, ALU.max)
 
         u_along_d = [sbuf("u_along_d%d" % q, [P, P, PACK], BF16) for q in four]
-        ud_codes, ud_scales = operand("ud")
         u_pair = [sbuf("u_pair%d" % h, [P, 2, SLOTS], BF16) for h in range(2)]
         u_plane = [u_pair[t // 2][:, t % 2, :] for t in four]
 
-        def gather_plane(t, part=slice(0, SLOTS)):
-            nc.vector.tensor_copy(u_plane[t][:, part], u_pool[t][:].indirect(i_list[:, part.start // 16 : part.stop // 16]))
+        def u_listed(t, part):
+            return u_pool[t][:].indirect(entries(i_list, part))
 
-        def weave(h, q):
-            nc.scalar.copy(u_along_d[q][:, :, 2 * h : 2 * h + 2], u_pair[h][:, :, block(q)].rearrange("p t i -> p i t"))
+        def weave(copy, h, q):
+            copy(u_along_d[q][:, :, 2 * h : 2 * h + 2], u_pair[h][:, :, block(q)].rearrange("p t i -> p i t"))
 
         def turn_words(name, rows, n):
-            turned = ps.tile([P, 2, P], F32, name=name + "_turned", tag="bank%d" % n)
+            turned = bank(n, name + "_turned", 2)
             for w in range(2):
                 nc.tensor.transpose(turned[:, w, :], rows[w], ident[:])
             return turned
-
-        def every_second_word(plane):
-            return [plane.bitcast(F32)[:, w::2] for w in range(2)]
 
         def lay_words(name, turned, over=None):
             along_i = sbuf(name + "_along_i", [P, P, PACK], BF16, over)
@@ -162,247 +142,217 @@ def tile_attend_gsink_v_kernel(tc, uT, vT, su, sv, y, offs, qoffs, out):
             nc.scalar.copy(words, turned[:].rearrange("s w x -> s x w"))
             return along_i
 
-        def quantise_ud(q):
-            nc.vector.quantize_mx(ud_codes[:, block(q)].bitcast(E4M3), ud_scales[:, block(q)], flat(u_along_d[q]))
-
         u_along_i = {}
         ui = {}
 
-        def quantise_ui(t, over):
+        def turn_u(t, n):
+            rows = [u_plane[t].bitcast(F32)[:, w::2] for w in range(2)]
+            u_along_i[t] = lay_words("u%d" % t, turn_words("u%d" % t, rows, n))
+
+        def quantise_ui(t, over=None):
             codes, scales = operand("ui%d" % t, P, over)
             nc.vector.quantize_mx(codes[:].bitcast(E4M3), scales[:], flat(u_along_i[t]))
-            ui[t] = (codes[:], scales[:])
+            ui[t] = (codes[:].bitcast(E4M3), scales[:])
 
         for t in range(PACK - 1):
-            gather_plane(t)
+            nc.vector.tensor_copy(u_plane[t], u_listed(t, whole))
             if t == 1:
                 for q in four:
-                    weave(0, q)
-            u_along_i[t] = lay_words("u%d" % t, turn_words("u%d" % t, every_second_word(u_plane[t]), t))
+                    weave(nc.scalar.copy, 0, q)
+            turn_u(t, t)
             if t > 0:
                 quantise_ui(t - 1, "u_pool%d" % t)
 
-        v_codes, v_scales = operand("v", SLOTS, "u_pool0")
-        nc.vector.quantize_mx(v_codes[:].bitcast(E4M3), v_scales[:], flat(v_along_d))
-
+        ud = [operand("ud%d" % q, P) for q in four]
         scores = []
 
         def score(q):
+            codes, scales = ud[q]
+            nc.vector.quantize_mx(codes[:].bitcast(E4M3), scales[:], flat(u_along_d[q]))
             a = bank(q, "scores%d" % q)
             nc.tensor.matmul_mx(
-                flat(a), lhsT=ud_codes[:, block(q)].bitcast(E4M3), lhsT_scale=ud_scales[:, block(q)],
+                flat(a), lhsT=codes[:].bitcast(E4M3), lhsT_scale=scales[:],
                 rhs=v_codes[:].bitcast(E4M3), rhs_scale=v_scales[:], start=True, stop=True,
             )
             scores.append(a)
 
+        for q in range(2):
+            nc.vector.tensor_copy(u_plane[3][:, block(q)], u_listed(3, block(q)))
+        nc.scalar.activation(u_plane[3][:, halves[1]], u_listed(3, halves[1]), ACT.Copy)
+        for q in four:
+            weave(nc.vector.tensor_copy if q < 2 else nc.scalar.copy, 1, q)
+        for q in four:
+            score(q)
+        turn_u(3, 7)
+        quantise_ui(2, "u_along_d3")
+
         z = [sbuf("z%d" % q, [P, SLOTS], F32) for q in four]
         e = [sbuf("e%d" % q, [P, SLOTS], F32) for q in four]
         f = [sbuf("f%d" % q, [P, SLOTS], F32) for q in four]
-        x = [[sbuf("x%d" % q, [P, HALF], F32)[:]] for q in four]
-        soft_sum = [sbuf("soft_sum%d" % q, [P, 1], F32) for q in range(SOFT_TILES)]
+        x = [sbuf("x%d" % q, [P, SLOTS], F32) for q in four]
         neg_shift = [sbuf("neg_shift%d" % q, [P, 1], F32) for q in four]
         row_sum = [sbuf("row_sum%d" % q, [P, 1], F32) for q in four]
-        row_inv_all = sbuf("row_inv_all", [P, PACK], F32)
-        row_inv = [row_inv_all[:, q : q + 1] for q in four]
+        row_inv = [sbuf("row_inv%d" % q, [P, 1], F32) for q in four]
 
-        def logits(q):
+        for q in four:
             nc.vector.scalar_tensor_tensor(z[q][:], flat(scores[q]), su_col[:, q : q + 1], sv_all[:], ALU.mult, ALU.mult)
-
-        def soft_bound(q):
-            nc.scalar.activation(e[q][:], z[q][:], ACT.Exp, scale=1.0 / SOFTEN, accum_out=soft_sum[q][:])
-
-        def soft_shift(q):
-            per_bit = SOFTEN * math.log(2.0)
-            slope = sbuf("slope%d" % q, [P, 1], F32)
-            nc.vector.tensor_scalar(
-                slope[:], soft_sum[q][:].bitcast(I32), -per_bit / 2.0**23, per_bit * (127 + 9), ALU.mult, ALU.add,
-                accum_out=neg_shift[q][:],
-            )
-
-        def row_max(q):
-            nc.vector.tensor_reduce(neg_shift[q][:], z[q][:], AXIS.X, ALU.max, negate=True)
-
-        def exponent(q):
-            nc.scalar.activation(e[q][:], z[q][:], ACT.Exp, bias=neg_shift[q][:], accum_out=row_sum[q][:])
-
-        def invert(q):
-            nc.vector.reciprocal(row_inv[q], row_sum[q][:])
-
-        def normalise(q, cols=slice(0, SLOTS)):
-            nc.vector.tensor_scalar(f[q][:, cols], e[q][:, cols], row_inv[q], None, ALU.mult)
-
-        def weigh(q):
-            nc.vector.tensor_scalar(x[q][0], e[q][:, halves[0]], row_inv[q], su_col[:, q : q + 1], ALU.mult, ALU.mult)
-
-        for q in four:
-            gather_plane(3, block(q))
-            weave(1, q)
-        for q in four:
-            quantise_ud(q)
-            score(q)
-        for q in range(SOFT_TILES):
-            logits(q)
-            soft_bound(q)
-        for q in range(SOFT_TILES):
-            soft_shift(q)
-        for q in range(SOFT_TILES, PACK):
-            logits(q)
-            row_max(q)
-        for q in four:
-            exponent(q)
-        u_last_turned = turn_words("u3", every_second_word(u_plane[3]), 0)
-
-        y_scaled = sbuf("y_scaled", [P, PACK, PAD], F32, "u_along_d3")
-        y_turned = [bank(4 + n, "y_turned%d" % n) for n in range(PACK - 1)]
-        for r in four:
-            nc.gpsimd.tensor_scalar(y_scaled[:, r, :], y_sb[:, r, 0:PAD], su_dealt[:, r : r + 1], 0.0, ALU.mult, ALU.add)
-            for n in range(PACK - 1):
-                nc.tensor.transpose(y_turned[n][:, r, :], y_scaled[:, r, block(n)], ident[:])
-
-        groups = ((0,), (1,), (2, 3))
-        sums = [ps.tile([P, len(groups[h]), P], F32, name="sums%d" % h, tag="bank%d" % (7, 2, 1)[h]) for h in range(3)]
-
-        def add_tile(q, cols=slice(0, SLOTS)):
-            nc.vector.scalar_tensor_tensor(f[q][:, cols], e[q][:, cols], row_inv[q], f[q - 1][:, cols], ALU.mult, ALU.add)
-
-        def turn_sums(q, h):
-            for k, n in enumerate(groups[h]):
-                nc.tensor.matmul(
-                    sums[h][:, k, :], f[q][:, block(n)], ident[:],
-                    start=q == h // 2 and k == 0, stop=q == PACK - 1 and n == groups[h][-1], is_transpose=True,
-                )
-
-        invert(0)
-        normalise(0)
-        invert(1)
-        normalise(1, halves[0])
-        for q in range(2):
-            for h in range(2):
-                turn_sums(q, h)
-        invert(2)
-        normalise(2)
-        invert(3)
-        for n in range(2):
-            add_tile(3, block(n))
-            turn_sums(3, n)
-        for q in four:
-            weigh(q)
-        u_along_i[3] = lay_words("u3", u_last_turned, "neg_shift3")
-        y_terms = sbuf("y_terms", [P, PACK - 1, 2, P, 2], F32, "z3")
-        y_term = [y_terms[:, n] for n in range(PACK - 1)]
-
-        def lay_y_term(n):
-            dealt = y_turned[n][:].rearrange("j (w e) s -> j w s e", w=2)
-            nc.scalar.activation(y_term[n], dealt, ACT.Copy, scale=sv_col[:, n : n + 1])
-
-        lay_y_term(0)
-        lay_y_term(1)
-
-        x_turned = {}
-
-        def turn_x(n):
-            t = bank((4, 5, 4, 3)[n], "x_turned%d" % n)
-            for q in four:
-                nc.tensor.transpose(t[:, q, :], x[q][n // 2][:, block(n % 2)], ident[:])
-            x_turned[n] = t
-
-        sum_tiles = [sbuf("col_sum%d" % h, [P, len(groups[h])], F32) for h in range(3)]
-        scale_tiles = [sbuf("col_scale%d" % h, [P, len(groups[h])], F32) for h in range(3)]
-        col_sum = [sum_tiles[h][:, k : k + 1] for h in range(3) for k in range(len(groups[h]))]
-        col_scale = [scale_tiles[h][:, k : k + 1] for h in range(3) for k in range(len(groups[h]))]
-        spent = [sbuf("spent%d" % n, [P, P], F32) for n in four]
-
-        def column_sum(n):
-            if n == 0:
+            if q < SOFT_TILES:
+                soft_sum = sbuf("soft_sum%d" % q, [P, 1], F32)
+                slope = sbuf("slope%d" % q, [P, 1], F32)
+                per_bit = SOFTEN * math.log(2.0)
+                nc.scalar.activation(e[q][:], z[q][:], ACT.Exp, scale=1.0 / SOFTEN, accum_out=soft_sum[:])
                 nc.vector.tensor_scalar(
-                    spent[n][:], sums[0][:, 0, :], sv_inv_col[:, n : n + 1], None, ALU.mult, ALU.add, accum_out=col_sum[n]
+                    slope[:], soft_sum[:].bitcast(I32), -per_bit / 2.0**23, per_bit * (127 + 9), ALU.mult, ALU.add,
+                    accum_out=neg_shift[q][:],
                 )
             else:
-                nc.scalar.activation(
-                    spent[n][:], sums[min(n, 2)][:, max(n - 2, 0), :], ACT.Copy, scale=sv_inv_col[:, n : n + 1], accum_out=col_sum[n]
-                )
+                nc.vector.tensor_reduce(neg_shift[q][:], z[q][:], AXIS.X, ALU.max, negate=True)
+        for q in four:
+            nc.scalar.activation(e[q][:], z[q][:], ACT.Exp, bias=neg_shift[q][:], accum_out=row_sum[q][:])
 
-        def column_scale(h):
-            nc.vector.reciprocal(scale_tiles[h][:], sum_tiles[h][:])
+        y_scaled = sbuf("y_scaled", [P, PACK, SLOTS], F32)
+        y_turned = [bank(4 + n, "y_turned%d" % n) for n in four]
+        for r in four:
+            nc.gpsimd.tensor_scalar(y_scaled[:, r, :], y_sb[:, r, :], su_dealt[:, r : r + 1], 0.0, ALU.mult, ALU.add)
+            for n in four:
+                nc.tensor.transpose(y_turned[n][:, r, :], y_scaled[:, r, block(n)], ident[:])
 
+        def normalise(q, cols):
+            nc.vector.tensor_scalar(f[q][:, cols], e[q][:, cols], row_inv[q][:], None, ALU.mult)
+            nc.vector.tensor_scalar(x[q][:, cols], e[q][:, cols], row_inv[q][:], su_col[:, q : q + 1], ALU.mult, ALU.mult)
+
+        for q in four:
+            nc.vector.reciprocal(row_inv[q][:], row_sum[q][:])
+            normalise(q, whole if q < PACK - 1 else block(0))
+        normalise(PACK - 1, slice(P, SLOTS))
+
+        y_terms = sbuf("y_terms", [P, PACK, 2, P, 2], F32, "z3")
+        for n in four:
+            dealt = y_turned[n][:].rearrange("j (w e) s -> j w s e", w=2)
+            nc.scalar.activation(y_terms[:, n], dealt, ACT.Copy, scale=sv_col[:, n : n + 1])
+
+        col_scale = {}
+        x_turned = {}
         g_along_i = {}
+        g_codes, g_scales = operand("g", SLOTS)
+
+        def turn_sums(blocks, into):
+            sums = bank(into, "sums%d" % blocks[0], len(blocks))
+            for k, n in enumerate(blocks):
+                for q in four:
+                    nc.tensor.matmul(
+                        sums[:, k, :], f[q][:, block(n)], ident[:],
+                        start=q == 0 and k == 0, stop=q == PACK - 1 and n == blocks[-1], is_transpose=True,
+                    )
+            return sums
+
+        def turn_x(n, into):
+            x_turned[n] = bank(into, "x_turned%d" % n)
+            for q in four:
+                nc.tensor.transpose(x_turned[n][:, q, :], x[q][:, block(n)], ident[:])
+
+        def column_scales(blocks, sums, on_vector):
+            col_sum = sbuf("col_sum%d" % blocks[0], [P, len(blocks)], F32)
+            scale = sbuf("col_scale%d" % blocks[0], [P, len(blocks)], F32)
+            for k, n in enumerate(blocks):
+                spent = sbuf("spent%d" % n, [P, P], F32)
+                if on_vector:
+                    nc.vector.tensor_scalar(
+                        spent[:], sums[:, k, :], sv_inv_col[:, n : n + 1], None, ALU.mult, ALU.add,
+                        accum_out=col_sum[:, k : k + 1],
+                    )
+                else:
+                    nc.scalar.activation(
+                        spent[:], sums[:, k, :], ACT.Copy, scale=sv_inv_col[:, n : n + 1], accum_out=col_sum[:, k : k + 1]
+                    )
+                col_scale[n] = scale[:, k : k + 1]
+            nc.vector.reciprocal(scale[:], col_sum[:])
 
         def gradient(n, into):
             g = [sbuf("g%d_%d" % (n, w), [P, P, 2], BF16) for w in range(2)]
             x_words = flat(x_turned[n]).rearrange("j (s w e) -> j w s e", w=2, e=2)
             for w in range(2):
                 nc.vector.scalar_tensor_tensor(
-                    g[w][:], x_words[:, w], col_scale[n], y_term[n][:, w], ALU.mult, ALU.subtract
+                    g[w][:], x_words[:, w], col_scale[n], y_terms[:, n, w], ALU.mult, ALU.subtract
                 )
             g_along_i[n] = lay_words("g%d" % n, turn_words("g%d" % n, [flat(t).bitcast(F32) for t in g], into))
 
         def quantise_gradient(n):
-            cols = slice(PAD + n * P, PAD + (n + 1) * P)
-            nc.vector.quantize_mx(g_codes[:, cols].bitcast(E5M2), g_scales[:, cols], flat(g_along_i[n]))
+            nc.vector.quantize_mx(g_codes[:, block(n)].bitcast(E5M2), g_scales[:, block(n)], flat(g_along_i[n]))
 
-        def product(t, n, cols):
-            acc = bank(n, "dv%d_%d" % (t, cols.start))
+        def product(acc, t, cols):
             nc.tensor.matmul_mx(
-                flat(acc), lhsT=ui[t][0].bitcast(E4M3), lhsT_scale=ui[t][1],
+                acc, lhsT=ui[t][0], lhsT_scale=ui[t][1],
                 rhs=g_codes[:, cols].bitcast(E5M2), rhs_scale=g_scales[:, cols], start=True, stop=True,
             )
-            return flat(acc)
 
-        def place(t, part, sums):
-            dv = sbuf("dv_sb%d_%d" % (t, part.start), [P, part.stop - part.start], F32)
-            nc.scalar.copy(dv[:], sums)
-            target = window[t]
-            listed = target[:].indirect(j_list[:, part.start // 16 : part.stop // 16])
-            if part.stop - part.start == P:
-                nc.vector.tensor_tensor(listed, dv[:], zeros[:], ALU.add)
-            else:
-                nc.vector.tensor_copy(listed, dv[:])
+        def leave(name, acc, copy, over=None):
+            dv = sbuf(name, [P, acc.shape[1]], F32, over)
+            copy(dv[:], acc)
+            return dv
 
-        turn_x(0)
-        column_sum(0)
-        column_scale(0)
-        column_sum(1)
-        lay_y_term(2)
-        turn_x(1)
+        def first_window(n, dv):
+            nc.vector.tensor_tensor(window[0][:].indirect(entries(j_list, block(n))), dv, zeros[:], ALU.add)
+
+        def first_plane(n, into, over=None):
+            acc = flat(bank(into, "dv0_%d" % n, 1))
+            product(acc, 0, block(n))
+            first_window(n, leave("dv0_sb%d" % n, acc, nc.scalar.copy, over)[:])
+
+        def scatter_on_scalar(t, h, dv):
+            nc.scalar.activation(window[t][:].indirect(entries(j_list, halves[h])), dv, ACT.Copy)
+
+        sums0 = turn_sums((0,), 0)
+        sums1 = turn_sums((1,), 1)
+        turn_x(0, 2)
+        sums23 = turn_sums((2, 3), 4)
+        column_scales((0,), sums0, True)
+        quantise_ui(3, "row_sum3")
+        column_scales((1,), sums1, True)
+        column_scales((2, 3), sums23, False)
         gradient(0, 0)
-        for q in (1, 3):
-            add_tile(q, halves[1])
-            turn_sums(q, 2)
-        for q in four:
-            x[q].append(sbuf("x_late%d" % q, [P, HALF], F32)[:])
-            nc.vector.tensor_scalar(x[q][1], e[q][:, halves[1]], row_inv[q], su_col[:, q : q + 1], ALU.mult, ALU.mult)
-        last_y_term = sbuf("last_y_term", [P, PACK, P], F32, "row_inv_all")
-        nc.gpsimd.tensor_tensor(last_y_term[:], y_sb[:, :, block(3)], last_factor[:], ALU.mult)
-        turn_x(3)
-        turn_x(2)
-        column_scale(1)
-        gradient(1, 7)
-        column_sum(3)
-        column_sum(2)
-        column_scale(2)
+        turn_x(1, 3)
+        gradient(1, 1)
+        turn_x(2, 5)
+        turn_x(3, 6)
         quantise_gradient(0)
-        early = [product(0, 2, slice(0, SLOTS))]
-        scaled = sbuf("scaled", [P, PACK, P], F32)
-        nc.scalar.activation(scaled[:], flat(x_turned[3]).rearrange("j (s r) -> j r s", r=PACK), ACT.Copy, scale=col_scale[3])
-        gradient(2, 1)
-        last_back = bank(6, "last_back")
-        for r in four:
-            nc.tensor.transpose(last_back[:, r, :], scaled[:, r, :], ident[:])
+        gradient(2, 7)
+        gradient(3, 4)
         quantise_gradient(1)
-        g_along_i[3] = sbuf("g3_along_i", [P, P, PACK], BF16)
-        nc.vector.tensor_tensor(
-            g_along_i[3][:], last_back[:].rearrange("s r j -> s j r"), last_y_term[:].rearrange("s r j -> s j r"), ALU.subtract
-        )
-        early.append(product(1, 4, slice(P, P + SLOTS)))
+        first_plane(0, 2)
         quantise_gradient(2)
         quantise_gradient(3)
-        quantise_ui(2, "e3")
-        quantise_ui(3, None)
+        first_plane(1, 3, "g3_1")
 
-        place(0, block(0), early[0][:, PAD:])
-        place(1, halves[0], early[1][:, HALF:])
-        left = [slice(P, SLOTS), halves[1], slice(0, SLOTS), slice(0, SLOTS)]
-        for t in four:
-            whole = product(t, (0, 7, 3, 5)[t], slice(PAD, PAD + SLOTS))
-            place(t, left[t], whole[:, left[t]])
+        def scatter_on_vector(t, part, dv):
+            nc.vector.tensor_copy(window[t][:].indirect(entries(j_list, part)), dv)
+
+        def store(t):
             nc.sync.dma_start(out_rows[:, t, :], window[t][:])
+
+        shared = flat(bank(5, "dv_shared"))
+        product(shared[:, halves[0]], 1, halves[0])
+        product(shared[:, halves[1]], 0, halves[1])
+        dv0_late = leave("dv0_late", shared[:, halves[1]], nc.scalar.copy)
+        dv1_early = leave("dv1_early", shared[:, halves[0]], nc.scalar.copy)
+        acc = flat(bank(0, "dv1_late", 2))
+        product(acc, 1, halves[1])
+        dv1_late = leave("dv1_late_sb", acc, nc.vector.tensor_copy)
+        scatter_on_vector(0, halves[1], dv0_late[:])
+        store(0)
+        scatter_on_scalar(1, 0, dv1_early[:])
+        scatter_on_vector(1, halves[1], dv1_late[:])
+        store(1)
+
+        acc = flat(bank(6, "dv2"))
+        product(acc, 2, whole)
+        dv2 = [leave("dv2_sb%d" % h, acc[:, halves[h]], nc.scalar.copy, (None, "dv1_early")[h]) for h in range(2)]
+        for h in range(2):
+            scatter_on_scalar(2, h, dv2[h][:])
+        store(2)
+
+        acc = flat(bank(7, "dv3"))
+        product(acc, 3, whole)
+        dv3 = leave("dv3_sb", acc, nc.vector.tensor_copy, "dv1_late_sb")
+        scatter_on_vector(3, whole, dv3[:])
+        store(3)

@@ -90,8 +90,8 @@ def tile_attend_gsink_v_kernel(tc, uT, vT, su, sv, y, offs, qoffs, out):
 
         su_row = sbuf("su_row", [P, SLOTS], F32)
         sv_row = sbuf("sv_row", [P, SLOTS], F32)
-        nc.scalar.activation(sv_row[:], sv_pool[:].indirect(j_list[:]), ACT.Copy)
-        nc.scalar.activation(su_row[:], su_pool[:].indirect(i_list[:]), ACT.Copy)
+        nc.vector.tensor_copy(sv_row[:], sv_pool[:].indirect(j_list[:]))
+        nc.vector.tensor_copy(su_row[:], su_pool[:].indirect(i_list[:]))
 
         def as_columns(name, n, rows):
             turned = bank(n, name + "_turned")
@@ -111,10 +111,13 @@ def tile_attend_gsink_v_kernel(tc, uT, vT, su, sv, y, offs, qoffs, out):
         nc.scalar.copy(sv_all[:], flat(sv_spread))
 
         v_along_d = sbuf("v_along_d", [P, SLOTS, PACK], BF16)
+        v_pairs = sbuf("v_pairs", [P, 2, SLOTS, 2], BF16)
         for t in four:
-            nc.vector.tensor_copy(v_along_d[:, :, t], v_pool[t // 2][:, t % 2, :].indirect(j_list[:]))
-        v_codes, v_scales = operand("v", SLOTS)
-        nc.vector.quantize_mx(v_codes[:].bitcast(E4M3), v_scales[:], flat(v_along_d))
+            nc.vector.tensor_copy(v_pairs[:, t // 2, :, t % 2], v_pool[t // 2][:, t % 2, :].indirect(j_list[:]))
+        nc.scalar.copy(
+            flat(v_along_d).bitcast(U32).rearrange("p (j h) -> p j h", h=2),
+            v_pairs[:].rearrange("p h j e -> p (h j e)").bitcast(U32).rearrange("p (h j) -> p j h", h=2),
+        )
         sv_inv = sbuf("sv_inv", [P, PACK], F32)
         sv_inv_col = sbuf("sv_inv_col", [P, PACK], F32)
         nc.vector.reciprocal(sv_inv[:], sv_col[:])
@@ -163,6 +166,9 @@ def tile_attend_gsink_v_kernel(tc, uT, vT, su, sv, y, offs, qoffs, out):
             if t > 0:
                 quantise_ui(t - 1, "u_pool%d" % t)
 
+        v_codes, v_scales = operand("v", SLOTS, "u_pool0")
+        nc.vector.quantize_mx(v_codes[:].bitcast(E4M3), v_scales[:], flat(v_along_d))
+
         ud = [operand("ud%d" % q, P) for q in four]
         scores = []
 
@@ -176,23 +182,20 @@ def tile_attend_gsink_v_kernel(tc, uT, vT, su, sv, y, offs, qoffs, out):
             )
             scores.append(a)
 
-        for q in range(2):
-            nc.vector.tensor_copy(u_plane[3][:, block(q)], u_listed(3, block(q)))
-        nc.scalar.activation(u_plane[3][:, halves[1]], u_listed(3, halves[1]), ACT.Copy)
         for q in four:
-            weave(nc.vector.tensor_copy if q < 2 else nc.scalar.copy, 1, q)
+            nc.vector.tensor_copy(u_plane[3][:, block(q)], u_listed(3, block(q)))
+            weave(nc.scalar.copy, 1, q)
         for q in four:
             score(q)
-        turn_u(3, 7)
-        quantise_ui(2, "u_along_d3")
 
         z = [sbuf("z%d" % q, [P, SLOTS], F32) for q in four]
         e = [sbuf("e%d" % q, [P, SLOTS], F32) for q in four]
         f = [sbuf("f%d" % q, [P, SLOTS], F32) for q in four]
-        x = [sbuf("x%d" % q, [P, SLOTS], F32) for q in four]
+        x = [sbuf("x%d" % q, [P, HALF], F32) for q in four]
         neg_shift = [sbuf("neg_shift%d" % q, [P, 1], F32) for q in four]
         row_sum = [sbuf("row_sum%d" % q, [P, 1], F32) for q in four]
-        row_inv = [sbuf("row_inv%d" % q, [P, 1], F32) for q in four]
+        row_invs = sbuf("row_invs", [P, PACK], F32)
+        row_inv = [row_invs[:, q : q + 1] for q in four]
 
         for q in four:
             nc.vector.scalar_tensor_tensor(z[q][:], flat(scores[q]), su_col[:, q : q + 1], sv_all[:], ALU.mult, ALU.mult)
@@ -210,7 +213,7 @@ def tile_attend_gsink_v_kernel(tc, uT, vT, su, sv, y, offs, qoffs, out):
         for q in four:
             nc.scalar.activation(e[q][:], z[q][:], ACT.Exp, bias=neg_shift[q][:], accum_out=row_sum[q][:])
 
-        y_scaled = sbuf("y_scaled", [P, PACK, SLOTS], F32)
+        y_scaled = sbuf("y_scaled", [P, PACK, SLOTS], F32, "u_along_d3")
         y_turned = [bank(4 + n, "y_turned%d" % n) for n in four]
         for r in four:
             nc.gpsimd.tensor_scalar(y_scaled[:, r, :], y_sb[:, r, :], su_dealt[:, r : r + 1], 0.0, ALU.mult, ALU.add)
@@ -218,38 +221,53 @@ def tile_attend_gsink_v_kernel(tc, uT, vT, su, sv, y, offs, qoffs, out):
                 nc.tensor.transpose(y_turned[n][:, r, :], y_scaled[:, r, block(n)], ident[:])
 
         def normalise(q, cols):
-            nc.vector.tensor_scalar(f[q][:, cols], e[q][:, cols], row_inv[q][:], None, ALU.mult)
-            nc.vector.tensor_scalar(x[q][:, cols], e[q][:, cols], row_inv[q][:], su_col[:, q : q + 1], ALU.mult, ALU.mult)
+            nc.vector.tensor_scalar(f[q][:, cols], e[q][:, cols], row_inv[q], None, ALU.mult)
+
+        def add_tile(q, cols):
+            nc.vector.scalar_tensor_tensor(f[q][:, cols], e[q][:, cols], row_inv[q], f[q - 1][:, cols], ALU.mult, ALU.add)
 
         for q in four:
-            nc.vector.reciprocal(row_inv[q][:], row_sum[q][:])
-            normalise(q, whole if q < PACK - 1 else block(0))
-        normalise(PACK - 1, slice(P, SLOTS))
+            nc.vector.reciprocal(row_inv[q], row_sum[q][:])
+            normalise(q, halves[0])
+            nc.vector.tensor_scalar(x[q][:], e[q][:, halves[0]], row_inv[q], su_col[:, q : q + 1], ALU.mult, ALU.mult)
+        normalise(0, halves[1])
+        for q in range(1, PACK):
+            add_tile(q, halves[1])
+        row_weight = sbuf("row_weight", [P, PACK], F32)
+        nc.vector.tensor_tensor(row_weight[:], row_invs[:], su_col[:], ALU.mult)
 
         y_terms = sbuf("y_terms", [P, PACK, 2, P, 2], F32, "z3")
-        for n in four:
+        x_late = sbuf("x_late", [P, PACK, HALF], F32)
+
+        def lay_y_term(n):
             dealt = y_turned[n][:].rearrange("j (w e) s -> j w s e", w=2)
             nc.scalar.activation(y_terms[:, n], dealt, ACT.Copy, scale=sv_col[:, n : n + 1])
+
+        lay_y_term(0)
+        lay_y_term(1)
+        for q in four:
+            nc.scalar.activation(x_late[:, q, :], e[q][:, halves[1]], ACT.Copy, scale=row_weight[:, q : q + 1])
+        lay_y_term(2)
 
         col_scale = {}
         x_turned = {}
         g_along_i = {}
         g_codes, g_scales = operand("g", SLOTS)
 
-        def turn_sums(blocks, into):
+        def turn_sums(blocks, into, tiles=four):
             sums = bank(into, "sums%d" % blocks[0], len(blocks))
             for k, n in enumerate(blocks):
-                for q in four:
+                for q in tiles:
                     nc.tensor.matmul(
                         sums[:, k, :], f[q][:, block(n)], ident[:],
-                        start=q == 0 and k == 0, stop=q == PACK - 1 and n == blocks[-1], is_transpose=True,
+                        start=q == tiles[0] and k == 0, stop=q == PACK - 1 and n == blocks[-1], is_transpose=True,
                     )
             return sums
 
         def turn_x(n, into):
             x_turned[n] = bank(into, "x_turned%d" % n)
             for q in four:
-                nc.tensor.transpose(x_turned[n][:, q, :], x[q][:, block(n)], ident[:])
+                nc.tensor.transpose(x_turned[n][:, q, :], (x[q][:], x_late[:, q, :])[n // 2][:, block(n % 2)], ident[:])
 
         def column_scales(blocks, sums, on_vector):
             col_sum = sbuf("col_sum%d" % blocks[0], [P, len(blocks)], F32)
@@ -302,15 +320,27 @@ def tile_attend_gsink_v_kernel(tc, uT, vT, su, sv, y, offs, qoffs, out):
         def scatter_on_scalar(t, h, dv):
             nc.scalar.activation(window[t][:].indirect(entries(j_list, halves[h])), dv, ACT.Copy)
 
+        def scatter_on_vector(t, part, dv):
+            nc.vector.tensor_copy(window[t][:].indirect(entries(j_list, part)), dv)
+
+        def store(t):
+            nc.sync.dma_start(out_rows[:, t, :], window[t][:])
+
+        def half_product(t, h, into):
+            acc = flat(bank(into, "dv%d_half%d" % (t, h), 2))
+            product(acc, t, halves[h])
+            return acc
+
         sums0 = turn_sums((0,), 0)
         sums1 = turn_sums((1,), 1)
         turn_x(0, 2)
-        sums23 = turn_sums((2, 3), 4)
+        sums23 = turn_sums((2, 3), 4, (PACK - 1,))
         column_scales((0,), sums0, True)
-        quantise_ui(3, "row_sum3")
+        quantise_ui(2, "row_sum3")
         column_scales((1,), sums1, True)
         column_scales((2, 3), sums23, False)
         gradient(0, 0)
+        lay_y_term(3)
         turn_x(1, 3)
         gradient(1, 1)
         turn_x(2, 5)
@@ -320,39 +350,25 @@ def tile_attend_gsink_v_kernel(tc, uT, vT, su, sv, y, offs, qoffs, out):
         gradient(3, 4)
         quantise_gradient(1)
         first_plane(0, 2)
+        turn_u(3, 2)
         quantise_gradient(2)
         quantise_gradient(3)
         first_plane(1, 3, "g3_1")
 
-        def scatter_on_vector(t, part, dv):
-            nc.vector.tensor_copy(window[t][:].indirect(entries(j_list, part)), dv)
-
-        def store(t):
-            nc.sync.dma_start(out_rows[:, t, :], window[t][:])
-
-        shared = flat(bank(5, "dv_shared"))
-        product(shared[:, halves[0]], 1, halves[0])
-        product(shared[:, halves[1]], 0, halves[1])
-        dv0_late = leave("dv0_late", shared[:, halves[1]], nc.scalar.copy)
-        dv1_early = leave("dv1_early", shared[:, halves[0]], nc.scalar.copy)
-        acc = flat(bank(0, "dv1_late", 2))
-        product(acc, 1, halves[1])
-        dv1_late = leave("dv1_late_sb", acc, nc.vector.tensor_copy)
-        scatter_on_vector(0, halves[1], dv0_late[:])
+        early = {1: leave("dv1_early", half_product(1, 0, 0), nc.scalar.copy, "g3_0")}
+        scatter_on_scalar(1, 0, early[1][:])
+        late = {t: leave("dv%d_late" % t, half_product(t, 1, (5, 1)[t]), nc.vector.tensor_copy) for t in range(2)}
+        scatter_on_vector(0, halves[1], late[0][:])
         store(0)
-        scatter_on_scalar(1, 0, dv1_early[:])
-        scatter_on_vector(1, halves[1], dv1_late[:])
+        quantise_ui(3, "g3_1")
+        scatter_on_vector(1, halves[1], late[1][:])
         store(1)
-
-        acc = flat(bank(6, "dv2"))
-        product(acc, 2, whole)
-        dv2 = [leave("dv2_sb%d" % h, acc[:, halves[h]], nc.scalar.copy, (None, "dv1_early")[h]) for h in range(2)]
-        for h in range(2):
-            scatter_on_scalar(2, h, dv2[h][:])
-        store(2)
-
-        acc = flat(bank(7, "dv3"))
-        product(acc, 3, whole)
-        dv3 = leave("dv3_sb", acc, nc.vector.tensor_copy, "dv1_late_sb")
-        scatter_on_vector(3, whole, dv3[:])
-        store(3)
+        whole_product = {t: flat(bank(4 + t, "dv%d" % t)) for t in (2, 3)}
+        for t in (2, 3):
+            product(whole_product[t], t, whole)
+            early[t] = leave("dv%d_early" % t, whole_product[t][:, halves[0]], nc.scalar.copy, ("g3_0", "g2_0")[t - 2])
+        for t in (2, 3):
+            scatter_on_scalar(t, 0, early[t][:])
+            late[t] = leave("dv%d_late" % t, whole_product[t][:, halves[1]], nc.vector.tensor_copy, "dv%d_late" % (t - 2))
+            scatter_on_vector(t, halves[1], late[t][:])
+            store(t)

@@ -68,13 +68,16 @@ def tile_attend_gsink_v_kernel(tc, uT, vT, su, sv, y, offs, qoffs, out):
         v_rows = vT.rearrange("(p t) c -> p t c", t=PACK)
         out_rows = out.rearrange("(p t) c -> p t c", t=PACK)
         u_pool = [sbuf("u_pool%d" % t, [P, POOL], F32) for t in four]
-        v_pool = [sbuf("v_pool%d" % h, [P, 2, POOL], F32) for h in range(2)]
+        v_first = [sbuf("v_first%d" % t, [P, POOL], F32) for t in range(2)]
+        v_last = sbuf("v_last", [P, 2, POOL], F32)
+        v_plane = [v_first[0][:], v_first[1][:], v_last[:, 0, :], v_last[:, 1, :]]
+        nc.sync.dma_start(v_plane[0], v_rows[:, 0, :])
         nc.sync.dma_start(j_list[:], qoffs)
         nc.sync.dma_start(i_list[:], offs)
         nc.scalar.dma_start(sv_pool[P - 1 : P, :], sv[0:1, :])
         nc.scalar.dma_start(su_pool[P - 1 : P, :], su[0:1, :])
-        for h in range(2):
-            nc.sync.dma_start(v_pool[h][:], v_rows[:, 2 * h : 2 * h + 2, :])
+        nc.sync.dma_start(v_plane[1], v_rows[:, 1, :])
+        nc.sync.dma_start(v_last[:], v_rows[:, 2:PACK, :])
         for t in four:
             nc.sync.dma_start(u_pool[t][:], u_rows[:, t, :])
         y_sb = sbuf("y_sb", [P, PACK, SLOTS], F32)
@@ -113,7 +116,7 @@ def tile_attend_gsink_v_kernel(tc, uT, vT, su, sv, y, offs, qoffs, out):
         v_along_d = sbuf("v_along_d", [P, SLOTS, PACK], BF16)
         v_pairs = sbuf("v_pairs", [P, 2, SLOTS, 2], BF16)
         for t in four:
-            nc.vector.tensor_copy(v_pairs[:, t // 2, :, t % 2], v_pool[t // 2][:, t % 2, :].indirect(j_list[:]))
+            nc.vector.tensor_copy(v_pairs[:, t // 2, :, t % 2], v_plane[t].indirect(j_list[:]))
         nc.scalar.copy(
             flat(v_along_d).bitcast(U32).rearrange("p (j h) -> p j h", h=2),
             v_pairs[:].rearrange("p h j e -> p (h j e)").bitcast(U32).rearrange("p (h j) -> p j h", h=2),
@@ -175,16 +178,22 @@ def tile_attend_gsink_v_kernel(tc, uT, vT, su, sv, y, offs, qoffs, out):
         def score(q):
             codes, scales = ud[q]
             nc.vector.quantize_mx(codes[:].bitcast(E4M3), scales[:], flat(u_along_d[q]))
-            a = bank(q, "scores%d" % q)
-            nc.tensor.matmul_mx(
-                flat(a), lhsT=codes[:].bitcast(E4M3), lhsT_scale=scales[:],
-                rhs=v_codes[:].bitcast(E4M3), rhs_scale=v_scales[:], start=True, stop=True,
-            )
-            scores.append(a)
+            parts = []
+            for cols, into in ((whole, q),) if q > 0 else zip(halves, (0, 4)):
+                a = flat(bank(into, "scores%d_%d" % (q, cols.start), (cols.stop - cols.start) // P))
+                nc.tensor.matmul_mx(
+                    a, lhsT=codes[:].bitcast(E4M3), lhsT_scale=scales[:],
+                    rhs=v_codes[:, cols].bitcast(E4M3), rhs_scale=v_scales[:, cols], start=True, stop=True,
+                )
+                parts.append((cols, a))
+            scores.append(parts)
 
-        for q in four:
+        for q in range(2):
             nc.vector.tensor_copy(u_plane[3][:, block(q)], u_listed(3, block(q)))
-            weave(nc.scalar.copy, 1, q)
+        for q in range(2, PACK):
+            nc.scalar.activation(u_plane[3][:, block(q)], u_listed(3, block(q)), ACT.Copy)
+        for q in four:
+            weave(nc.vector.tensor_copy if q < 2 else nc.scalar.copy, 1, q)
         for q in four:
             score(q)
 
@@ -198,7 +207,8 @@ def tile_attend_gsink_v_kernel(tc, uT, vT, su, sv, y, offs, qoffs, out):
         row_inv = [row_invs[:, q : q + 1] for q in four]
 
         for q in four:
-            nc.vector.scalar_tensor_tensor(z[q][:], flat(scores[q]), su_col[:, q : q + 1], sv_all[:], ALU.mult, ALU.mult)
+            for cols, a in scores[q]:
+                nc.vector.scalar_tensor_tensor(z[q][:, cols], a, su_col[:, q : q + 1], sv_all[:, cols], ALU.mult, ALU.mult)
             if q < SOFT_TILES:
                 soft_sum = sbuf("soft_sum%d" % q, [P, 1], F32)
                 slope = sbuf("slope%d" % q, [P, 1], F32)
@@ -355,7 +365,7 @@ def tile_attend_gsink_v_kernel(tc, uT, vT, su, sv, y, offs, qoffs, out):
         quantise_gradient(3)
         first_plane(1, 3, "g3_1")
 
-        early = {1: leave("dv1_early", half_product(1, 0, 0), nc.scalar.copy, "g3_0")}
+        early = {1: leave("dv1_early", half_product(1, 0, 4), nc.scalar.copy)}
         scatter_on_scalar(1, 0, early[1][:])
         late = {t: leave("dv%d_late" % t, half_product(t, 1, (5, 1)[t]), nc.vector.tensor_copy) for t in range(2)}
         scatter_on_vector(0, halves[1], late[0][:])
@@ -364,11 +374,13 @@ def tile_attend_gsink_v_kernel(tc, uT, vT, su, sv, y, offs, qoffs, out):
         scatter_on_vector(1, halves[1], late[1][:])
         store(1)
         whole_product = {t: flat(bank(4 + t, "dv%d" % t)) for t in (2, 3)}
+        last_early = sbuf("last_early", [P, 2, HALF], F32, "dv1_early")
         for t in (2, 3):
             product(whole_product[t], t, whole)
-            early[t] = leave("dv%d_early" % t, whole_product[t][:, halves[0]], nc.scalar.copy, ("g3_0", "g2_0")[t - 2])
+            early[t] = last_early[:, t - 2, :]
+            nc.scalar.copy(early[t], whole_product[t][:, halves[0]])
         for t in (2, 3):
-            scatter_on_scalar(t, 0, early[t][:])
+            scatter_on_scalar(t, 0, early[t])
             late[t] = leave("dv%d_late" % t, whole_product[t][:, halves[1]], nc.vector.tensor_copy, "dv%d_late" % (t - 2))
             scatter_on_vector(t, halves[1], late[t][:])
             store(t)

@@ -23,7 +23,7 @@ HALF = SLOTS // 2
 POOL = 2048
 FEATURES = 512
 SOFTEN = 8.0
-SOFT_TILES = 3
+SOFT_TILES = 2
 LARGE = 2.0**100
 
 FLOPS = 2 * 2 * SLOTS * SLOTS * FEATURES
@@ -211,12 +211,10 @@ def tile_attend_gsink_v_kernel(tc, uT, vT, su, sv, y, offs, qoffs, out):
                 nc.vector.scalar_tensor_tensor(z[q][:, cols], a, su_col[:, q : q + 1], sv_all[:, cols], ALU.mult, ALU.mult)
             if q < SOFT_TILES:
                 soft_sum = sbuf("soft_sum%d" % q, [P, 1], F32)
-                slope = sbuf("slope%d" % q, [P, 1], F32)
                 per_bit = SOFTEN * math.log(2.0)
                 nc.scalar.activation(e[q][:], z[q][:], ACT.Exp, scale=1.0 / SOFTEN, accum_out=soft_sum[:])
                 nc.vector.tensor_scalar(
-                    slope[:], soft_sum[:].bitcast(I32), -per_bit / 2.0**23, per_bit * (127 + 9), ALU.mult, ALU.add,
-                    accum_out=neg_shift[q][:],
+                    neg_shift[q][:], soft_sum[:].bitcast(I32), -per_bit / 2.0**23, per_bit * (127 + 9), ALU.mult, ALU.add
                 )
             else:
                 nc.vector.tensor_reduce(neg_shift[q][:], z[q][:], AXIS.X, ALU.max, negate=True)

import math
from contextlib import ExitStack

import concourse.mybir as mybir
from concourse.masks import make_identity

F32 = mybir.dt.float32
BF16 = mybir.dt.bfloat16
U32 = mybir.dt.uint32
I32 = mybir.dt.int32
U16 = mybir.dt.uint16
U8 = mybir.dt.uint8
E4M3 = mybir.dt.float8_e4m3fn_x4
E5M2 = mybir.dt.float8_e5m2_x4
ALU = mybir.AluOpType
ACT = mybir.ActivationFunctionType
AXIS = mybir.AxisListType

P = 128
PACK = 4
SLOTS = 512
HALF = SLOTS // 2
POOL = 2048
FEATURES = 512
SOFTEN = 8.0
SOFT_TILES = 2
LARGE = 2.0**100

FLOPS = 2 * 2 * SLOTS * SLOTS * FEATURES
BYTES = 4 * (3 * FEATURES * POOL + SLOTS * SLOTS + 2 * POOL) + 2 * 2 * P * (SLOTS // 16)


def tile_attend_gsink_v_kernel(tc, uT, vT, su, sv, y, offs, qoffs, out):
    nc = tc.nc
    four = range(PACK)
    whole = slice(0, SLOTS)
    halves = (slice(0, HALF), slice(HALF, SLOTS))

    def block(n):
        return slice(n * P, (n + 1) * P)

    def flat(t):
        return t[:].rearrange("p a b -> p (a b)")

    def entries(listed, part):
        return listed[:, part.start // 16 : part.stop // 16]

    with ExitStack() as ctx:
        sb = ctx.enter_context(tc.tile_pool(name="sb", bufs=1))
        ps = ctx.enter_context(tc.psum_pool(name="ps", bufs=1))

        def sbuf(name, shape, dtype, over=None):
            return sb.tile(shape, dtype, name=name, tag=over or name, align_bytes=64)

        def bank(n, name, parts=PACK):
            return ps.tile([P, parts, P], F32, name=name, tag="bank%d" % n)

        def operand(name, width, over=None):
            return sbuf(name + "_codes", [P, width], U32, over), sbuf(name + "_scales", [P, width], U8)

        i_list = sb.tile([P, SLOTS // 16], U16, name="i_list")
        j_list = sb.tile([P, SLOTS // 16], U16, name="j_list")
        su_pool = sbuf("su_pool", [P, POOL], F32)
        sv_pool = sbuf("sv_pool", [P, POOL], F32)
        nc.vector.memset(sv_pool[0 : P - 1, :].bitcast(I32), 0)
        nc.vector.memset(su_pool[0 : P - 1, :].bitcast(I32), 0)
        u_rows = uT.rearrange("(p t) c -> p t c", t=PACK)
        v_rows = vT.rearrange("(p t) c -> p t c", t=PACK)
        out_rows = out.rearrange("(p t) c -> p t c", t=PACK)
        u_pool = [sbuf("u_pool%d" % t, [P, POOL], F32) for t in four]
        v_first = [sbuf("v_first%d" % t, [P, POOL], F32) for t in range(2)]
        v_last = sbuf("v_last", [P, 2, POOL], F32)
        v_plane = [v_first[0][:], v_first[1][:], v_last[:, 0, :], v_last[:, 1, :]]
        nc.sync.dma_start(v_plane[0], v_rows[:, 0, :])
        nc.sync.dma_start(j_list[:], qoffs)
        nc.sync.dma_start(i_list[:], offs)
        nc.scalar.dma_start(sv_pool[P - 1 : P, :], sv[0:1, :])
        nc.scalar.dma_start(su_pool[P - 1 : P, :], su[0:1, :])
        nc.sync.dma_start(v_plane[1], v_rows[:, 1, :])
        nc.sync.dma_start(v_last[:], v_rows[:, 2:PACK, :])
        for t in four:
            nc.sync.dma_start(u_pool[t][:], u_rows[:, t, :])
        y_sb = sbuf("y_sb", [P, PACK, SLOTS], F32)
        nc.sync.dma_start(y_sb[:], y.rearrange("(p r) j -> p r j", r=PACK))

        ident = sbuf("ident", [P, P], F32)
        make_identity(nc, ident[:])
        zeros = sbuf("zeros", [P, P], F32)
        nc.gpsimd.memset(zeros[:], 0.0)
        window = [sbuf("window%d" % t, [P, POOL], F32) for t in four]
        for cleared in window:
            nc.gpsimd.memset(cleared[:].bitcast(I32), 0)

        su_row = sbuf("su_row", [P, SLOTS], F32)
        sv_row = sbuf("sv_row", [P, SLOTS], F32)
        nc.vector.tensor_copy(sv_row[:], sv_pool[:].indirect(j_list[:]))
        nc.vector.tensor_copy(su_row[:], su_pool[:].indirect(i_list[:]))

        def as_columns(name, n, rows):
            turned = bank(n, name + "_turned")
            for k in four:
                nc.tensor.transpose(turned[:, k, :], rows[k], ident[:])
            columns = sbuf(name, [P, PACK], F32)
            nc.scalar.copy(columns[:], turned[:, :, P - 1])
            return columns

        sv_col = as_columns("sv_col", 4, [sv_row[:, block(n)] for n in four])
        su_col = as_columns("su_col", 5, [su_row[:, block(n)] for n in four])
        su_dealt = as_columns("su_dealt", 6, [su_row[:, r::PACK] for r in four])
        sv_spread = bank(7, "sv_spread")
        for n in four:
            nc.tensor.transpose(sv_spread[:, n, :], sv_col[:, n : n + 1].to_broadcast([P, P]), ident[:])
        sv_all = sbuf("sv_all", [P, SLOTS], F32)
        nc.scalar.copy(sv_all[:], flat(sv_spread))

        v_along_d = sbuf("v_along_d", [P, SLOTS, PACK], BF16)
        v_pairs = sbuf("v_pairs", [P, 2, SLOTS, 2], BF16)
        for t in four:
            nc.vector.tensor_copy(v_pairs[:, t // 2, :, t % 2], v_plane[t].indirect(j_list[:]))
        nc.scalar.copy(
            flat(v_along_d).bitcast(U32).rearrange("p (j h) -> p j h", h=2),
            v_pairs[:].rearrange("p h j e -> p (h j e)").bitcast(U32).rearrange("p (h j) -> p j h", h=2),
        )
        sv_inv = sbuf("sv_inv", [P, PACK], F32)
        sv_inv_col = sbuf("sv_inv_col", [P, PACK], F32)
        nc.vector.reciprocal(sv_inv[:], sv_col[:])
        nc.vector.tensor_scalar(sv_inv_col[:], sv_inv[:], LARGE, -LARGE, ALU.min, ALU.max)

        u_along_d = [sbuf("u_along_d%d" % q, [P, P, PACK], BF16) for q in four]
        u_pair = [sbuf("u_pair%d" % h, [P, 2, SLOTS], BF16) for h in range(2)]
        u_plane = [u_pair[t // 2][:, t % 2, :] for t in four]

        def u_listed(t, part):
            return u_pool[t][:].indirect(entries(i_list, part))

        def weave(copy, h, q):
            copy(u_along_d[q][:, :, 2 * h : 2 * h + 2], u_pair[h][:, :, block(q)].rearrange("p t i -> p i t"))

        def turn_words(name, rows, n):
            turned = bank(n, name + "_turned", 2)
            for w in range(2):
                nc.tensor.transpose(turned[:, w, :], rows[w], ident[:])
            return turned

        def lay_words(name, turned, over=None):
            along_i = sbuf(name + "_along_i", [P, P, PACK], BF16, over)
            words = flat(along_i).bitcast(F32).rearrange("s (x w) -> s x w", w=2)
            nc.scalar.copy(words, turned[:].rearrange("s w x -> s x w"))
            return along_i

        u_along_i = {}
        ui = {}

        def turn_u(t, n):
            rows = [u_plane[t].bitcast(F32)[:, w::2] for w in range(2)]
            u_along_i[t] = lay_words("u%d" % t, turn_words("u%d" % t, rows, n))

        def quantise_ui(t, over=None):
            codes, scales = operand("ui%d" % t, P, over)
            nc.vector.quantize_mx(codes[:].bitcast(E4M3), scales[:], flat(u_along_i[t]))
            ui[t] = (codes[:].bitcast(E4M3), scales[:])

        for t in range(PACK - 1):
            nc.vector.tensor_copy(u_plane[t], u_listed(t, whole))
            if t == 1:
                for q in four:
                    weave(nc.scalar.copy, 0, q)
            turn_u(t, t)
            if t > 0:
                quantise_ui(t - 1, "u_pool%d" % t)

        v_codes, v_scales = operand("v", SLOTS, "u_pool0")
        nc.vector.quantize_mx(v_codes[:].bitcast(E4M3), v_scales[:], flat(v_along_d))

        ud = [operand("ud%d" % q, P) for q in four]
        scores = []

        def score(q):
            codes, scales = ud[q]
            nc.vector.quantize_mx(codes[:].bitcast(E4M3), scales[:], flat(u_along_d[q]))
            parts = []
            for cols, into in ((whole, q),) if q > 0 else zip(halves, (0, 4)):
                a = flat(bank(into, "scores%d_%d" % (q, cols.start), (cols.stop - cols.start) // P))
                nc.tensor.matmul_mx(
                    a, lhsT=codes[:].bitcast(E4M3), lhsT_scale=scales[:],
                    rhs=v_codes[:, cols].bitcast(E4M3), rhs_scale=v_scales[:, cols], start=True, stop=True,
                )
                parts.append((cols, a))
            scores.append(parts)

        for q in range(2):
            nc.vector.tensor_copy(u_plane[3][:, block(q)], u_listed(3, block(q)))
        for q in range(2, PACK):
            nc.scalar.activation(u_plane[3][:, block(q)], u_listed(3, block(q)), ACT.Copy)
        for q in four:
            weave(nc.vector.tensor_copy if q < 2 else nc.scalar.copy, 1, q)
        for q in four:
            score(q)

        z = [sbuf("z%d" % q, [P, SLOTS], F32) for q in four]
        e = [sbuf("e%d" % q, [P, SLOTS], F32) for q in four]
        f = [sbuf("f%d" % q, [P, SLOTS], F32) for q in four]
        x = [sbuf("x%d" % q, [P, HALF], F32) for q in four]
        neg_shift = [sbuf("neg_shift%d" % q, [P, 1], F32) for q in four]
        row_sum = [sbuf("row_sum%d" % q, [P, 1], F32) for q in four]
        row_invs = sbuf("row_invs", [P, PACK], F32)
        row_inv = [row_invs[:, q : q + 1] for q in four]

        for q in four:
            for cols, a in scores[q]:
                nc.vector.scalar_tensor_tensor(z[q][:, cols], a, su_col[:, q : q + 1], sv_all[:, cols], ALU.mult, ALU.mult)
            if q < SOFT_TILES:
                soft_sum = sbuf("soft_sum%d" % q, [P, 1], F32)
                per_bit = SOFTEN * math.log(2.0)
                nc.scalar.activation(e[q][:], z[q][:], ACT.Exp, scale=1.0 / SOFTEN, accum_out=soft_sum[:])
                nc.vector.tensor_scalar(
                    neg_shift[q][:], soft_sum[:].bitcast(I32), -per_bit / 2.0**23, per_bit * (127 + 9), ALU.mult, ALU.add
                )
            else:
                nc.vector.tensor_reduce(neg_shift[q][:], z[q][:], AXIS.X, ALU.max, negate=True)
        for q in four:
            nc.scalar.activation(e[q][:], z[q][:], ACT.Exp, bias=neg_shift[q][:], accum_out=row_sum[q][:])

        y_scaled = sbuf("y_scaled", [P, PACK, SLOTS], F32, "u_along_d3")
        y_turned = [bank(4 + n, "y_turned%d" % n) for n in four]
        for r in four:
            nc.gpsimd.tensor_scalar(y_scaled[:, r, :], y_sb[:, r, :], su_dealt[:, r : r + 1], 0.0, ALU.mult, ALU.add)
            for n in four:
                nc.tensor.transpose(y_turned[n][:, r, :], y_scaled[:, r, block(n)], ident[:])

        def normalise(q, cols):
            nc.vector.tensor_scalar(f[q][:, cols], e[q][:, cols], row_inv[q], None, ALU.mult)

        def add_tile(q, cols):
            nc.vector.scalar_tensor_tensor(f[q][:, cols], e[q][:, cols], row_inv[q], f[q - 1][:, cols], ALU.mult, ALU.add)

        for q in four:
            nc.vector.reciprocal(row_inv[q], row_sum[q][:])
            normalise(q, halves[0])
            nc.vector.tensor_scalar(x[q][:], e[q][:, halves[0]], row_inv[q], su_col[:, q : q + 1], ALU.mult, ALU.mult)
        normalise(0, halves[1])
        for q in range(1, PACK):
            add_tile(q, halves[1])
        row_weight = sbuf("row_weight", [P, PACK], F32)
        nc.vector.tensor_tensor(row_weight[:], row_invs[:], su_col[:], ALU.mult)

        y_terms = sbuf("y_terms", [P, PACK, 2, P, 2], F32, "z3")
        x_late = sbuf("x_late", [P, PACK, HALF], F32)

        def lay_y_term(n):
            dealt = y_turned[n][:].rearrange("j (w e) s -> j w s e", w=2)
            nc.scalar.activation(y_terms[:, n], dealt, ACT.Copy, scale=sv_col[:, n : n + 1])

        lay_y_term(0)
        lay_y_term(1)
        for q in four:
            nc.scalar.activation(x_late[:, q, :], e[q][:, halves[1]], ACT.Copy, scale=row_weight[:, q : q + 1])
        lay_y_term(2)

        col_scale = {}
        x_turned = {}
        g_along_i = {}
        g_codes, g_scales = operand("g", SLOTS)

        def turn_sums(blocks, into, tiles=four):
            sums = bank(into, "sums%d" % blocks[0], len(blocks))
            for k, n in enumerate(blocks):
                for q in tiles:
                    nc.tensor.matmul(
                        sums[:, k, :], f[q][:, block(n)], ident[:],
                        start=q == tiles[0] and k == 0, stop=q == PACK - 1 and n == blocks[-1], is_transpose=True,
                    )
            return sums

        def turn_x(n, into):
            x_turned[n] = bank(into, "x_turned%d" % n)
            for q in four:
                nc.tensor.transpose(x_turned[n][:, q, :], (x[q][:], x_late[:, q, :])[n // 2][:, block(n % 2)], ident[:])

        def column_scales(blocks, sums, on_vector):
            col_sum = sbuf("col_sum%d" % blocks[0], [P, len(blocks)], F32)
            scale = sbuf("col_scale%d" % blocks[0], [P, len(blocks)], F32)
            for k, n in enumerate(blocks):
                spent = sbuf("spent%d" % n, [P, P], F32)
                if on_vector:
                    nc.vector.tensor_scalar(
                        spent[:], sums[:, k, :], sv_inv_col[:, n : n + 1], None, ALU.mult, ALU.add,
                        accum_out=col_sum[:, k : k + 1],
                    )
                else:
                    nc.scalar.activation(
                        spent[:], sums[:, k, :], ACT.Copy, scale=sv_inv_col[:, n : n + 1], accum_out=col_sum[:, k : k + 1]
                    )
                col_scale[n] = scale[:, k : k + 1]
            nc.vector.reciprocal(scale[:], col_sum[:])

        def gradient(n, into):
            g = [sbuf("g%d_%d" % (n, w), [P, P, 2], BF16) for w in range(2)]
            x_words = flat(x_turned[n]).rearrange("j (s w e) -> j w s e", w=2, e=2)
            for w in range(2):
                nc.vector.scalar_tensor_tensor(
                    g[w][:], x_words[:, w], col_scale[n], y_terms[:, n, w], ALU.mult, ALU.subtract
                )
            g_along_i[n] = lay_words("g%d" % n, turn_words("g%d" % n, [flat(t).bitcast(F32) for t in g], into))

        def quantise_gradient(n):
            nc.vector.quantize_mx(g_codes[:, block(n)].bitcast(E5M2), g_scales[:, block(n)], flat(g_along_i[n]))

        def product(acc, t, cols):
            nc.tensor.matmul_mx(
                acc, lhsT=ui[t][0], lhsT_scale=ui[t][1],
                rhs=g_codes[:, cols].bitcast(E5M2), rhs_scale=g_scales[:, cols], start=True, stop=True,
            )

        def leave(name, acc, copy, over=None):
            dv = sbuf(name, [P, acc.shape[1]], F32, over)
            copy(dv[:], acc)
            return dv

        def first_window(n, dv):
            nc.vector.tensor_tensor(window[0][:].indirect(entries(j_list, block(n))), dv, zeros[:], ALU.add)

        def first_plane(n, into, over=None):
            acc = flat(bank(into, "dv0_%d" % n, 1))
            product(acc, 0, block(n))
            first_window(n, leave("dv0_sb%d" % n, acc, nc.scalar.copy, over)[:])

        def scatter_on_scalar(t, h, dv):
            nc.scalar.activation(window[t][:].indirect(entries(j_list, halves[h])), dv, ACT.Copy)

        def scatter_on_vector(t, part, dv):
            nc.vector.tensor_copy(window[t][:].indirect(entries(j_list, part)), dv)

        def store(t):
            nc.sync.dma_start(out_rows[:, t, :], window[t][:])

        def half_product(t, h, into):
            acc = flat(bank(into, "dv%d_half%d" % (t, h), 2))
            product(acc, t, halves[h])
            return acc

        sums0 = turn_sums((0,), 0)
        sums1 = turn_sums((1,), 1)
        turn_x(0, 2)
        sums23 = turn_sums((2, 3), 4, (PACK - 1,))
        column_scales((0,), sums0, True)
        quantise_ui(2, "row_sum3")
        column_scales((1,), sums1, True)
        column_scales((2, 3), sums23, False)
        gradient(0, 0)
        lay_y_term(3)
        turn_x(1, 3)
        gradient(1, 1)
        turn_x(2, 5)
        turn_x(3, 6)
        quantise_gradient(0)
        gradient(2, 7)
        gradient(3, 4)
        quantise_gradient(1)
        first_plane(0, 2)
        turn_u(3, 2)
        quantise_gradient(2)
        quantise_gradient(3)
        first_plane(1, 3, "g3_1")

        early = {1: leave("dv1_early", half_product(1, 0, 4), nc.scalar.copy)}
        scatter_on_scalar(1, 0, early[1][:])
        late = {t: leave("dv%d_late" % t, half_product(t, 1, (5, 1)[t]), nc.vector.tensor_copy) for t in range(2)}
        scatter_on_vector(0, halves[1], late[0][:])
        store(0)
        quantise_ui(3, "g3_1")
        scatter_on_vector(1, halves[1], late[1][:])
        store(1)
        whole_product = {t: flat(bank(4 + t, "dv%d" % t)) for t in (2, 3)}
        last_early = sbuf("last_early", [P, 2, HALF], F32, "dv1_early")
        for t in (2, 3):
            product(whole_product[t], t, whole)
            early[t] = last_early[:, t - 2, :]
            nc.scalar.copy(early[t], whole_product[t][:, halves[0]])
        for t in (2, 3):
            scatter_on_scalar(t, 0, early[t])
            late[t] = leave("dv%d_late" % t, whole_product[t][:, halves[1]], nc.vector.tensor_copy, "dv%d_late" % (t - 2))
            scatter_on_vector(t, halves[1], late[t][:])
            store(t)
